import numpy as np, ml_dtypes
CORES = [242,247,114,119]
N = 4
BF = ml_dtypes.bfloat16
W, V, L, F, B, TH, S, RO, SV = 2048, 512, 256, 4, 2, 9, 2, 3, 2
def parts(rng):
    x = np.clip(rng.integers(0, 256, (N, 8, 1, W)) + rng.integers(-70, 71, (N, 8, 16, W)), 0, 255)
    q = np.clip(rng.integers(0, 200, (N, 8, 1, L)) + rng.integers(-70, 71, (N, 8, 16, L)), 0, 255)
    return x, q, rng.integers(0, W, (N, 8, W)), rng.integers(0, W, (N, 8, W)), rng.integers(0, V, (N, 8, W)), rng.integers(0, W, (N, 8, 16, V))
def pack(x, q, nx, pv, rc, u):
    return {"xd": np.ascontiguousarray(x.reshape(N, 128, W)).astype(np.float32).astype(BF), "nx": nx.astype(np.int32), "pv": pv.astype(np.int32), "rc": rc.astype(np.int32),
            "ul": np.ascontiguousarray(u.reshape(N, 128, V)).astype(np.int32), "mv": np.ascontiguousarray(q.reshape(N, 128, L)).astype(np.float32).astype(BF)}
def some(rng, n):
    return 255 * (np.argsort(rng.random((N, 8, 16, L)), axis=2) < n[:, :, None, :])
def setup_inputs(rng):
    return pack(*parts(rng))
def setup_inputs_corners(rng):
    x, q, nx, pv, rc, u = parts(rng); c = np.arange(W); sh = int(rng.integers(0, 8))
    x[..., ::64] = 255; x[..., 63::64] = 0; q[..., :8] = 0; q[..., L - 8:] = 255
    for r in range(N):
        for g in range(8):
            k = (g + 3 * r + sh) % 8
            if k == 0: nx[r, g] = c; pv[r, g] = c; rc[r, g] = c % V
            elif k == 1: nx[r, g] = np.minimum(c + 1, W - 1); pv[r, g] = np.maximum(c - 1, 0); rc[r, g] = V - 1 - c % V
            elif k == 2: nx[r, g] = (c + 1) % W; pv[r, g] = (c + W - 1) % W
            elif k == 3: nx[r, g] = 0; pv[r, g] = W - 1; rc[r, g] = V - 1
            elif k == 4: nx[r, g] = W - 1; pv[r, g] = 0; rc[r, g] = 0
            elif k == 5: u[r, g] = u[r, g, :1] + np.zeros((16, 1), np.int64)
            elif k == 6: u[r, g] = rng.choice(np.array([0, W - 1, W // 2]), (16, V))
            else: nx[r, g] = c ^ 1; pv[r, g] = c ^ 1
            if (g + r) % 2 == 0:
                z, p, e, t1, t2, t3 = [int(b) for b in 1 + rng.permutation(W - 2)[:6]]; xb, ub, i = x[r, g], u[r, g], int(rng.integers(0, 16))
                xb[:, [z, p]] = 0; xb[i, p] = 1; xb[:, [e, t1, t2, t3]] = 255; xb[i, e] = 254
                nx[r, g, [z, p, t1, t2, t3]] = z; pv[r, g, [z, t1, t3]] = t1; pv[r, g, [p, e, t2]] = t2
                ub[:, (L - 1) * SV] = p; ub[15, (L - 1) * SV] = z
                ub[:, (L - 2) * SV] = t3
                ub[:, SV] = t1; ub[15, SV] = e
    return pack(x, q, nx, pv, rc, u)
def setup_inputs_counts(rng):
    x, q, nx, pv, rc, u = parts(rng); x = np.clip(x, 1, 254)
    much = rng.permutation(np.array((256, 511, 1024, 8 * L - 1, 255, 257, 8 * L, 0)[:N]))
    hit = (np.argsort(rng.random((N, 8 * L)), axis=1) < much[:, None]).reshape(N, 8, L)
    n = np.where(hit, rng.integers(TH, 17, (N, 8, L)), rng.integers(0, TH, (N, 8, L)))
    return pack(x, some(rng, n), nx, pv, rc, u)
def setup_inputs_ends(rng):
    x = 255 * rng.integers(0, 2, (N, 8, 16, W)); m = rng.random((N, 8, 1, W)); x = np.where(m < 0.3, 0, np.where(m < 0.6, 255, x))
    fl = rng.integers(0, 2, (N, 8)); fl[0] = 0; fl[N - 1] = 0; f2 = rng.integers(0, 2, (N, 8))
    x[:, :, :, 0] = 255 * fl[:, :, None]; x[:, :, :, W - 1] = 255 * (1 - fl)[:, :, None]
    odd = (np.arange(8) % 2 == 1)[None, :, None]
    def far(hi, n):
        a = hi * rng.integers(0, 2, (N, 8, n))
        return np.where((rng.random((N, 8, n)) < 0.35) & odd, rng.integers(0, hi + 1, (N, 8, n)), a)
    nx = far(W - 1, W); pv = far(W - 1, W); rc = far(V - 1, W); u = far(W - 1, 16 * V).reshape(N, 8, 16, V)
    u[N - 1] = (W - 1) * rng.integers(0, 2, (8, 16, V)); nx[N - 1, :, 0] = 0; nx[N - 1, :, W - 1] = 0
    rc[:, :, 0] = (V - 1) * f2; rc[:, :, W - 1] = (V - 1) * (1 - f2)
    n = rng.choice(np.array([0, TH - 1, TH, 16]), (N, 8, L))
    n[0] = rng.choice(np.array([0, TH - 1, TH // 2]), (8, L)); n[N - 1] = rng.choice(np.array([16, TH]), (8, L))
    z = (L - 1) * SV; n[0, 7, L - 2:] = 0; n[N - 1, 7, L - 1] = 16
    u[0, 7, :, z] = W - 1; u[0, 7, :, z - SV] = W - 1; u[0, 7, 15, z - SV] = 0
    u[N - 1, 7, :, z] = W - 1; u[N - 1, 7, 15, z] = 0
    n[1, 7, L - 1] = 16; x[1, 7, :, 0] = 0; x[1, 7, :, 1] = 255; x[1, 7, :, 2] = 0; x[1, 7, :, W - 1] = 255
    nx[1, 7, 0] = W - 1; nx[1, 7, W - 1] = W - 1; nx[1, 7, 1] = 2; u[1, 7, :15, z] = 1; u[1, 7, 15, z] = 0
    return pack(x, some(rng, n), nx, pv, rc, u)
def setup_inputs_near(rng):
    x, q, nx, pv, rc, u = parts(rng); b = rng.integers(0, 255, (N, 8, 1, 1)); b[0, 0] = 0; b[1, 1] = 254
    x = b + (rng.random((N, 8, 16, W)) < rng.choice(np.array([0.2, 0.5, 0.8]), (N, 8, 1, W)))
    q = b + (rng.random((N, 8, 16, L)) < rng.choice(np.array([0.2, 0.5, 0.8, 1.0]), (N, 8, 1, L)))
    few = rng.integers(0, W, (N, 8, 64)); u = np.take_along_axis(few, rng.integers(0, 64, (N, 8, 16 * V)), 2).reshape(N, 8, 16, V)
    return pack(x, q, nx, pv, rc, u)
def setup_inputs_spread(rng):
    x = (np.exp2(8 * rng.random((N, 8, 1, W))) * rng.random((N, 8, 16, W))).astype(np.int64)
    q = (np.exp2(8 * rng.random((N, 8, 1, L))) * rng.random((N, 8, 16, L))).astype(np.int64)
    def skew(hi, n):
        return np.minimum((hi * rng.random((N, 8, n)) ** rng.choice(np.array([1, 2, 4]), (N, 8, 1))).astype(np.int64), hi - 1)
    return pack(np.minimum(x, 255), np.minimum(q, 255), skew(W, W), skew(W, W), skew(V, W), skew(W, 16 * V).reshape(N, 8, 16, V))
def check_inputs(d):
    bad = []
    for k, lo, hi in (("xd", 0, 255), ("nx", 0, W - 1), ("pv", 0, W - 1), ("rc", 0, V - 1), ("ul", 0, W - 1), ("mv", 0, 255)):
        a = np.asarray(d[k]).astype(np.float64)
        if not (np.min(a) >= lo and np.max(a) <= hi): bad.append("range of " + k)
        elif np.any(a != np.floor(a)): bad.append("whole numbers in " + k)
    return bad
def lowest(n):
    same = n[:, :, :, None] == n[:, :, None, :]
    return ~np.any(same & np.tril(np.ones((L, L), bool), -1), axis=3)
def reference(xd, nx, pv, rc, ul, mv):
    X = np.ascontiguousarray(xd.astype(np.float32).astype(np.int32).reshape(N, 8, 16, W).transpose(0, 1, 3, 2))
    q = np.ascontiguousarray(mv.astype(np.float32).astype(np.int32).reshape(N, 8, 16, L).transpose(0, 1, 3, 2))
    nxt, pre, rec = nx.astype(np.int64), pv.astype(np.int64), rc.astype(np.int64)
    U = ul.astype(np.int64).reshape(N, 8, 16, V); v = np.zeros((N, 8, L), np.int64) + SV * np.arange(L)
    R3, G3 = np.arange(N)[:, None, None], np.arange(8)[None, :, None]; R4, G4 = R3[..., None], G3[..., None]
    for t in range(RO):
        d = np.take_along_axis(U, v[:, :, None, :], 3)
        score = np.add.reduce(np.abs(X[R4, G4, d] - q[:, :, None]), axis=4)
        cleared = np.zeros(d.shape, bool); c = d
        for f in range(F):
            c = nxt[R4, G4, c]
            cleared = cleared | (np.add.reduce((X[R4, G4, c] < q[:, :, None]).astype(np.int32), axis=4) >= TH)
        none = np.all(cleared, axis=2)
        k = np.where(none, np.argmax(score, axis=2), np.argmin(np.where(cleared, 2 ** 20, score), axis=2))
        a = np.take_along_axis(d, k[:, :, None, :], 2)[:, :, 0]; go = np.ones(a.shape, bool)
        for s in range(B):
            b = pre[R3, G3, a]
            go = go & (np.add.reduce((X[R3, G3, b] < q).astype(np.int32), axis=3) < TH)
            a = np.where(go, b, a)
        w = rec[R3, G3, a]
        A = np.add.reduce(none.reshape(N, -1).astype(np.int32), axis=1) & 255
        z = (q + A[:, None, None, None]) >> 1
        xn = (X[R3, G3, a] + q + 1) >> 1; nn = nxt[R3, G3, nxt[R3, G3, a]]
        r, g, i = np.nonzero(lowest(v)); U[r, g, k[r, g, i], v[r, g, i]] = a[r, g, i]
        r, g, i = np.nonzero(lowest(a)); X[r, g, a[r, g, i]] = xn[r, g, i]; nxt[r, g, a[r, g, i]] = nn[r, g, i]
        v = w + 0; q = z + 0
        for h in range(1, S):
            s = 1 + (t + h - 1) % (N - 1)
            v[:, :, h::S] = np.roll(w, s, axis=0)[:, :, h::S]; q[:, :, h::S] = np.roll(z, s, axis=0)[:, :, h::S]
    return {"yu": U.reshape(N, 128, V).astype(np.float32), "yx": np.ascontiguousarray(X.transpose(0, 1, 3, 2)).reshape(N, 128, W).astype(np.float32).astype(BF),
            "yv": v.astype(np.float32), "yq": np.ascontiguousarray(q.transpose(0, 1, 3, 2)).reshape(N, 128, L).astype(np.float32).astype(BF)}

@@ -1,0 +1,570 @@
+import numpy as np
+from concourse.bass import DstId, RemoteDMATransfer
+from concourse.mybir import dt, AluOpType as A, AxisListType, ActivationFunctionType as F
+
+SCRATCH = {}
+for _n, _c, _d in (
+        ("xt", 2304, "bfloat16"), ("x1", 2048, "bfloat16"), ("x2", 2048, "bfloat16"), ("x3", 2048, "bfloat16"),
+        ("x4", 2048, "bfloat16"), ("q16", 4096, "bfloat16"), ("qa", 256, "bfloat16"), ("qb", 256, "bfloat16"),
+        ("qo", 128, "bfloat16"), ("qr0", 128, "bfloat16"), ("qr1", 128, "bfloat16"), ("qr2", 128, "bfloat16"),
+        ("xg", 4096, "bfloat16"), ("ab", 4096, "bfloat16"), ("ca", 4096, "bfloat16"), ("cb", 4096, "bfloat16"),
+        ("xg4", 2048, "bfloat16"), ("sg4", 2048, "bfloat16"),
+        ("uw", 768, "float32"), ("ui", 512, "int32"), ("i16", 128, "bfloat16"), ("i32", 128, "bfloat16"), ("k8", 128, "bfloat16"), ("kk1", 128, "bfloat16"), ("nxr", 2304, "float32"),
+        ("pvr", 2048, "int32"), ("rcr", 2048, "int32"), ("idw", 2048, "float32"),
+        ("npi", 128, "int32"), ("npf", 128, "float32"), ("nxl", 128, "uint16"),
+        ("dd", 256, "float32"), ("d16", 256, "uint16"), ("vl", 16, "float32"), ("vl16", 16, "uint16"),
+        ("vn", 16, "float32"), ("vr", 256, "float32"), ("vx", 256, "float32"), ("yv1", 2176, "bfloat16"), ("ev", 2176, "bfloat16"),
+        ("ar", 256, "float16"), ("ar32", 256, "float32"), ("ax", 256, "float32"), ("ed", 256, "bfloat16"),
+        ("em", 1920, "bfloat16"), ("zz", 256, "bfloat16"),
+        ("dm", 256, "float32"), ("ds", 256, "float32"), ("lx", 16, "float32"),
+        ("vp16", 16, "uint16"), ("ap16", 16, "uint16"), ("m1", 256, "float32"), ("nph", 128, "float16"), ("npt", 128, "float16"),
+        ("rr", 768, "bfloat16"), ("tk", 256, "float32"),
+        ("key", 256, "float32"), ("keyt", 256, "float32"), ("s1", 256, "float32"), ("eqt", 256, "float32"),
+        ("pd", 256, "float32"), ("s2", 256, "float16"), ("oh", 256, "float32"), ("fl", 16, "bfloat16"),
+        ("a016", 16, "uint16"), ("w1", 256, "float32"), ("sc1", 256, "float32"), ("w2", 256, "float32"),
+        ("sc2", 256, "float32"), ("bl", 32, "uint16"), ("xc", 512, "bfloat16"),
+        ("f1", 16, "float32"), ("d1", 16, "float32"), ("d2", 16, "float32"), ("f2", 16, "float32"), ("al", 16, "float32"),
+        ("al16", 16, "uint16"), ("w3", 256, "float32"), ("sc3", 256, "float32"), ("w4", 256, "float32"),
+        ("sc4", 256, "float32"), ("ws", 16, "float32"), ("we", 16, "float32"), ("wr0", 16, "float32"),
+        ("wr1", 16, "float32"), ("wr2", 16, "float32"), ("nl16", 16, "uint16"), ("nx2", 256, "float32"),
+        ("xga", 256, "bfloat16"), ("h1", 256, "float32"), ("xn", 256, "bfloat16"),
+        ("nj", 16, "float32"), ("cols", 64, "float32"), ("yy", 256, "float32"), ("y2", 256, "float32"),
+        ("ci", 64, "int32"), ("cf", 256, "float32"), ("cg", 128, "float32"), ("ch", 128, "float32"),
+        ("dg", 256, "float32"), ("dgt", 256, "float32"), ("dgu", 256, "float32"), ("tri", 256, "bfloat16"),
+        ("rst", 256, "float32"), ("zr", 256, "float32"), ("ek", 2048, "bfloat16"), ("cc", 128, "bfloat16"),
+        ("b4", 128, "bfloat16"), ("idf", 128, "float32"), ("idfn", 128, "float32"), ("idb", 128, "bfloat16"),
+        ("idn", 128, "bfloat16"), ("idh", 128, "float16"), ("sw", 512, "float16"), ("ones", 128, "bfloat16"),
+        ("exl", 16, "uint16"), ("exc", 16, "uint16"), ("sa", 4, "float32"), ("ra", 4, "float32")):
+    _d = {"w1": "float16", "w2": "float16", "w3": "float16", "w4": "float16", "sc1": "float16", "sc2": "float16",
+          "sc3": "float16", "sc4": "float16", "dm": "float16", "ds": "float16", "pd": "float16",
+          "zr": "bfloat16", "eqt": "bfloat16", "oh": "bfloat16"}.get(_n, _d)
+    SCRATCH[_n] = ("sbuf", [128, 2560 if _c == 2304 else _c], _d)
+for _k in range(8):
+    SCRATCH["p%d" % _k] = ("psum", [128, 512], "float32")
+
+SCRATCH["nxd"] = ("dram", [8, 2048], "float32")
+
+ROUNDS = 3
+LSS = (64, 64, 64)
+XV0, XV = 512, 1024
+SEMAPHORES = ["cv", "cs", "ct", "cp", "ldx", "ldq", "ldu", "ldn", "ldr", "ldd", "ldp", "ldc", "nd0", "nd1", "out"]
+for _t in range(ROUNDS):
+    SEMAPHORES += ["%s%d" % (_a, _t) for _a in ("rq", "ra", "rw", "lq", "la", "lw")]
+GK0, GK = 4, 8
+VM = 0
+FAR = 262144.0
+BIG = 1048576.0
+MAG = 12582912.0
+
+
+def rank_program(g, core, T, topo):
+    rank = T.rank_of(core)
+    if rank is None:
+        return
+    N = len(T.cores)
+    V, S, P = g.vector, g.scalar, g.tensor
+    eng = {"v": V, "s": S, "t": P, "p": g, "y": g.sync}
+    own = {"v": "cv", "s": "cs", "t": "ct", "p": "cp"}
+    total = {}
+    known = {e: {} for e in eng}
+    clocks = {}
+    wr, rd, bank = {}, {}, {}
+
+    def need(e, deps):
+        for s in sorted(deps):
+            n = deps[s]
+            if known[e].get(s, 0) >= n:
+                continue
+            eng[e].wait_ge(T.sem[s], n)
+            for k, c in clocks.get((s, n), {}).items():
+                known[e][k] = max(known[e].get(k, 0), c)
+            known[e][s] = n
+
+    def deps_of(R, W, X, me):
+        d = {}
+
+        def put(s, n):
+            d[s] = max(d.get(s, 0), n)
+        for k in R:
+            if k in wr:
+                put(*wr[k])
+        for k in W:
+            if k in wr and wr[k][0] != me:
+                put(*wr[k])
+            for s, n in rd.get(k, {}).items():
+                if s != me:
+                    put(s, n)
+        for k in X:
+            for s, n in bank.get(k, {}).items():
+                if s != me:
+                    put(s, n)
+        return d
+
+    def note(s, n, R, W, X):
+        for k in R:
+            rd.setdefault(k, {})[s] = n
+        for k in W:
+            wr[k] = (s, n)
+            rd[k] = {}
+        for k in X:
+            bank.setdefault(k, {})[s] = n
+
+    def op(e, R, W, X, call):
+        me = own[e]
+        need(e, deps_of(R, W, X, me))
+        n = total.get(me, 0) + 1
+        total[me] = n
+        call().then_inc(T.sem[me], 1)
+        c = dict(known[e])
+        c[me] = n
+        clocks[(me, n)] = c
+        note(me, n, R, W, X)
+
+    def dma(e, sem, full, R, W, out, in_):
+        need(e, deps_of(R, W, [], sem))
+        total[sem] = total.get(sem, 0) + 16
+        eng[e].dma_start(out, in_).then_inc(T.sem[sem], 16)
+        c = dict(known[e])
+        c[sem] = full
+        clocks[(sem, full)] = c
+        note(sem, full, R, W, [])
+
+    def send(t, kind, src, key, dst, land):
+        d = T.cores[(rank + 1 + t % (N - 1)) % N]
+        es = topo.engines(core, d)[:8]
+        m = 0
+        for x in es:
+            m |= 1 << x
+        need("p", deps_of([key], [], [], None))
+        rid, pid = topo.addr(d, core)
+        rs, ls = "r" + kind + str(t), "l" + kind + str(t)
+        g.remote_dma(dst, src, T.sem[rs], T.sem[ls], pid, rid, m)
+        total[ls] = len(es)
+        note(ls, len(es), [key], [], [])
+        sender = T.cores[(rank - 1 - t % (N - 1)) % N]
+        total[rs] = len(topo.engines(sender, core)[:8])
+        wr[land] = (rs, total[rs])
+
+    def act(out, in_, R, W, X=(), func=F.Identity, **kw):
+        op("s", R, W, X, lambda: S.activation(out, in_, func, **kw))
+
+    def tt(out, a, b, o, R, W, X=()):
+        op("v", R, W, X, lambda: V.tensor_tensor(out, a, b, o))
+
+    def ts(out, a, s1, o1, R, W, X=(), s2=None, o2=None):
+        if o2 is None:
+            op("v", R, W, X, lambda: V.tensor_scalar(out, a, s1, None, o1))
+        else:
+            op("v", R, W, X, lambda: V.tensor_scalar(out, a, s1, s2, o1, o2))
+
+    def cp(out, in_, R, W, X=()):
+        op("v", R, W, X, lambda: V.tensor_copy(out, in_))
+
+    def vtr(out, in_, R, W, X=()):
+        op("v", R, W, X, lambda: V.transpose(out, in_))
+
+    def scan(out, d0, d1, o0, o1, R, W):
+        op("v", R, W, [], lambda: V.tensor_tensor_scan(out, d0, d1, 0.0, o0, o1))
+
+    def mm(out, l, r, st, sp, R, W, X):
+        op("t", R, W, X, lambda: P.matmul(out, l, r, st, sp))
+
+    def iota(out, pat, base, cm, W, whole=False):
+        if whole:
+            op("p", [], W, [], lambda: g.iota(out, pat, base, cm))
+        else:
+            op("p", [], W, [], lambda: g.iota(out, pat, base, cm, allow_small_or_imprecise_dtypes=True))
+
+    def col(j):
+        return T.cols[:, j:j + 1]
+
+    dma("y", "ldn", 16, [], ["npi"], T.npi[:], T.nx[:])
+    dma("y", "ldx", 16, [], ["xt"], T.xt[:, 0:2048], T.xd[:])
+    dma("s", "ldq", 16, [], ["qa"], T.qa[:], T.mv[:])
+    dma("s", "ldu", 16, [], ["ui"], T.ui[:], T.ul[:])
+    for s, dst, src, k in (("ldp", T.pvr, T.pv, "pvr"), ("ldc", T.rcr, T.rc, "rcr")):
+        for i in range(16):
+            dma("y", s, 256, ["xt", "ui", "qa"], [k], dst[i:128:16, :], src[:])
+
+    def repeat_nx():
+        dma("y", "ldd", 16, ["npf"], ["nxd"], T.nxd[:], T.npf[:])
+        for i in range(16):
+            dma("y", "ldr", 256, ["nxd"], ["nxr"], T.nxr[i:128:16, 0:2048], T.nxd[:])
+
+    iota(T.ch[:], [[1, 128]], 0, -1, ["ch"])
+    iota(T.ci[:, 0:1], [[0, 1]], 0, 1, ["ci0"], True)
+    iota(T.cf[:], [[0, 16], [1, 16]], 0, 0, ["cf"])
+    iota(T.cg[:], [[1, 8], [0, 16]], 0, 0, ["cg"])
+    ts(T.idf[:], T.ch[:], 0.0, A.is_equal, ["ch"], ["idf"])
+    op("v", ["ci0"], ["ci3"], [], lambda: V.tensor_scalar(T.ci[:, 1:2], T.ci[:, 0:1], 15, None, A.bitwise_and))
+    op("v", ["ci0"], ["ci4"], [], lambda: V.tensor_scalar(T.ci[:, 2:3], T.ci[:, 0:1], 4, None, A.arith_shift_right))
+    op("v", ["ci0"], ["ci6"], [], lambda: V.tensor_scalar(T.ci[:, 4:5], T.ci[:, 0:1], 1, None, A.bitwise_and))
+    cp(col(0), T.ci[:, 1:2], ["ci3"], ["c0"])
+    cp(col(1), T.ci[:, 2:3], ["ci4"], ["c1"])
+    op("v", ["ci4"], ["ci5"], [], lambda: V.tensor_scalar(T.ci[:, 3:4], T.ci[:, 2:3], 1, None, A.bitwise_and))
+    cp(col(4), T.ci[:, 4:5], ["ci6"], ["c4"])
+    ts(T.idb[:], T.ch[:], 0.0, A.is_equal, ["ch"], ["idb"])
+    cp(col(2), T.ci[:, 3:4], ["ci5"], ["c2"])
+    ts(col(3), T.ci[:, 3:4], 0.0, A.is_equal, ["ci5"], ["c3"])
+    ts(T.idn[:], T.ch[:], 0.0, A.is_equal, ["ch"], ["idn"], (), -1.0, A.mult)
+    ts(T.m1[:, 0:128], T.cg[:], col(1), A.is_equal, ["cg", "c1"], ["bs"])
+    ts(T.m1[:, 128:256], T.cf[:, 0:128], 1.0, A.add, ["cf"], ["cg2"])
+    tt(T.cc[:], T.m1[:, 0:128], T.m1[:, 128:256], A.mult, ["bs", "cg2"], ["cc"])
+    act(T.zr[:], T.cf[:], ["cf"], ["zr"], func=F.Sign)
+    act(T.rst[:], T.zr[:], ["zr"], ["rst"], scale=-2.0 * BIG, bias=BIG)
+    act(col(8), col(0), ["c0"], ["c8"], bias=0.5)
+    act(T.y2[:], T.cf[:], ["cf", "c8"], ["tri0"], scale=-1.0, bias=col(8), func=F.Sign)
+    act(T.tri[:], T.y2[:], ["tri0"], ["tri"], scale=4096.0, func=F.Relu)
+    act(T.qo[:], T.qa[:, 1::2], ["qa"], ["qo"])
+    send(0, "q", T.qo[:], "qo", T.qr0[:], "qr0")
+
+    def repeat_q(ks, q, qk):
+        for k in ks:
+            op("p", [qk], ["q16g"], [], lambda: g.affine_select(T.q16[:, k::16], q[:], [[0, 256]], A.is_gt, 0.0, 1, 0))
+
+    repeat_q(range(16 - GK0, 16), T.qa, "qa")
+    iota(T.ci[:, 16:32], [[16, 16]], 15, 0, ["ci1"], True)
+    iota(T.ci[:, 32:48], [[1, 16]], 0, 0, ["ci2"], True)
+    iota(T.nj[:], [[32, 16]], 0, 0, ["nj"])
+    iota(T.dgt[:], [[2, 256]], 2048, 0, ["dgt0"])
+    iota(T.dgu[:], [[1, 256]], 512, 0, ["dgu0"])
+    iota(T.idw[:], [[1, 2048]], 0, 0, ["idw"])
+
+    def make_ek(ks):
+        for k in ks:
+            ts(T.ek[:, 128 * k:128 * k + 128], T.cc[:], float(k + 1), A.is_equal, ["cc"], ["ek"], (), FAR, A.mult)
+
+    make_ek(range(8))
+    cp(T.d16[:], T.ui[:, 0:512:2], ["ui"], ["d16"])
+    cp(T.nph[:], T.npi[:], ["npi"], ["nph"])
+    cp(T.npf[:], T.npi[:], ["npi"], ["npf"])
+    repeat_nx()
+
+    def list_of_nx():
+        vtr(T.npt[:], T.nph[:], ["nph"], ["npt"])
+        for e in (0, 1):
+            for b in range(4):
+                for h in (0, 1):
+                    mm(T.p7[:, 2 * b + e:128:8], T.sw[:, 128 * (2 * e + h):128 * (2 * e + h) + 128],
+                       T.npt[:, 32 * b + 16 * h:32 * b + 16 * h + 16], h == 0, h == 1, ["sw", "npt"], ["nxt"], ["p7"])
+
+    for j, (x, c) in enumerate(((0.0, 3), (16.0, 3), (-16.0, 2), (0.0, 2))):
+        ts(T.sw[:, 128 * j:128 * j + 128], T.ch[:], x, A.is_equal, ["ch", "c%d" % c], ["sw"], (), col(c), A.mult)
+    list_of_nx()
+    make_ek(range(8, 16))
+    cp(T.nxl[:], T.p7[:, 0:128], ["nxt"], ["nxl"], ["p7"])
+    cp(T.dd[:], T.ui[:, 0:512:2], ["ui"], ["dd"])
+
+    def first_fill():
+        for k in range(16 - GK0):
+            cp(T.q16[:, k::16], T.qa[:], ["qa"], ["q16"])
+        vtr(T.p4[:, 0:256], T.dd[:], ["dd"], ["dt"], ["p4"])
+
+    def constants_on_scalar():
+        act(col(5), col(4), ["c4"], ["c5"], scale=-1.0, bias=1.0)
+        act(col(6), col(0), ["c0"], ["c6"], scale=2.0)
+        act(col(7), col(0), ["c0"], ["c7"], bias=65536.0)
+        act(col(9), col(0), ["c0"], ["c9"], bias=-65536.0)
+        for w, k, x in ((T.i16, "i16", 16.0), (T.i32, "i32", 32.0), (T.k8, "k8", -8.4 * FAR), (T.kk1, "kk1", -FAR)):
+            act(w[:], T.idb[:], ["idb"], [k], scale=x)
+        act(T.idfn[:], T.idf[:], ["idf"], ["idfn"], scale=-1.0)
+        act(T.ones[:], T.cf[:, 0:128], ["cf"], ["ones"], scale=0.0, bias=1.0)
+        act(T.zz[:], T.cf[:], ["cf"], ["zz"], scale=0.0)
+
+    def constants_on_vector():
+        ts(T.dg[:], T.cf[:], col(0), A.is_equal, ["cf", "c0"], ["dg"])
+
+    def later_constants():
+        ts(T.b4[:], T.cc[:], 0.0, A.is_gt, ["cc"], ["b4"], (), 4096.0, A.mult)
+        ts(T.idh[:], T.ch[:], 0.0, A.is_equal, ["ch"], ["idh"])
+        cp(T.exl[:], T.ci[:, 16:32], ["ci1"], ["exl"])
+        cp(T.exc[:], T.ci[:, 32:48], ["ci2"], ["exc"])
+        ts(T.vl[:], T.nj[:], col(6), A.add, ["nj", "c6"], ["vl"])
+        cp(T.vp16[:], T.vl[:], ["vl"], ["vp16"])
+        cp(T.uw[:, 0:512], T.ui[:], ["ui"], ["uw"])
+
+    def places_past_the_end(step):
+        if step == 0:
+            act(T.yy[:], T.dg[:], ["dg"], ["dgs"], scale=4096.0, bias=-4096.0)
+        for w, k, pb in ((T.dgt, "dgt", "p4"), (T.dgu, "dgu", "p5")):
+            pw = T[pb][:, 256:512]
+            if step == 0:
+                mm(pw, T.idf[:], w[:], True, False, ["idf", k + "0"], [k + "p"], [pb])
+                mm(pw, T.idf[:], T.yy[:], False, True, ["idf", "dgs"], [k + "p"], [pb])
+            else:
+                act(w[:], pw, [k + "p"], [k], [pb], func=F.Relu)
+
+    def places(jobs):
+        for cb, pk, dgx, dk, al, alk, out16, outk, (dm, ds, lx) in jobs:
+            tt(dm[:], T[pk][:, 0:256], dgx[:], A.min, [cb, dk], ["dm" + pk], [pk])
+        for cb, pk, dgx, dk, al, alk, out16, outk, (dm, ds, lx) in jobs:
+            scan(ds[:], T.zr[:], dm[:], A.mult, A.add, ["zr", "dm" + pk], ["ds" + pk])
+        for cb, pk, dgx, dk, al, alk, out16, outk, (dm, ds, lx) in jobs:
+            tt(lx[:], ds[:, 15::16], al[:], A.max, ["ds" + pk, alk], ["lx" + pk])
+        for cb, pk, dgx, dk, al, alk, out16, outk, (dm, ds, lx) in jobs:
+            cp(out16[:], lx[:], ["lx" + pk], [outk])
+
+    def sums(pout, src, keys, l0, l1, pk, dk):
+        for k in range(16):
+            mm(pout[:, l0:l1], T.ek[:, 128 * k:128 * k + 128], src(k), k == 0, k == 15, ["ek"] + keys, [dk], [pk])
+
+    SEG = [(0, 0)] * 15
+    _o = 0
+    for m in range(15):
+        SEG[m] = (_o, 240 - 16 * m)
+        _o += 240 - 16 * m
+
+    Q, QN, qk, qnk = T.qa, T.qb, "qa", "qb"
+    for t in range(ROUNDS):
+        last = t == ROUNDS - 1
+        LS = LSS[t]
+        LV = 256 - LS
+        xv = XV if t else XV0
+
+        def walk(x, xk, out, ok, l0, l1):
+            tt(out[:, 16 * l0:16 * l1], x[:].indirect(T.d16[:, l0:l1]), T.q16[:, 16 * l0:16 * l1], A.is_lt,
+               xk + ["d16", "q16", "q16g"], [ok + str(l0)])
+
+        def wsum(pout, out, ok, l0, l1, pk, dk):
+            sums(pout, lambda k: out[:, 16 * l0 + k:16 * l1:16], [ok + str(l0)], l0, l1, pk, dk + str(l0))
+
+        def diff(c, src, sk, lane0):
+            pk = ("p2", "p3")[c % 2]
+            j = 512 * c
+            mm(T[pk][:], T.idb[:], src[:, j:j + 512], True, False, ["idb", sk], [pk + "d"], [pk])
+            mm(T[pk][:], T.idn[:], T.q16[:, 16 * lane0 + j:16 * lane0 + j + 512], False, True, ["idn", "q16", "q16g"], [pk + "d"], [pk])
+
+        def absc(c):
+            pk = ("p2", "p3")[c % 2]
+            act(T.ab[:, 512 * c:512 * c + 512], T[pk][:], [pk + "d"], ["ab%d" % (c // 4)], [pk], func=F.Abs)
+
+        def marks(l0, l1, k):
+            act(T.xg[:, 16 * l0:16 * l1], T.xt[:, 0:2048].indirect(T.d16[:, l0:l1]), ["xt", "d16"], [k])
+
+        if t:
+            cp(T.d16[:], T.uw[:, 0:512].indirect(T.vl16[:]), ["uw", "vl16"], ["d16"])
+            act(T.dd[:], T.uw[:, 0:512].indirect(T.vl16[:]), ["uw", "vl16"], ["dd"])
+            marks(VM, 64, "xga0")
+            vtr(T.p4[:, 0:256], T.dd[:], ["dd"], ["dt"], ["p4"])
+            if VM:
+                cp(T.xg[:, 0:16 * VM], T.xt[:, 0:2048].indirect(T.d16[:, 0:VM]), ["xt", "d16"], ["xgv"])
+            cp(T.nph[:], T.npf[:], ["npf"], ["nph"])
+            list_of_nx()
+            cp(T.nxl[:], T.p7[:, 0:128], ["nxt"], ["nxl"], ["p7"])
+            cp(T.x1[:, 0:xv], T.xt[:, 0:2048].indirect(T.nxl[:, 0:xv // 16]), ["xt", "nxl"], ["x1a"])
+        else:
+            constants_on_scalar()
+        act(T.x1[:, xv:2048], T.xt[:, 0:2048].indirect(T.nxl[:, xv // 16:128]), ["xt", "nxl"], ["x1b"])
+        if t == 0:
+            marks(0, 64, "xga0")
+            first_fill()
+            cp(T.x1[:, 0:xv], T.xt[:, 0:2048].indirect(T.nxl[:, 0:xv // 16]), ["xt", "nxl"], ["x1a"])
+            constants_on_vector()
+            places_past_the_end(0)
+        act(T.x2[:], T.x1[:].indirect(T.nxl[:]), ["x1a", "x1b", "nxl"], ["x2"])
+        walk(T.x1, ["x1a", "x1b"], T.ca, "ca", 0, 128)
+        marks(64, 128, "xgb0")
+        diff(0, T.xg, "xgv" if t and VM == 32 else "xga0", 0)
+        diff(1, T.xg, "xga0", 0)
+        wsum(T.p0, T.ca, "ca", 0, 128, "p0", "k1")
+        walk(T.x1, ["x1a", "x1b"], T.ca, "ca", 128, 256)
+        absc(0)
+        absc(1)
+        diff(2, T.xg, "xgb0", 0)
+        diff(3, T.xg, "xgb0", 0)
+        absc(2)
+        absc(3)
+        wsum(T.p0, T.ca, "ca", 128, 256, "p0", "k1")
+        act(T.x3[:], T.x2[:].indirect(T.nxl[:]), ["x2", "nxl"], ["x3"])
+        act(T.rr[:, 0:256], T.p0[:, 0:256], ["k10", "k1128"], ["rr0"], ["p0"], func=F.Relu, bias=-8.0 * FAR)
+        if t == 0:
+            act(T.x4[:], T.x3[:].indirect(T.nxl[:]), ["x3", "nxl"], ["x4"])
+        marks(128, 256, "xg1")
+        walk(T.x2, ["x2"], T.cb, "cb", 0, 128)
+        sums(T.p5, lambda k: T.ab[:, k:2048:16], ["ab0"], 0, 128, "p5", "sc0")
+        wsum(T.p1, T.cb, "cb", 0, 128, "p1", "k2")
+        walk(T.x2, ["x2"], T.cb, "cb", 128, 256)
+        wsum(T.p1, T.cb, "cb", 128, 256, "p1", "k2")
+        walk(T.x3, ["x3"], T.ca, "ca", 0, 128)
+        if t == 0:
+            wsum(T.p0, T.ca, "ca", 0, 128, "p0", "k3")
+        diff(4, T.xg, "xg1", 0)
+        diff(5, T.xg, "xg1", 0)
+        absc(4)
+        absc(5)
+        diff(6, T.xg, "xg1", 0)
+        diff(7, T.xg, "xg1", 0)
+        if t:
+            act(T.x4[:], T.x3[:].indirect(T.nxl[:]), ["x3", "nxl"], ["x4"])
+        absc(6)
+        absc(7)
+        if t:
+            wsum(T.p0, T.ca, "ca", 0, 128, "p0", "k3")
+        walk(T.x3, ["x3"], T.ca, "ca", 128, 256)
+        act(T.rr[:, 256:512], T.p1[:, 0:256], ["k20", "k2128"], ["rr1"], ["p1"], func=F.Relu, bias=-8.0 * FAR)
+        if t == 0:
+            sums(T.p5, lambda k: T.ab[:, 2048 + k::16], ["ab1"], 128, 256, "p5", "sc1")
+        wsum(T.p0, T.ca, "ca", 128, 256, "p0", "k3")
+        if t:
+            sums(T.p5, lambda k: T.ab[:, 2048 + k::16], ["ab1"], 128, 256, "p5", "sc1")
+        act(T.xg4[:, 0:16 * LS], T.x4[:].indirect(T.d16[:, LV:256]), ["x4", "d16"], ["xg4"])
+        for c in range(LS // 32):
+            pk = ("p2", "p3")[c % 2]
+            diff(c, T.xg4, "xg4", LV)
+            act(T.sg4[:, 512 * c:512 * c + 512], T[pk][:], [pk + "d"], ["sg4"], [pk], func=F.Sign, scale=-1.0, bias=-0.5)
+            if c == 0:
+                act(T.m1[:], T.p5[:, 0:256], ["sc0", "sc1", "c9"], ["ka"], ["p5"], scale=16.0 / FAR, bias=col(9))
+                act(T.p6[:, 256:512], T.p5[:, 0:256], ["sc0", "sc1", "c7"], ["kb"], ["p5", "p6"], scale=-16.0 / FAR, bias=col(7))
+        walk(T.x4, ["x4"], T.cb, "cb", 0, 128)
+        act(T.rr[:, 512:768], T.p0[:, 0:256], ["k30", "k3128"], ["rr2"], ["p0"], func=F.Relu, bias=-8.0 * FAR)
+
+        def fourth(pout, p0, pk, w, wk, base, bk, src, sk, l0, l1, dk):
+            po = pout[:, p0 + l0:p0 + l1]
+            mm(po, base[:], T.ones[:, 0:l1 - l0], True, False, [bk, "ones"], [dk], [pk])
+            for j in range(2):
+                mm(po, w[:], T.rr[:, 256 * j + l0:256 * j + l1], False, False, [wk, "rr%d" % j], [dk], [pk])
+            for k in range(16):
+                mm(po, T.ek[:, 128 * k:128 * k + 128], src(k), False, False, ["ek", sk], [dk], [pk])
+            mm(po, w[:], T.rr[:, 512 + l0:512 + l1], False, True, [wk, "rr2"], [dk], [pk])
+
+        walk(T.x4, ["x4"], T.cb, "cb", 128, LV)
+        fourth(T.p1, 0, "p1", T.i16, "i16", T.k8, "k8", lambda k: T.cb[:, k:2048:16], "cb0", 0, 128, "k40")
+        fourth(T.p5, 0, "p5", T.i32, "i32", T.kk1, "kk1", lambda k: T.sg4[:, k:16 * LS:16], "sg4", LV, 256, "k4s")
+        fourth(T.p0, 256, "p0", T.i16, "i16", T.k8, "k8", lambda k: T.cb[:, 2048 + k:16 * LV:16], "cb128", 128, LV, "k4128")
+        if t == 0:
+            later_constants()
+        if t:
+            act(T.vn[:], T.vl[:], ["vl"], ["vn"], scale=-1.0)
+            act(T.vx[:], T.vl[:].indirect(T.exc[:]), ["vl", "exc"], ["vx"])
+            act(T.vr[:], T.idw[:].indirect(T.vl16[:]), ["idw", "vl16"], ["vr"])
+            mm(T.p3[:, 0:256], T.idfn[:], T.vx[:], True, False, ["idfn", "vx"], ["dv"], ["p3"])
+            mm(T.p3[:, 0:256], T.idf[:], T.vr[:], False, False, ["idf", "vr"], ["dv"], ["p3"])
+            mm(T.p3[:, 0:256], T.idb[:], T.tri[:], False, True, ["idb", "tri"], ["dv"], ["p3"])
+            for m, (o, n) in enumerate(SEG):
+                act(T.yv1[:, 256 + o:256 + o + n], T.vr[:, 256 - n:256], ["vr", "vn"], ["yv1"], func=F.Abs, bias=T.vn[:, m:m + 1])
+            act(T.yv1[:, 0:256], T.p3[:, 0:256], ["dv"], ["yv1"], ["p3"], func=F.Abs)
+        for h, parts in enumerate((((T.p1, "p1", 0, "k40", 0, 128),), ((T.p5, "p5", 0, "k4s", LV, 256), (T.p0, "p0", 256, "k4128", 128, LV)))):
+            H, k = slice(128 * h, 128 * h + 128), str(h)
+            for pp, pk, po, ck, l0, l1 in parts:
+                tt(T.tk[:, l0:l1], pp[:, po + l0:po + l1], T.m1[:, l0:l1], A.max, ["ka", ck], ["tk" + k], [pk])
+            tt(T.key[:, H], T.p6[:, 256 + 128 * h:384 + 128 * h], T.tk[:, H], A.min, ["tk" + k, "kb"], ["key" + k], ["p6"])
+            vtr(T.keyt[:, H], T.key[:, H], ["key" + k], ["keyt" + k])
+            scan(T.s1[:, H], T.rst[:, H], T.keyt[:, H], A.max, A.min, ["rst", "keyt" + k], ["s1" + k])
+            tt(T.eqt[:, H], T.s1[:, H].indirect(T.exl[:, 0:8]), T.keyt[:, H], A.is_equal, ["s1" + k, "exl", "keyt" + k], ["eqt" + k])
+            tt(T.pd[:, H], T.p4[:, H], T.eqt[:, H], A.mult, ["dt", "eqt" + k], ["pd" + k], ["p4"])
+            scan(T.s2[:, H], T.zr[:, H], T.pd[:, H], A.mult, A.add, ["zr", "pd" + k], ["s2" + k])
+        for e in (0, 1):
+            for h in (0, 1):
+                mm(T.p7[:, e:16:2], T.sw[:, 128 * (2 * e + h):128 * (2 * e + h) + 128], T.s2[:, 15 + 16 * h::32], h == 0, h == 1,
+                   ["sw", "s20", "s21"], ["a0"], ["p7"])
+        ts(T.fl[:], T.s1[:, 15::16], 0.0, A.is_ge, ["s10", "s11"], ["fl"])
+        vtr(T.oh[:], T.eqt[:], ["eqt0", "eqt1"], ["oh"])
+        cp(T.a016[:], T.p7[:, 0:16], ["a0"], ["a016"], ["p7"])
+        mm(T.p7[:, 32:48], T.ones[:], T.fl[:], True, True, ["ones", "fl"], ["nn"], ["p7"])
+        sa, ra = T.sa[:, t:t + 1], T.ra[:, t:t + 1]
+        act(T.nj[:], T.p7[:, 32:48], ["nn"], ["nj", "n"], ["p7"], accum_out=col(16))
+        act(col(17), col(16), ["n"], ["n1"], scale=1.0 / 256, bias=-0.498046875)
+        act(col(20), col(16), ["n"], ["n4"], scale=0.5, bias=-0.25)
+        act(col(18), col(17), ["n1"], ["n2"], bias=MAG)
+        act(col(19), col(18), ["n2"], ["n3"], bias=-MAG)
+        act(sa, col(19), ["n3", "n4"], ["sa%d" % t], scale=-128.0, bias=col(20))
+        send(t, "a", sa, "sa%d" % t, ra, "ra%d" % t)
+        if t == 0:
+            places_past_the_end(1)
+        if t:
+            act(T.ev[:], T.yv1[:], ["yv1"], ["ev"], func=F.Relu, scale=-1.0, bias=1.0)
+        tt(T.w1[:], T.pvr[:].indirect(T.a016[:]), T.dg[:], A.mult, ["pvr", "a016", "dg"], ["w1"])
+        scan(T.sc1[:], T.zr[:], T.w1[:], A.mult, A.add, ["zr", "w1"], ["sc1"])
+        cp(T.bl[:, 0:16], T.sc1[:, 15::16], ["sc1"], ["bl0"])
+        tt(T.w2[:], T.pvr[:].indirect(T.bl[:, 0:16]), T.dg[:], A.mult, ["pvr", "bl0", "dg"], ["w2"])
+        tt(T.xc[:, 0:256], T.xt[:, 0:2048].indirect(T.bl[:, 0:16]), Q[:], A.is_lt, ["xt", "bl0", qk], ["xc0"])
+        sums(T.p7, lambda k: T.xc[:, k:256:16], ["xc0"], 16, 32, "p7", "b1")
+        scan(T.sc2[:], T.zr[:], T.w2[:], A.mult, A.add, ["zr", "w2"], ["sc2"])
+        cp(T.bl[:, 16:32], T.sc2[:, 15::16], ["sc2"], ["bl1"])
+        tt(T.xc[:, 256:512], T.xt[:, 0:2048].indirect(T.bl[:, 16:32]), Q[:], A.is_lt, ["xt", "bl1", qk], ["xc1"])
+        sums(T.p0, lambda k: T.xc[:, 256 + k::16], ["xc1"], 0, 16, "p0", "b2")
+        mm(T.p5[:, 0:256], T.b4[:], T.zz[:], True, False, ["b4", "zz"], ["ca_"], ["p5"])
+        mm(T.p3[:, 0:256], T.idb[:], T.tri[:], True, False, ["idb", "tri"], ["da"], ["p3"])
+        mm(T.p1[:, 256:512], T.idb[:], Q[:], True, False, ["idb", qk], ["xq"], ["p1"])
+        mm(T.p6[:, 0:256], T.idfn[:], T.dd[:], True, False, ["idfn", "dd"], ["ad"], ["p6"])
+        tt(T.d1[:], T.sc1[:, 15::16], T.p7[:, 0:16], A.subtract, ["sc1", "a0"], ["d1"], ["p7"])
+        ts(T.f1[:], T.p7[:, 16:32], 9.0 * FAR, A.is_lt, ["b1"], ["f1"], ["p7"])
+        tt(T.d2[:], T.sc2[:, 15::16], T.sc1[:, 15::16], A.subtract, ["sc1", "sc2"], ["d2"])
+        tt(T.d1[:], T.d1[:], T.f1[:], A.mult, ["d1", "f1"], ["d1"])
+        tt(T.d2[:], T.d2[:], T.f1[:], A.mult, ["d2", "f1"], ["d2"])
+        tt(T.d1[:], T.d1[:], T.p7[:, 0:16], A.add, ["d1", "a0"], ["d1"], ["p7"])
+        ts(T.f2[:], T.p0[:, 0:16], 9.0 * FAR, A.is_lt, ["b2"], ["f2"], ["p0"])
+        tt(T.f2[:], T.f2[:], T.d2[:], A.mult, ["f2", "d2"], ["f2"])
+        tt(T.al[:], T.f2[:], T.d1[:], A.add, ["f2", "d1"], ["al"])
+        cp(T.al16[:], T.al[:], ["al"], ["al16"])
+        tt(T.w3[:], T.rcr[:].indirect(T.al16[:]), T.dg[:], A.mult, ["rcr", "al16", "dg"], ["w3"])
+        act(T.ar32[:], T.idw[:].indirect(T.al16[:]), ["idw", "al16"], ["ar32"])
+        act(T.ax[:], T.al[:].indirect(T.exc[:]), ["al", "exc"], ["ax"])
+        act(T.xga[:], T.xt[:, 0:2048].indirect(T.al16[:]), ["xt", "al16"], ["xga"])
+        if not last:
+            tt(T.w4[:], T.nxr[:, 0:2048].indirect(T.al16[:]), T.dg[:], A.mult, ["nxr", "al16", "dg"], ["w4"])
+        scan(T.sc3[:], T.zr[:], T.w3[:], A.mult, A.add, ["zr", "w3"], ["sc3"])
+        if not last:
+            scan(T.sc4[:], T.zr[:], T.w4[:], A.mult, A.add, ["zr", "w4"], ["sc4"])
+        ts(T.ws[:], T.sc3[:, 15::16], col(4), A.mult, ["sc3", "c4"], ["ws"])
+        wrt, wk = T["wr%d" % t], "wr%d" % t
+        send(t, "w", T.ws[:], "ws", wrt[:], wk)
+        if not last:
+            cp(T.nl16[:], T.sc4[:, 15::16], ["sc4"], ["nl16"])
+        cp(T.ar[:], T.ar32[:], ["ar32"], ["ar"])
+        ts(T.we[:], T.sc3[:, 15::16], col(5), A.mult, ["sc3", "c5"], ["we"])
+        if t:
+            for m, (o, n) in enumerate([(-256, 256)] + SEG):
+                mm(T.p2[:, 256 - n:256], T.b4[:], T.ev[:, 256 + o:256 + o + n], m == 0, m == 15, ["b4", "ev"], ["cv_"], ["p2"])
+        mm(T.p3[:, 0:256], T.idfn[:], T.ax[:], False, False, ["idfn", "ax"], ["da"], ["p3"])
+        mm(T.p1[:, 256:512], T.idb[:], T.xga[:], False, True, ["idb", "xga"], ["xq"], ["p1"])
+        mm(T.p3[:, 0:256], T.idh[:], T.ar[:], False, True, ["idh", "ar"], ["da"], ["p3"])
+        mm(T.p6[:, 0:256], T.idh[:], T.ar[:], False, True, ["idh", "ar"], ["ad"], ["p6"])
+        if not last:
+            act(T.nx2[:], T.nxr[:, 0:2048].indirect(T.nl16[:]), ["nxr", "nl16"], ["nx2"])
+        act(T.h1[:], T.p1[:, 256:512], ["xq"], ["h1"], ["p1"], scale=0.5, bias=0.25)
+        qrt = T["qr%d" % t]
+        act(T.yy[:, 0::2], Q[:, 0::2], [qk, "sa%d" % t], ["yy0"], scale=0.5, bias=sa)
+        act(T.h1[:], T.h1[:], ["h1"], ["h2"], bias=MAG)
+        act(T.yy[:, 1::2], qrt[:], ["qr%d" % t, "ra%d" % t], ["yy1"], scale=0.5, bias=ra)
+        act(T.xn[:], T.h1[:], ["h2"], ["xn"], bias=-MAG)
+        act(T.y2[:], T.yy[:], ["yy0", "yy1"], ["y2"], bias=MAG)
+        act(QN[:], T.y2[:], ["y2"], [qnk], bias=-MAG)
+        if not last:
+            act(T.qo[:], QN[:, 1::2], [qnk], ["qo"])
+            send(t + 1, "q", T.qo[:], "qo", T["qr%d" % (t + 1)][:], "qr%d" % (t + 1))
+            repeat_q(range(16 - GK, 16), QN, qnk)
+            for k in range(16 - GK):
+                act(T.q16[:, k::16], T.y2[:], ["y2"], ["q16"], bias=-MAG)
+        else:
+            dma("y", "out", 64, [qnk], ["yq"], T.yq[:], QN[:])
+        for m, (o, n) in enumerate(SEG):
+            ts(T.em[:, o:o + n], T.ar[:, 256 - n:256], T.al[:, m:m + 1], A.is_equal, ["ar", "al"], ["em%d" % m])
+            mm(T.p5[:, 256 - n:256], T.b4[:], T.em[:, o:o + n], False, False, ["b4", "em%d" % m], ["ca_"], ["p5"])
+        ts(T.ed[:], T.p3[:, 0:256], 0.0, A.is_equal, ["da"], ["ed"], ["p3"])
+        mm(T.p5[:, 0:256], T.b4[:], T.ed[:], False, True, ["b4", "ed"], ["ca_"], ["p5"])
+        tt(T.tk[:], T.p6[:, 0:256], T.oh[:], A.mult, ["ad", "oh"], ["ut"], ["p6"])
+        jobs = [("ca_", "p5", T.dgt, "dgt", T.al, "al", T.ap16, "ap16", (T.dm, T.ds, T.lx))]
+        if t:
+            jobs = [("cv_", "p2", T.dgu, "dgu", T.vl, "vl", T.vp16, "vp16", (T.w1, T.sc1, T.d1))] + jobs
+        places(jobs)
+        if not last:
+            cp(T.nxr[:].indirect(T.ap16[:]), T.nx2[:], ["nx2", "ap16"], ["nxr"])
+            dma("y", "nd%d" % t, 16, ["nxr"], ["npf"], T.npf[:], T.nxr[0:128:16, 0:2048])
+        cp(T.xt[:].indirect(T.ap16[:]), T.xn[:], ["xn", "ap16"], ["xt"])
+        if last:
+            dma("y", "out", 64, ["xt"], ["yx"], T.yx[:], T.xt[:, 0:2048])
+        tt(T.vl[:], T.we[:], wrt[:], A.add, ["we", wk], ["vl"])
+        if last:
+            cp(T.vl16[:], T.vl[:], ["vl"], ["vl16"])
+        tt(T.uw[:].indirect(T.vp16[:]), T.tk[:], T.dd[:], A.add, ["ut", "dd", "vp16"], ["uw"])
+        if last:
+            dma("y", "out", 64, ["uw"], ["yu"], T.yu[:], T.uw[:, 0:512])
+        else:
+            cp(T.vl16[:], T.vl[:], ["vl"], ["vl16"])
+        Q, QN, qk, qnk = QN, Q, qnk, qk
+    act(T.vr[:], T.idw[:].indirect(T.vl16[:]), ["idw", "vl16"], ["vr"])
+    dma("y", "out", 64, ["vr"], ["yv"], T.yv[:], T.vr[0:128:16, :])
+    for s in SEMAPHORES:
+        if total.get(s, 0) > known["p"].get(s, 0):
+            g.wait_ge(T.sem[s], total[s])

@@ -3,55 +3,41 @@ from concourse.bass import DstId, RemoteDMATransfer
 from concourse.mybir import dt, AluOpType as A, AxisListType, ActivationFunctionType as F
 
 SCRATCH = {}
-for _n, _c, _d in (
-        ("xt", 2304, "bfloat16"), ("x1", 2048, "bfloat16"), ("x2", 2048, "bfloat16"), ("x3", 2048, "bfloat16"),
-        ("x4", 2048, "bfloat16"), ("q16", 4096, "bfloat16"), ("qa", 256, "bfloat16"), ("qb", 256, "bfloat16"),
-        ("qo", 128, "bfloat16"), ("qr0", 128, "bfloat16"), ("qr1", 128, "bfloat16"), ("qr2", 128, "bfloat16"),
-        ("xg", 4096, "bfloat16"), ("ab", 4096, "bfloat16"), ("ca", 4096, "bfloat16"), ("cb", 4096, "bfloat16"),
-        ("xg4", 2048, "bfloat16"), ("sg4", 2048, "bfloat16"),
-        ("uw", 768, "float32"), ("ui", 512, "int32"), ("i16", 128, "bfloat16"), ("i32", 128, "bfloat16"), ("k8", 128, "bfloat16"), ("kk1", 128, "bfloat16"), ("nxr", 2304, "float32"),
-        ("pvr", 2048, "int32"), ("rcr", 2048, "int32"), ("idw", 2048, "float32"),
-        ("npi", 128, "int32"), ("npf", 128, "float32"), ("nxl", 128, "uint16"),
-        ("dd", 256, "float32"), ("d16", 256, "uint16"), ("vl", 16, "float32"), ("vl16", 16, "uint16"),
-        ("vn", 16, "float32"), ("vr", 256, "float32"), ("vx", 256, "float32"), ("yv1", 2176, "bfloat16"), ("ev", 2176, "bfloat16"),
-        ("ar", 256, "float16"), ("ar32", 256, "float32"), ("ax", 256, "float32"), ("ed", 256, "bfloat16"),
-        ("em", 1920, "bfloat16"), ("zz", 256, "bfloat16"),
-        ("dm", 256, "float32"), ("ds", 256, "float32"), ("lx", 16, "float32"),
-        ("vp16", 16, "uint16"), ("ap16", 16, "uint16"), ("m1", 256, "float32"), ("nph", 128, "float16"), ("npt", 128, "float16"),
-        ("rr", 768, "bfloat16"), ("tk", 256, "float32"),
-        ("key", 256, "float32"), ("keyt", 256, "float32"), ("s1", 256, "float32"), ("eqt", 256, "float32"),
-        ("pd", 256, "float32"), ("s2", 256, "float16"), ("oh", 256, "float32"), ("fl", 16, "bfloat16"),
-        ("a016", 16, "uint16"), ("w1", 256, "float32"), ("sc1", 256, "float32"), ("w2", 256, "float32"),
-        ("sc2", 256, "float32"), ("bl", 32, "uint16"), ("xc", 512, "bfloat16"),
-        ("f1", 16, "float32"), ("d1", 16, "float32"), ("d2", 16, "float32"), ("f2", 16, "float32"), ("al", 16, "float32"),
-        ("al16", 16, "uint16"), ("w3", 256, "float32"), ("sc3", 256, "float32"), ("w4", 256, "float32"),
-        ("sc4", 256, "float32"), ("ws", 16, "float32"), ("we", 16, "float32"), ("wr0", 16, "float32"),
-        ("wr1", 16, "float32"), ("wr2", 16, "float32"), ("nl16", 16, "uint16"), ("nx2", 256, "float32"),
-        ("xga", 256, "bfloat16"), ("h1", 256, "float32"), ("xn", 256, "bfloat16"),
-        ("nj", 16, "float32"), ("cols", 64, "float32"), ("yy", 256, "float32"), ("y2", 256, "float32"),
-        ("ci", 64, "int32"), ("cf", 256, "float32"), ("cg", 128, "float32"), ("ch", 128, "float32"),
-        ("dg", 256, "float32"), ("dgt", 256, "float32"), ("dgu", 256, "float32"), ("tri", 256, "bfloat16"),
-        ("rst", 256, "float32"), ("zr", 256, "float32"), ("ek", 2048, "bfloat16"), ("cc", 128, "bfloat16"),
-        ("b4", 128, "bfloat16"), ("idf", 128, "float32"), ("idfn", 128, "float32"), ("idb", 128, "bfloat16"),
-        ("idn", 128, "bfloat16"), ("idh", 128, "float16"), ("sw", 512, "float16"), ("ones", 128, "bfloat16"),
-        ("exl", 16, "uint16"), ("exc", 16, "uint16"), ("sa", 4, "float32"), ("ra", 4, "float32")):
-    _d = {"w1": "float16", "w2": "float16", "w3": "float16", "w4": "float16", "sc1": "float16", "sc2": "float16",
-          "sc3": "float16", "sc4": "float16", "dm": "float16", "ds": "float16", "pd": "float16",
-          "zr": "bfloat16", "eqt": "bfloat16", "oh": "bfloat16"}.get(_n, _d)
-    SCRATCH[_n] = ("sbuf", [128, 2560 if _c == 2304 else _c], _d)
+for _d, _names in (
+        ("bfloat16", (("xt", 2560), ("nxb", 2560), ("rcb", 2048), ("x1", 2048), ("x2", 2048), ("x3", 2048), ("x4", 2048),
+                      ("q16", 4096), ("qa", 256), ("qb", 256), ("qo", 128), ("qr0", 128), ("qr1", 128), ("qr2", 128),
+                      ("xg", 4096), ("ab", 4096), ("ca", 4096), ("cb", 4096), ("xg4", 2048), ("sg4", 2048), ("rr", 768),
+                      ("eq", 256), ("fl", 16), ("xc", 512), ("f3", 48), ("em", 1920), ("ed", 256), ("yv1", 2176),
+                      ("ev", 2176), ("vf", 256), ("gg", 512), ("nx2", 256), ("xga", 256), ("xn", 256),
+                      ("hl", 512), ("ch", 144), ("cg", 128), ("cf", 256), ("dg", 256), ("zr", 256), ("tri", 256),
+                      ("wf", 144), ("w2", 144), ("b8f", 8), ("b8g", 8), ("bs", 16), ("b4", 128),
+                      ("base", 256), ("idb", 128), ("idn", 128), ("i4k", 128), ("i4n", 128), ("ones", 128))),
+        ("float16", (("nph", 128), ("npt", 128), ("sw", 512), ("idh", 128), ("ihn", 128), ("b8h", 8), ("b8n", 8),
+                     ("pd", 256), ("ex", 256), ("w1", 256), ("wb", 256), ("sc1", 256), ("sc2", 256), ("ar", 256),
+                     ("az", 256), ("ax", 256), ("vrh", 256), ("vlh", 16), ("dm", 256), ("ds", 256))),
+        ("float32", (("uw", 768), ("idw", 2048), ("dd", 256), ("vl", 16), ("vn", 16), ("vr", 256), ("lx", 16), ("lc", 16),
+                     ("ka", 256), ("key", 256), ("s1", 256), ("s2", 256), ("a3", 48), ("u1", 256), ("u2", 256),
+                     ("ws", 16), ("we", 16), ("wr0", 16), ("wr1", 16), ("wr2", 16), ("h1", 256), ("yy", 256), ("y2", 256),
+                     ("nj", 32), ("nk", 16), ("cols", 32), ("dgt", 256), ("rst", 256), ("idf", 128),
+                     ("sa", 4), ("ra", 4))),
+        ("int32", (("ui", 512), ("pvr", 2048), ("npi", 128), ("rpi", 128), ("ci", 16))),
+        ("uint16", (("nxl", 128), ("d16", 256), ("vl16", 16), ("vp16", 16), ("ap16", 16), ("a016", 16), ("bl", 32),
+                    ("al16", 16), ("nl16", 16), ("exl", 8)))):
+    for _n, _c in _names:
+        SCRATCH[_n] = ("sbuf", [128, _c], _d)
 for _k in range(8):
     SCRATCH["p%d" % _k] = ("psum", [128, 512], "float32")
 
-SCRATCH["nxd"] = ("dram", [8, 2048], "float32")
-
 ROUNDS = 3
-LSS = (64, 64, 64)
-XV0, XV = 512, 1024
-SEMAPHORES = ["cv", "cs", "ct", "cp", "ldx", "ldq", "ldu", "ldn", "ldr", "ldd", "ldp", "ldc", "nd0", "nd1", "out"]
+LS = 64
+XV0, XV = 896, 768
+SEMAPHORES = ["cv", "cs", "ct", "cp", "ldx", "ldq", "ldu", "ldn", "ldr", "ldp", "ldb", "ldc", "out"]
 for _t in range(ROUNDS):
     SEMAPHORES += ["%s%d" % (_a, _t) for _a in ("rq", "ra", "rw", "lq", "la", "lw")]
-GK0, GK = 4, 8
-VM = 0
+G0, S0 = 1, 8
+GE, GO = 9, 9
+CA = 2
+MV = 7
 FAR = 262144.0
 BIG = 1048576.0
 MAG = 12582912.0
@@ -163,8 +149,8 @@ def rank_program(g, core, T, topo):
     def vtr(out, in_, R, W, X=()):
         op("v", R, W, X, lambda: V.transpose(out, in_))
 
-    def scan(out, d0, d1, o0, o1, R, W):
-        op("v", R, W, [], lambda: V.tensor_tensor_scan(out, d0, d1, 0.0, o0, o1))
+    def scan(out, d0, d1, o0, o1, R, W, X=()):
+        op("v", R, W, X, lambda: V.tensor_tensor_scan(out, d0, d1, 0.0, o0, o1))
 
     def mm(out, l, r, st, sp, R, W, X):
         op("t", R, W, X, lambda: P.matmul(out, l, r, st, sp))
@@ -175,138 +161,109 @@ def rank_program(g, core, T, topo):
         else:
             op("p", [], W, [], lambda: g.iota(out, pat, base, cm, allow_small_or_imprecise_dtypes=True))
 
+    def gcopy(out, in_, n, R, W):
+        op("p", R, W, [], lambda: g.affine_select(out, in_, [[0, n]], A.is_gt, 0.0, 1, 0))
+
     def col(j):
         return T.cols[:, j:j + 1]
 
+    def to_list(out, w, wk, src, sk, n, dk, pk, st=True, sp=True):
+        for k in range(16):
+            mm(out, w[:, 15 - k:143 - k], src[:, k:16 * n:16], st and k == 0, sp and k == 15, [wk, sk], [dk], [pk])
+
+    def by_lane(pout, o, src, s0, l0, l1, w, wk, keys, dk, pk, alone, close=False):
+        n = w.shape[1]
+        for k in range(16):
+            mm(pout[l0 % 128:(l1 - 1) % 128 + 1, o + k:o + 16 * n:16], src[:, 16 * (l0 - s0) + k:16 * (l1 - s0):16], w[:],
+               alone, alone or (close and k == 15), [wk] + keys, [dk], [pk])
+
+    Q16 = ["q16v", "q16g", "q16h", "q16s"]
+
     dma("y", "ldn", 16, [], ["npi"], T.npi[:], T.nx[:])
-    dma("y", "ldx", 16, [], ["xt"], T.xt[:, 0:2048], T.xd[:])
     dma("s", "ldq", 16, [], ["qa"], T.qa[:], T.mv[:])
-    dma("s", "ldu", 16, [], ["ui"], T.ui[:], T.ul[:])
-    for s, dst, src, k in (("ldp", T.pvr, T.pv, "pvr"), ("ldc", T.rcr, T.rc, "rcr")):
-        for i in range(16):
-            dma("y", s, 256, ["xt", "ui", "qa"], [k], dst[i:128:16, :], src[:])
+    dma("y", "ldx", 16, [], ["xt"], T.xt[:, 0:2048], T.xd[:])
+    dma("y", "ldu", 16, [], ["ui"], T.ui[:], T.ul[:])
+    dma("s", "ldr", 16, [], ["rpi"], T.rpi[:], T.rc[:])
+    for i in range(16):
+        dma("y", "ldp", 256, ["xt", "ui", "qa"], ["pvr"], T.pvr[i:128:16, :], T.pv[:])
 
-    def repeat_nx():
-        dma("y", "ldd", 16, ["npf"], ["nxd"], T.nxd[:], T.npf[:])
-        for i in range(16):
-            dma("y", "ldr", 256, ["nxd"], ["nxr"], T.nxr[i:128:16, 0:2048], T.nxd[:])
-
-    iota(T.ch[:], [[1, 128]], 0, -1, ["ch"])
     iota(T.ci[:, 0:1], [[0, 1]], 0, 1, ["ci0"], True)
-    iota(T.cf[:], [[0, 16], [1, 16]], 0, 0, ["cf"])
+    iota(T.ch[:], [[1, 144]], 0, -1, ["ch"])
     iota(T.cg[:], [[1, 8], [0, 16]], 0, 0, ["cg"])
-    ts(T.idf[:], T.ch[:], 0.0, A.is_equal, ["ch"], ["idf"])
-    op("v", ["ci0"], ["ci3"], [], lambda: V.tensor_scalar(T.ci[:, 1:2], T.ci[:, 0:1], 15, None, A.bitwise_and))
+    iota(T.cf[:], [[0, 16], [1, 16]], 0, 0, ["cf"])
+    iota(T.ci[:, 8:16], [[16, 8]], 15, 0, ["ci1"], True)
     op("v", ["ci0"], ["ci4"], [], lambda: V.tensor_scalar(T.ci[:, 2:3], T.ci[:, 0:1], 4, None, A.arith_shift_right))
+    op("v", ["ci0"], ["ci3"], [], lambda: V.tensor_scalar(T.ci[:, 1:2], T.ci[:, 0:1], 15, None, A.bitwise_and))
     op("v", ["ci0"], ["ci6"], [], lambda: V.tensor_scalar(T.ci[:, 4:5], T.ci[:, 0:1], 1, None, A.bitwise_and))
-    cp(col(0), T.ci[:, 1:2], ["ci3"], ["c0"])
-    cp(col(1), T.ci[:, 2:3], ["ci4"], ["c1"])
     op("v", ["ci4"], ["ci5"], [], lambda: V.tensor_scalar(T.ci[:, 3:4], T.ci[:, 2:3], 1, None, A.bitwise_and))
+    cp(T.cols[:, 0:2], T.ci[:, 1:3], ["ci3", "ci4"], ["c0", "c1"])
     cp(col(4), T.ci[:, 4:5], ["ci6"], ["c4"])
-    ts(T.idb[:], T.ch[:], 0.0, A.is_equal, ["ch"], ["idb"])
     cp(col(2), T.ci[:, 3:4], ["ci5"], ["c2"])
     ts(col(3), T.ci[:, 3:4], 0.0, A.is_equal, ["ci5"], ["c3"])
-    ts(T.idn[:], T.ch[:], 0.0, A.is_equal, ["ch"], ["idn"], (), -1.0, A.mult)
-    ts(T.m1[:, 0:128], T.cg[:], col(1), A.is_equal, ["cg", "c1"], ["bs"])
-    ts(T.m1[:, 128:256], T.cf[:, 0:128], 1.0, A.add, ["cf"], ["cg2"])
-    tt(T.cc[:], T.m1[:, 0:128], T.m1[:, 128:256], A.mult, ["bs", "cg2"], ["cc"])
+    ts(col(7), T.ci[:, 1:2], -1.0, A.mult, ["ci3"], ["c7"], (), 15.0, A.add)
+    ts(col(9), T.ci[:, 1:2], 2.0, A.is_lt, ["ci3"], ["c9"])
+    C = T.ch[:, 0:128]
+    for j, (x, c) in enumerate(((0.0, 3), (16.0, 3), (-16.0, 2), (0.0, 2))):
+        ts(T.sw[:, 128 * j:128 * j + 128], C, x, A.is_equal, ["ch", "c%d" % c], ["sw"], (), col(c), A.mult)
+    for w, k, x in ((T.idb, "idb", 1.0), (T.idh, "idh", 1.0), (T.ihn, "ihn", -1.0)):
+        ts(w[:], C, 0.0, A.is_equal, ["ch"], [k], (), x, A.mult)
+    ts(T.wf[:], T.ch[:], col(7), A.is_equal, ["ch", "c7"], ["wf"], (), FAR, A.mult)
+    ts(T.w2[:], T.ch[:], col(7), A.is_equal, ["ch", "c7", "c9"], ["w2"], (), col(9), A.mult)
+    for w, k, x in ((T.b8f[:], "b8f", FAR), (T.b8h[:], "b8h", 1.0), (T.b8n[:], "b8n", -1.0)):
+        ts(w, T.cg[:, 0:128:16], col(1), A.is_equal, ["cg", "c1"], [k], (), x, A.mult)
+    ts(T.b4[:], T.cg[:], col(1), A.is_equal, ["cg", "c1"], ["b4"], (), 4096.0, A.mult)
+    ts(T.dg[:], T.cf[:], col(0), A.is_equal, ["cf", "c0"], ["dg"])
+    cp(T.exl[:], T.ci[:, 8:16], ["ci1"], ["exl"])
+    act(col(8), col(0), ["c0"], ["c8"], bias=0.5)
+    act(col(5), col(4), ["c4"], ["c5"], scale=-1.0, bias=1.0)
+    act(col(6), col(0), ["c0"], ["c6"], scale=2.0)
+    act(T.ones[:], T.cg[:], ["cg"], ["ones"], scale=0.0, bias=1.0)
+    for w, k, x in ((T.idn, "idn", -1.0), (T.i4k, "i4k", 4096.0), (T.i4n, "i4n", -4096.0), (T.idf, "idf", 1.0)):
+        act(w[:], T.idb[:], ["idb"], [k], scale=x)
+    for w, k, x in ((T.b8g[:], "b8g", 0.5), (T.bs[:, 0:8], "bs", 16.0 / FAR), (T.bs[:, 8:16], "bs", -16.0 / FAR)):
+        act(w, T.b8f[:], ["b8f"], [k], scale=x)
+    act(T.base[:, 0:128], T.cg[:], ["cg"], ["base"], scale=0.0, bias=-8.5 * FAR)
+    for p in range(0, 128, 32):
+        act(T.base[p:p + 32, 128:256], T.cg[p:p + 32, :], ["cg"], ["base"], scale=0.0, bias=(-8.5 if p < 128 - LS else -0.5) * FAR)
+    act(T.qo[:], T.qa[:, 1::2], ["qa"], ["qo"])
+    iota(T.nj[:], [[512, 2], [16, 16]], 0, 0, ["nj"])
+    iota(T.dgt[:], [[2, 256]], 2048, 0, ["dgt"])
+    for k in range(G0):
+        gcopy(T.q16[:, k::16], T.qa[:], 256, ["qa"], ["q16g"])
+    send(0, "q", T.qo[:], "qo", T.qr0[:], "qr0")
+    for k in range(G0, G0 + S0):
+        act(T.q16[:, k::16], T.qa[:], ["qa"], ["q16s"])
+    iota(T.idw[:], [[1, 2048]], 0, 0, ["idw"])
+    iota(T.rcb[:], [[0, 2048]], 0, 0, ["rcb"])
+    iota(T.nxb[:, 0:2048], [[0, 2048]], 0, 0, ["nxb"])
+    cp(T.nph[:], T.npi[:], ["npi"], ["nph"])
+    vtr(T.npt[:], T.nph[:], ["nph"], ["npt"])
+    for e in (0, 1):
+        for b in range(4):
+            for h in (0, 1):
+                mm(T.p7[:, 128 + 2 * b + e:256:8], T.sw[:, 128 * (2 * e + h):128 * (2 * e + h) + 128],
+                   T.npt[:, 32 * b + 16 * h:32 * b + 16 * h + 16], h == 0, h == 1, ["sw", "npt"], ["nxt"], ["p7"])
+    for k in range(G0 + S0, 16):
+        cp(T.q16[:, k::16], T.qa[:], ["qa"], ["q16v"])
+    cp(T.nxl[:], T.p7[:, 128:256], ["nxt"], ["nxl"], ["p7"])
+
+    def two_parts(o, src, sk, tab, tk, sem):
+        cp(T.hl[:, o:o + 128], src[:], [sk], ["hi" + sk])
+        tt(T.hl[:, o + 128:o + 256], src[:], T.hl[:, o:o + 128], A.subtract, [sk, "hi" + sk], ["lo" + sk])
+        for j, k in enumerate(("hi" + sk, "lo" + sk)):
+            dma("y", sem, 32, [k], [tk], tab[j:128:16, 0:2048], T.hl[:, o + 128 * j:o + 128 * j + 128])
+
+    two_parts(256, T.rpi, "rpi", T.rcb, "rcb", "ldc")
+    two_parts(0, T.nph, "nph", T.nxb, "nxb", "ldb")
+    ts(T.vl[:], T.nj[:, 0:16], 2.0, A.mult, ["nj", "c6"], ["vl"], (), col(6), A.add)
+    ts(T.lc[:], T.nj[:, 16:32], col(0), A.add, ["nj", "c0"], ["lc"])
+    cp(T.vp16[:], T.vl[:], ["vl"], ["vp16"])
+    ts(T.az[:], T.cf[:], 0.0, A.mult, ["cf"], ["az"])
+    tt(T.dgt[:], T.dgt[:], T.dg[:], A.mult, ["dgt", "dg"], ["dgt"])
     act(T.zr[:], T.cf[:], ["cf"], ["zr"], func=F.Sign)
     act(T.rst[:], T.zr[:], ["zr"], ["rst"], scale=-2.0 * BIG, bias=BIG)
-    act(col(8), col(0), ["c0"], ["c8"], bias=0.5)
-    act(T.y2[:], T.cf[:], ["cf", "c8"], ["tri0"], scale=-1.0, bias=col(8), func=F.Sign)
-    act(T.tri[:], T.y2[:], ["tri0"], ["tri"], scale=4096.0, func=F.Relu)
-    act(T.qo[:], T.qa[:, 1::2], ["qa"], ["qo"])
-    send(0, "q", T.qo[:], "qo", T.qr0[:], "qr0")
-
-    def repeat_q(ks, q, qk):
-        for k in ks:
-            op("p", [qk], ["q16g"], [], lambda: g.affine_select(T.q16[:, k::16], q[:], [[0, 256]], A.is_gt, 0.0, 1, 0))
-
-    repeat_q(range(16 - GK0, 16), T.qa, "qa")
-    iota(T.ci[:, 16:32], [[16, 16]], 15, 0, ["ci1"], True)
-    iota(T.ci[:, 32:48], [[1, 16]], 0, 0, ["ci2"], True)
-    iota(T.nj[:], [[32, 16]], 0, 0, ["nj"])
-    iota(T.dgt[:], [[2, 256]], 2048, 0, ["dgt0"])
-    iota(T.dgu[:], [[1, 256]], 512, 0, ["dgu0"])
-    iota(T.idw[:], [[1, 2048]], 0, 0, ["idw"])
-
-    def make_ek(ks):
-        for k in ks:
-            ts(T.ek[:, 128 * k:128 * k + 128], T.cc[:], float(k + 1), A.is_equal, ["cc"], ["ek"], (), FAR, A.mult)
-
-    make_ek(range(8))
-    cp(T.d16[:], T.ui[:, 0:512:2], ["ui"], ["d16"])
-    cp(T.nph[:], T.npi[:], ["npi"], ["nph"])
-    cp(T.npf[:], T.npi[:], ["npi"], ["npf"])
-    repeat_nx()
-
-    def list_of_nx():
-        vtr(T.npt[:], T.nph[:], ["nph"], ["npt"])
-        for e in (0, 1):
-            for b in range(4):
-                for h in (0, 1):
-                    mm(T.p7[:, 2 * b + e:128:8], T.sw[:, 128 * (2 * e + h):128 * (2 * e + h) + 128],
-                       T.npt[:, 32 * b + 16 * h:32 * b + 16 * h + 16], h == 0, h == 1, ["sw", "npt"], ["nxt"], ["p7"])
-
-    for j, (x, c) in enumerate(((0.0, 3), (16.0, 3), (-16.0, 2), (0.0, 2))):
-        ts(T.sw[:, 128 * j:128 * j + 128], T.ch[:], x, A.is_equal, ["ch", "c%d" % c], ["sw"], (), col(c), A.mult)
-    list_of_nx()
-    make_ek(range(8, 16))
-    cp(T.nxl[:], T.p7[:, 0:128], ["nxt"], ["nxl"], ["p7"])
-    cp(T.dd[:], T.ui[:, 0:512:2], ["ui"], ["dd"])
-
-    def first_fill():
-        for k in range(16 - GK0):
-            cp(T.q16[:, k::16], T.qa[:], ["qa"], ["q16"])
-        vtr(T.p4[:, 0:256], T.dd[:], ["dd"], ["dt"], ["p4"])
-
-    def constants_on_scalar():
-        act(col(5), col(4), ["c4"], ["c5"], scale=-1.0, bias=1.0)
-        act(col(6), col(0), ["c0"], ["c6"], scale=2.0)
-        act(col(7), col(0), ["c0"], ["c7"], bias=65536.0)
-        act(col(9), col(0), ["c0"], ["c9"], bias=-65536.0)
-        for w, k, x in ((T.i16, "i16", 16.0), (T.i32, "i32", 32.0), (T.k8, "k8", -8.4 * FAR), (T.kk1, "kk1", -FAR)):
-            act(w[:], T.idb[:], ["idb"], [k], scale=x)
-        act(T.idfn[:], T.idf[:], ["idf"], ["idfn"], scale=-1.0)
-        act(T.ones[:], T.cf[:, 0:128], ["cf"], ["ones"], scale=0.0, bias=1.0)
-        act(T.zz[:], T.cf[:], ["cf"], ["zz"], scale=0.0)
-
-    def constants_on_vector():
-        ts(T.dg[:], T.cf[:], col(0), A.is_equal, ["cf", "c0"], ["dg"])
-
-    def later_constants():
-        ts(T.b4[:], T.cc[:], 0.0, A.is_gt, ["cc"], ["b4"], (), 4096.0, A.mult)
-        ts(T.idh[:], T.ch[:], 0.0, A.is_equal, ["ch"], ["idh"])
-        cp(T.exl[:], T.ci[:, 16:32], ["ci1"], ["exl"])
-        cp(T.exc[:], T.ci[:, 32:48], ["ci2"], ["exc"])
-        ts(T.vl[:], T.nj[:], col(6), A.add, ["nj", "c6"], ["vl"])
-        cp(T.vp16[:], T.vl[:], ["vl"], ["vp16"])
-        cp(T.uw[:, 0:512], T.ui[:], ["ui"], ["uw"])
-
-    def places_past_the_end(step):
-        if step == 0:
-            act(T.yy[:], T.dg[:], ["dg"], ["dgs"], scale=4096.0, bias=-4096.0)
-        for w, k, pb in ((T.dgt, "dgt", "p4"), (T.dgu, "dgu", "p5")):
-            pw = T[pb][:, 256:512]
-            if step == 0:
-                mm(pw, T.idf[:], w[:], True, False, ["idf", k + "0"], [k + "p"], [pb])
-                mm(pw, T.idf[:], T.yy[:], False, True, ["idf", "dgs"], [k + "p"], [pb])
-            else:
-                act(w[:], pw, [k + "p"], [k], [pb], func=F.Relu)
-
-    def places(jobs):
-        for cb, pk, dgx, dk, al, alk, out16, outk, (dm, ds, lx) in jobs:
-            tt(dm[:], T[pk][:, 0:256], dgx[:], A.min, [cb, dk], ["dm" + pk], [pk])
-        for cb, pk, dgx, dk, al, alk, out16, outk, (dm, ds, lx) in jobs:
-            scan(ds[:], T.zr[:], dm[:], A.mult, A.add, ["zr", "dm" + pk], ["ds" + pk])
-        for cb, pk, dgx, dk, al, alk, out16, outk, (dm, ds, lx) in jobs:
-            tt(lx[:], ds[:, 15::16], al[:], A.max, ["ds" + pk, alk], ["lx" + pk])
-        for cb, pk, dgx, dk, al, alk, out16, outk, (dm, ds, lx) in jobs:
-            cp(out16[:], lx[:], ["lx" + pk], [outk])
-
-    def sums(pout, src, keys, l0, l1, pk, dk):
-        for k in range(16):
-            mm(pout[:, l0:l1], T.ek[:, 128 * k:128 * k + 128], src(k), k == 0, k == 15, ["ek"] + keys, [dk], [pk])
+    act(T.vf[:], T.cf[:], ["cf", "c8"], ["vf"], scale=-1.0, bias=col(8), func=F.Sign)
+    act(T.tri[:], T.vf[:], ["vf"], ["tri"], scale=4096.0, func=F.Relu)
 
     SEG = [(0, 0)] * 15
     _o = 0
@@ -314,257 +271,315 @@ def rank_program(g, core, T, topo):
         SEG[m] = (_o, 240 - 16 * m)
         _o += 240 - 16 * m
 
-    Q, QN, qk, qnk = T.qa, T.qb, "qa", "qb"
+    def new_places(t, first=True, second=True):
+        if first:
+            if t:
+                tt(T.lx[:], T.p2[:, 256:272], T.lc[:], A.min, ["cvl", "lc"], ["lx"], ["p2"])
+                cp(T.vp16[:], T.lx[:], ["lx"], ["vp16"])
+            tt(T.uw[:].indirect(T.vp16[:]), T.u1[:], T.u2[:], A.max, ["u1", "u2", "vp16"], ["uw"])
+        if second:
+            tt(T.vl[:], T.we[:], T["wr%d" % t][:], A.add, ["we", "wr%d" % t], ["vl"])
+            cp(T.vl16[:], T.vl[:], ["vl"], ["vl16"])
+
+    Q, QN, qk, qnk = T.qa, T.qb, ["qa"], ["qbe", "qbo"]
+    LV = 256 - LS
+    X0 = T.xt[:, 0:2048]
     for t in range(ROUNDS):
         last = t == ROUNDS - 1
-        LS = LSS[t]
-        LV = 256 - LS
         xv = XV if t else XV0
 
         def walk(x, xk, out, ok, l0, l1):
             tt(out[:, 16 * l0:16 * l1], x[:].indirect(T.d16[:, l0:l1]), T.q16[:, 16 * l0:16 * l1], A.is_lt,
-               xk + ["d16", "q16", "q16g"], [ok + str(l0)])
+               xk + ["d16"] + Q16, [ok + str(l0)])
 
-        def wsum(pout, out, ok, l0, l1, pk, dk):
-            sums(pout, lambda k: out[:, 16 * l0 + k:16 * l1:16], [ok + str(l0)], l0, l1, pk, dk + str(l0))
+        def wsum(pout, o, out, ok, h, pk, dk):
+            by_lane(pout, o + 128 * h, out, 0, 128 * h, 128 * h + 128, T.b8f, "b8f", [ok + str(128 * h)], dk + str(h), pk, True)
 
         def diff(c, src, sk, lane0):
             pk = ("p2", "p3")[c % 2]
             j = 512 * c
             mm(T[pk][:], T.idb[:], src[:, j:j + 512], True, False, ["idb", sk], [pk + "d"], [pk])
-            mm(T[pk][:], T.idn[:], T.q16[:, 16 * lane0 + j:16 * lane0 + j + 512], False, True, ["idn", "q16", "q16g"], [pk + "d"], [pk])
+            mm(T[pk][:], T.idn[:], T.q16[:, 16 * lane0 + j:16 * lane0 + j + 512], False, True, ["idn"] + Q16, [pk + "d"], [pk])
 
         def absc(c):
             pk = ("p2", "p3")[c % 2]
             act(T.ab[:, 512 * c:512 * c + 512], T[pk][:], [pk + "d"], ["ab%d" % (c // 4)], [pk], func=F.Abs)
 
         def marks(l0, l1, k):
-            act(T.xg[:, 16 * l0:16 * l1], T.xt[:, 0:2048].indirect(T.d16[:, l0:l1]), ["xt", "d16"], [k])
+            act(T.xg[:, 16 * l0:16 * l1], X0.indirect(T.d16[:, l0:l1]), ["xt", "d16"], [k])
 
+        def scores(h):
+            pk = ("p4", "p5")[h]
+            mm(T[pk][:, 0:256], T.idb[:], T.cf[:], True, False, ["idb", "cf"], ["sc%d" % h], [pk])
+            by_lane(T[pk], 0, T.ab, 0, 128 * h, 128 * h + 128, T.bs, "bs", ["ab%d" % h], "sc%d" % h, pk, False)
+            mm(T[pk][:, 256:384], T.dd[:, 128 * h:128 * h + 128], T.idf[:], False, True, ["dd", "idf"], ["sc%d" % h], [pk])
+
+        def lower(h):
+            pk = ("p4", "p5")[h]
+            act(T.ka[:, 128 * h:128 * h + 128], T[pk][:, 0:128], ["sc%d" % h], ["ka%d" % h], [pk], bias=-0.5 * FAR)
+
+        def over(j, pp, o, keys, pk):
+            act(T.rr[:, 256 * j:256 * j + 256], pp[:, o:o + 256], keys, ["rr%d" % j], [pk], func=F.Relu, scale=16.0, bias=-128.0 * FAR)
+
+        act(T.x1[:, xv:2048], X0.indirect(T.nxl[:, xv // 16:128]), ["xt", "nxl"], ["x1b"])
+        cp(T.x1[:, 0:xv], X0.indirect(T.nxl[:, 0:xv // 16]), ["xt", "nxl"], ["x1a"])
         if t:
+            new_places(t - 1)
             cp(T.d16[:], T.uw[:, 0:512].indirect(T.vl16[:]), ["uw", "vl16"], ["d16"])
-            act(T.dd[:], T.uw[:, 0:512].indirect(T.vl16[:]), ["uw", "vl16"], ["dd"])
-            marks(VM, 64, "xga0")
-            vtr(T.p4[:, 0:256], T.dd[:], ["dd"], ["dt"], ["p4"])
-            if VM:
-                cp(T.xg[:, 0:16 * VM], T.xt[:, 0:2048].indirect(T.d16[:, 0:VM]), ["xt", "d16"], ["xgv"])
-            cp(T.nph[:], T.npf[:], ["npf"], ["nph"])
-            list_of_nx()
-            cp(T.nxl[:], T.p7[:, 0:128], ["nxt"], ["nxl"], ["p7"])
-            cp(T.x1[:, 0:xv], T.xt[:, 0:2048].indirect(T.nxl[:, 0:xv // 16]), ["xt", "nxl"], ["x1a"])
+            cp(T.vlh[:], T.vl[:], ["vl"], ["vlh"])
         else:
-            constants_on_scalar()
-        act(T.x1[:, xv:2048], T.xt[:, 0:2048].indirect(T.nxl[:, xv // 16:128]), ["xt", "nxl"], ["x1b"])
-        if t == 0:
-            marks(0, 64, "xga0")
-            first_fill()
-            cp(T.x1[:, 0:xv], T.xt[:, 0:2048].indirect(T.nxl[:, 0:xv // 16]), ["xt", "nxl"], ["x1a"])
-            constants_on_vector()
-            places_past_the_end(0)
+            cp(T.d16[:], T.ui[:, 0:512:2], ["ui"], ["d16"])
+            cp(T.dd[:], T.ui[:, 0:512:2], ["ui"], ["dd"])
         act(T.x2[:], T.x1[:].indirect(T.nxl[:]), ["x1a", "x1b", "nxl"], ["x2"])
         walk(T.x1, ["x1a", "x1b"], T.ca, "ca", 0, 128)
+        marks(0, 64, "xga0")
         marks(64, 128, "xgb0")
-        diff(0, T.xg, "xgv" if t and VM == 32 else "xga0", 0)
+        wsum(T.p0, 0, T.ca, "ca", 0, "p0", "k1")
+        diff(0, T.xg, "xga0", 0)
         diff(1, T.xg, "xga0", 0)
-        wsum(T.p0, T.ca, "ca", 0, 128, "p0", "k1")
         walk(T.x1, ["x1a", "x1b"], T.ca, "ca", 128, 256)
         absc(0)
         absc(1)
+        wsum(T.p0, 0, T.ca, "ca", 1, "p0", "k1")
         diff(2, T.xg, "xgb0", 0)
         diff(3, T.xg, "xgb0", 0)
+        act(T.x3[:], T.x2[:].indirect(T.nxl[:]), ["x2", "nxl"], ["x3"])
         absc(2)
         absc(3)
-        wsum(T.p0, T.ca, "ca", 128, 256, "p0", "k1")
-        act(T.x3[:], T.x2[:].indirect(T.nxl[:]), ["x2", "nxl"], ["x3"])
-        act(T.rr[:, 0:256], T.p0[:, 0:256], ["k10", "k1128"], ["rr0"], ["p0"], func=F.Relu, bias=-8.0 * FAR)
-        if t == 0:
-            act(T.x4[:], T.x3[:].indirect(T.nxl[:]), ["x3", "nxl"], ["x4"])
-        marks(128, 256, "xg1")
+        if t:
+            act(T.dd[:], T.uw[:, 0:512].indirect(T.vl16[:]), ["uw", "vl16"], ["dd"])
+        over(0, T.p0, 0, ["k10", "k11"], "p0")
+        marks(128, 192, "xga1")
         walk(T.x2, ["x2"], T.cb, "cb", 0, 128)
-        sums(T.p5, lambda k: T.ab[:, k:2048:16], ["ab0"], 0, 128, "p5", "sc0")
-        wsum(T.p1, T.cb, "cb", 0, 128, "p1", "k2")
+        wsum(T.p1, 0, T.cb, "cb", 0, "p1", "k2")
+        scores(0)
+        act(T.x4[:], T.x3[:].indirect(T.nxl[:]), ["x3", "nxl"], ["x4"])
         walk(T.x2, ["x2"], T.cb, "cb", 128, 256)
-        wsum(T.p1, T.cb, "cb", 128, 256, "p1", "k2")
-        walk(T.x3, ["x3"], T.ca, "ca", 0, 128)
-        if t == 0:
-            wsum(T.p0, T.ca, "ca", 0, 128, "p0", "k3")
-        diff(4, T.xg, "xg1", 0)
-        diff(5, T.xg, "xg1", 0)
+        wsum(T.p1, 0, T.cb, "cb", 1, "p1", "k2")
+        diff(4, T.xg, "xga1", 0)
+        diff(5, T.xg, "xga1", 0)
         absc(4)
         absc(5)
-        diff(6, T.xg, "xg1", 0)
-        diff(7, T.xg, "xg1", 0)
-        if t:
-            act(T.x4[:], T.x3[:].indirect(T.nxl[:]), ["x3", "nxl"], ["x4"])
+        marks(192, 256, "xgb1")
+        walk(T.x3, ["x3"], T.ca, "ca", 0, 128)
+        wsum(T.p0, 256, T.ca, "ca", 0, "p0", "k3")
+        over(1, T.p1, 0, ["k20", "k21"], "p1")
+        lower(0)
+        act(T.xg4[:, 0:16 * LS], T.x4[:].indirect(T.d16[:, LV:256]), ["x4", "d16"], ["xg4"])
+        walk(T.x3, ["x3"], T.ca, "ca", 128, 256)
+        wsum(T.p0, 256, T.ca, "ca", 1, "p0", "k3")
+        diff(6, T.xg, "xgb1", 0)
+        diff(7, T.xg, "xgb1", 0)
         absc(6)
         absc(7)
-        if t:
-            wsum(T.p0, T.ca, "ca", 0, 128, "p0", "k3")
-        walk(T.x3, ["x3"], T.ca, "ca", 128, 256)
-        act(T.rr[:, 256:512], T.p1[:, 0:256], ["k20", "k2128"], ["rr1"], ["p1"], func=F.Relu, bias=-8.0 * FAR)
-        if t == 0:
-            sums(T.p5, lambda k: T.ab[:, 2048 + k::16], ["ab1"], 128, 256, "p5", "sc1")
-        wsum(T.p0, T.ca, "ca", 128, 256, "p0", "k3")
-        if t:
-            sums(T.p5, lambda k: T.ab[:, 2048 + k::16], ["ab1"], 128, 256, "p5", "sc1")
-        act(T.xg4[:, 0:16 * LS], T.x4[:].indirect(T.d16[:, LV:256]), ["x4", "d16"], ["xg4"])
+        walk(T.x4, ["x4"], T.cb, "cb", 0, 128)
+
+        FOURTH = ((T.p1, 256, "p1"), (T.p6, 0, "p6"))
+
+        def on_top(h, src, sk, st, sp):
+            pp, o, pk = FOURTH[h]
+            mm(pp[:, o:o + 128], T.idb[:], src, st, sp, ["idb", sk], ["k4%d" % h], [pk])
+
+        mm(T.p7[:, 16:64:3], T.idn[:], T.base[:, 0:16], True, True, ["idn", "base"], ["b0"], ["p7"])
+        for h in (0, 1):
+            on_top(h, T.base[:, 128 * h:128 * h + 128], "base", True, False)
+            for j in range(2):
+                on_top(h, T.rr[:, 256 * j + 128 * h:256 * j + 128 * h + 128], "rr%d" % j, False, False)
+        over(2, T.p0, 256, ["k30", "k31"], "p0")
+        for c in range(LS // 32):
+            diff(c, T.xg4, "xg4", LV)
+        on_top(0, T.rr[:, 512:640], "rr2", False, False)
+        by_lane(T.p1, 256, T.cb, 0, 0, 128, T.b8f, "b8f", ["cb0"], "k40", "p1", False, True)
+        scores(1)
         for c in range(LS // 32):
             pk = ("p2", "p3")[c % 2]
-            diff(c, T.xg4, "xg4", LV)
             act(T.sg4[:, 512 * c:512 * c + 512], T[pk][:], [pk + "d"], ["sg4"], [pk], func=F.Sign, scale=-1.0, bias=-0.5)
-            if c == 0:
-                act(T.m1[:], T.p5[:, 0:256], ["sc0", "sc1", "c9"], ["ka"], ["p5"], scale=16.0 / FAR, bias=col(9))
-                act(T.p6[:, 256:512], T.p5[:, 0:256], ["sc0", "sc1", "c7"], ["kb"], ["p5", "p6"], scale=-16.0 / FAR, bias=col(7))
-        walk(T.x4, ["x4"], T.cb, "cb", 0, 128)
-        act(T.rr[:, 512:768], T.p0[:, 0:256], ["k30", "k3128"], ["rr2"], ["p0"], func=F.Relu, bias=-8.0 * FAR)
-
-        def fourth(pout, p0, pk, w, wk, base, bk, src, sk, l0, l1, dk):
-            po = pout[:, p0 + l0:p0 + l1]
-            mm(po, base[:], T.ones[:, 0:l1 - l0], True, False, [bk, "ones"], [dk], [pk])
-            for j in range(2):
-                mm(po, w[:], T.rr[:, 256 * j + l0:256 * j + l1], False, False, [wk, "rr%d" % j], [dk], [pk])
-            for k in range(16):
-                mm(po, T.ek[:, 128 * k:128 * k + 128], src(k), False, False, ["ek", sk], [dk], [pk])
-            mm(po, w[:], T.rr[:, 512 + l0:512 + l1], False, True, [wk, "rr2"], [dk], [pk])
-
+        lower(1)
         walk(T.x4, ["x4"], T.cb, "cb", 128, LV)
-        fourth(T.p1, 0, "p1", T.i16, "i16", T.k8, "k8", lambda k: T.cb[:, k:2048:16], "cb0", 0, 128, "k40")
-        fourth(T.p5, 0, "p5", T.i32, "i32", T.kk1, "kk1", lambda k: T.sg4[:, k:16 * LS:16], "sg4", LV, 256, "k4s")
-        fourth(T.p0, 256, "p0", T.i16, "i16", T.k8, "k8", lambda k: T.cb[:, 2048 + k:16 * LV:16], "cb128", 128, LV, "k4128")
-        if t == 0:
-            later_constants()
+        by_lane(T.p6, 0, T.cb, 0, 128, LV, T.b8f, "b8f", ["cb128"], "k41", "p6", False)
+        by_lane(T.p6, 0, T.sg4, LV, LV, 256, T.b8g, "b8g", ["sg4"], "k41", "p6", False)
+        on_top(1, T.rr[:, 640:768], "rr2", False, True)
         if t:
-            act(T.vn[:], T.vl[:], ["vl"], ["vn"], scale=-1.0)
-            act(T.vx[:], T.vl[:].indirect(T.exc[:]), ["vl", "exc"], ["vx"])
             act(T.vr[:], T.idw[:].indirect(T.vl16[:]), ["idw", "vl16"], ["vr"])
-            mm(T.p3[:, 0:256], T.idfn[:], T.vx[:], True, False, ["idfn", "vx"], ["dv"], ["p3"])
-            mm(T.p3[:, 0:256], T.idf[:], T.vr[:], False, False, ["idf", "vr"], ["dv"], ["p3"])
-            mm(T.p3[:, 0:256], T.idb[:], T.tri[:], False, True, ["idb", "tri"], ["dv"], ["p3"])
-            for m, (o, n) in enumerate(SEG):
-                act(T.yv1[:, 256 + o:256 + o + n], T.vr[:, 256 - n:256], ["vr", "vn"], ["yv1"], func=F.Abs, bias=T.vn[:, m:m + 1])
-            act(T.yv1[:, 0:256], T.p3[:, 0:256], ["dv"], ["yv1"], ["p3"], func=F.Abs)
-        for h, parts in enumerate((((T.p1, "p1", 0, "k40", 0, 128),), ((T.p5, "p5", 0, "k4s", LV, 256), (T.p0, "p0", 256, "k4128", 128, LV)))):
-            H, k = slice(128 * h, 128 * h + 128), str(h)
-            for pp, pk, po, ck, l0, l1 in parts:
-                tt(T.tk[:, l0:l1], pp[:, po + l0:po + l1], T.m1[:, l0:l1], A.max, ["ka", ck], ["tk" + k], [pk])
-            tt(T.key[:, H], T.p6[:, 256 + 128 * h:384 + 128 * h], T.tk[:, H], A.min, ["tk" + k, "kb"], ["key" + k], ["p6"])
-            vtr(T.keyt[:, H], T.key[:, H], ["key" + k], ["keyt" + k])
-            scan(T.s1[:, H], T.rst[:, H], T.keyt[:, H], A.max, A.min, ["rst", "keyt" + k], ["s1" + k])
-            tt(T.eqt[:, H], T.s1[:, H].indirect(T.exl[:, 0:8]), T.keyt[:, H], A.is_equal, ["s1" + k, "exl", "keyt" + k], ["eqt" + k])
-            tt(T.pd[:, H], T.p4[:, H], T.eqt[:, H], A.mult, ["dt", "eqt" + k], ["pd" + k], ["p4"])
+            act(T.vn[:], T.vl[:], ["vl"], ["vn"], scale=-1.0)
+            for m in range(MV, 15):
+                o, n = SEG[m]
+                act(T.yv1[:, o:o + n], T.vr[:, 256 - n:256], ["vr", "vn"], ["yv1"], func=F.Abs, bias=T.vn[:, m:m + 1])
+        for h, (pp, pk, o) in enumerate(((T.p1, "p1", 256), (T.p6, "p6", 0))):
+            H, k, ps = slice(128 * h, 128 * h + 128), str(h), ("p4", "p5")[h]
+            tt(T.key[:, H], pp[:, o:o + 128], T.ka[:, H], A.max, ["ka" + k, "k4" + k], ["key" + k], [pk])
+            tt(T.key[:, H], T[ps][:, 128:256], T.key[:, H], A.min, ["key" + k, "sc" + k], ["key" + k], [ps])
+            scan(T.s1[:, H], T.rst[:, H], T.key[:, H], A.max, A.min, ["rst", "key" + k], ["s1" + k])
+            tt(T.eq[:, H], T.s1[:, H].indirect(T.exl[:]), T.key[:, H], A.is_equal, ["s1" + k, "exl", "key" + k], ["eq" + k])
+            tt(T.pd[:, H], T[ps][:, 256:384], T.eq[:, H], A.mult, ["sc" + k, "eq" + k], ["pd" + k], [ps])
             scan(T.s2[:, H], T.zr[:, H], T.pd[:, H], A.mult, A.add, ["zr", "pd" + k], ["s2" + k])
-        for e in (0, 1):
-            for h in (0, 1):
-                mm(T.p7[:, e:16:2], T.sw[:, 128 * (2 * e + h):128 * (2 * e + h) + 128], T.s2[:, 15 + 16 * h::32], h == 0, h == 1,
-                   ["sw", "s20", "s21"], ["a0"], ["p7"])
-        ts(T.fl[:], T.s1[:, 15::16], 0.0, A.is_ge, ["s10", "s11"], ["fl"])
-        vtr(T.oh[:], T.eqt[:], ["eqt0", "eqt1"], ["oh"])
-        cp(T.a016[:], T.p7[:, 0:16], ["a0"], ["a016"], ["p7"])
-        mm(T.p7[:, 32:48], T.ones[:], T.fl[:], True, True, ["ones", "fl"], ["nn"], ["p7"])
+            if h:
+                ts(T.fl[:], T.s1[:, 15::16], -65536.0, A.is_ge, ["s10", "s11"], ["fl"])
+            tt(T.ex[:, H], T.s2[:, H].indirect(T.exl[:]), T.dg[:, 0:128], A.mult, ["s2" + k, "exl", "dg"], ["ex" + k])
+            if h:
+                mm(T.p4[:, 400:416], T.ones[:], T.fl[:], True, True, ["ones", "fl"], ["nn"], ["p4"])
+            mm(T.p7[:, 8 * h:8 * h + 8], T.ex[:, H], T.b8h[:], True, True, ["ex" + k, "b8h"], ["a0" + k], ["p7"])
+        cp(T.a016[:], T.p7[:, 0:16], ["a00", "a01"], ["a016"], ["p7"])
         sa, ra = T.sa[:, t:t + 1], T.ra[:, t:t + 1]
-        act(T.nj[:], T.p7[:, 32:48], ["nn"], ["nj", "n"], ["p7"], accum_out=col(16))
+        act(T.nk[:], T.p4[:, 400:416], ["nn"], ["nk", "n"], ["p4"], accum_out=col(16))
         act(col(17), col(16), ["n"], ["n1"], scale=1.0 / 256, bias=-0.498046875)
         act(col(20), col(16), ["n"], ["n4"], scale=0.5, bias=-0.25)
         act(col(18), col(17), ["n1"], ["n2"], bias=MAG)
         act(col(19), col(18), ["n2"], ["n3"], bias=-MAG)
         act(sa, col(19), ["n3", "n4"], ["sa%d" % t], scale=-128.0, bias=col(20))
         send(t, "a", sa, "sa%d" % t, ra, "ra%d" % t)
-        if t == 0:
-            places_past_the_end(1)
+        act(T.yy[:, 0:128], Q[:, 0::2], qk + ["sa%d" % t], ["yy0"], scale=0.5, bias=sa)
+        act(T.y2[:, 0:128], T.yy[:, 0:128], ["yy0"], ["y20"], bias=MAG)
+        act(QN[:, 0::2], T.y2[:, 0:128], ["y20"], [qnk[0]], bias=-MAG)
+        if not last:
+            for k in range(GE):
+                gcopy(T.q16[:, k::32], QN[:, 0::2], 128, [qnk[0]], ["q16g"])
+        for h in (0, 1):
+            mm(T.p6[:, 128 + 24 * h + 2:128 + 24 * h + 24:3], T.ex[:, 128 * h:128 * h + 128], T.b8h[:], True, True,
+               ["ex%d" % h, "b8h"], ["d3"], ["p6"])
         if t:
-            act(T.ev[:], T.yv1[:], ["yv1"], ["ev"], func=F.Relu, scale=-1.0, bias=1.0)
+            mm(T.p2[:, 0:256], T.idf[:], T.vr[:], True, False, ["idf", "vr"], ["dv"], ["p2"])
+            for j in range(16):
+                mm(T.p2[:, j:256:16], T.ihn[:], T.vlh[:], False, False, ["ihn", "vlh"], ["dv"], ["p2"])
+            mm(T.p2[:, 0:256], T.idb[:], T.tri[:], False, True, ["idb", "tri"], ["dv"], ["p2"])
+        if not last:
+            for k in range(GE, 16):
+                act(T.q16[:, k::32], T.y2[:, 0:128], ["y20"], ["q16s"], bias=-MAG)
+        if t:
+            o = SEG[MV][0]
+            act(T.yv1[:, 1920:2176], T.p2[:, 0:256], ["dv"], ["yv1"], ["p2"], func=F.Abs)
+            act(T.ev[:, o:2176], T.yv1[:, o:2176], ["yv1"], ["ev"], func=F.Relu, scale=-1.0, bias=1.0)
+
+        def equal_v(ms):
+            for m in ms:
+                o, n = SEG[m]
+                ts(T.ev[:, o:o + n], T.vrh[:, 256 - n:256], T.vl[:, m:m + 1], A.is_equal, ["vrh", "vl"], ["evv"])
+
         tt(T.w1[:], T.pvr[:].indirect(T.a016[:]), T.dg[:], A.mult, ["pvr", "a016", "dg"], ["w1"])
         scan(T.sc1[:], T.zr[:], T.w1[:], A.mult, A.add, ["zr", "w1"], ["sc1"])
         cp(T.bl[:, 0:16], T.sc1[:, 15::16], ["sc1"], ["bl0"])
-        tt(T.w2[:], T.pvr[:].indirect(T.bl[:, 0:16]), T.dg[:], A.mult, ["pvr", "bl0", "dg"], ["w2"])
-        tt(T.xc[:, 0:256], T.xt[:, 0:2048].indirect(T.bl[:, 0:16]), Q[:], A.is_lt, ["xt", "bl0", qk], ["xc0"])
-        sums(T.p7, lambda k: T.xc[:, k:256:16], ["xc0"], 16, 32, "p7", "b1")
-        scan(T.sc2[:], T.zr[:], T.w2[:], A.mult, A.add, ["zr", "w2"], ["sc2"])
+        tt(T.wb[:], T.pvr[:].indirect(T.bl[:, 0:16]), T.dg[:], A.mult, ["pvr", "bl0", "dg"], ["wb"])
+        tt(T.xc[:, 0:256], X0.indirect(T.bl[:, 0:16]), Q[:], A.is_lt, ["xt", "bl0"] + qk, ["xc0"])
+        for h in (0, 1):
+            po = T.p6[:, 128 + 24 * h + 1:128 + 24 * h + 24:3]
+            mm(po, T.ex[:, 128 * h:128 * h + 128], T.b8n[:], True, False, ["ex%d" % h, "b8n"], ["d3"], ["p6"])
+            mm(po, T.idh[:], T.sc1[:, 128 * h + 15:128 * h + 128:16], False, True, ["idh", "sc1"], ["d3"], ["p6"])
+        to_list(T.p7[:, 18:64:3], T.wf, "wf", T.xc, "xc0", 16, "b1", "p7")
+        scan(T.sc2[:], T.zr[:], T.wb[:], A.mult, A.add, ["zr", "wb"], ["sc2"])
         cp(T.bl[:, 16:32], T.sc2[:, 15::16], ["sc2"], ["bl1"])
-        tt(T.xc[:, 256:512], T.xt[:, 0:2048].indirect(T.bl[:, 16:32]), Q[:], A.is_lt, ["xt", "bl1", qk], ["xc1"])
-        sums(T.p0, lambda k: T.xc[:, 256 + k::16], ["xc1"], 0, 16, "p0", "b2")
-        mm(T.p5[:, 0:256], T.b4[:], T.zz[:], True, False, ["b4", "zz"], ["ca_"], ["p5"])
-        mm(T.p3[:, 0:256], T.idb[:], T.tri[:], True, False, ["idb", "tri"], ["da"], ["p3"])
-        mm(T.p1[:, 256:512], T.idb[:], Q[:], True, False, ["idb", qk], ["xq"], ["p1"])
-        mm(T.p6[:, 0:256], T.idfn[:], T.dd[:], True, False, ["idfn", "dd"], ["ad"], ["p6"])
-        tt(T.d1[:], T.sc1[:, 15::16], T.p7[:, 0:16], A.subtract, ["sc1", "a0"], ["d1"], ["p7"])
-        ts(T.f1[:], T.p7[:, 16:32], 9.0 * FAR, A.is_lt, ["b1"], ["f1"], ["p7"])
-        tt(T.d2[:], T.sc2[:, 15::16], T.sc1[:, 15::16], A.subtract, ["sc1", "sc2"], ["d2"])
-        tt(T.d1[:], T.d1[:], T.f1[:], A.mult, ["d1", "f1"], ["d1"])
-        tt(T.d2[:], T.d2[:], T.f1[:], A.mult, ["d2", "f1"], ["d2"])
-        tt(T.d1[:], T.d1[:], T.p7[:, 0:16], A.add, ["d1", "a0"], ["d1"], ["p7"])
-        ts(T.f2[:], T.p0[:, 0:16], 9.0 * FAR, A.is_lt, ["b2"], ["f2"], ["p0"])
-        tt(T.f2[:], T.f2[:], T.d2[:], A.mult, ["f2", "d2"], ["f2"])
-        tt(T.al[:], T.f2[:], T.d1[:], A.add, ["f2", "d1"], ["al"])
-        cp(T.al16[:], T.al[:], ["al"], ["al16"])
-        tt(T.w3[:], T.rcr[:].indirect(T.al16[:]), T.dg[:], A.mult, ["rcr", "al16", "dg"], ["w3"])
-        act(T.ar32[:], T.idw[:].indirect(T.al16[:]), ["idw", "al16"], ["ar32"])
-        act(T.ax[:], T.al[:].indirect(T.exc[:]), ["al", "exc"], ["ax"])
-        act(T.xga[:], T.xt[:, 0:2048].indirect(T.al16[:]), ["xt", "al16"], ["xga"])
-        if not last:
-            tt(T.w4[:], T.nxr[:, 0:2048].indirect(T.al16[:]), T.dg[:], A.mult, ["nxr", "al16", "dg"], ["w4"])
-        scan(T.sc3[:], T.zr[:], T.w3[:], A.mult, A.add, ["zr", "w3"], ["sc3"])
-        if not last:
-            scan(T.sc4[:], T.zr[:], T.w4[:], A.mult, A.add, ["zr", "w4"], ["sc4"])
-        ts(T.ws[:], T.sc3[:, 15::16], col(4), A.mult, ["sc3", "c4"], ["ws"])
-        wrt, wk = T["wr%d" % t], "wr%d" % t
-        send(t, "w", T.ws[:], "ws", wrt[:], wk)
-        if not last:
-            cp(T.nl16[:], T.sc4[:, 15::16], ["sc4"], ["nl16"])
-        cp(T.ar[:], T.ar32[:], ["ar32"], ["ar"])
-        ts(T.we[:], T.sc3[:, 15::16], col(5), A.mult, ["sc3", "c5"], ["we"])
+        tt(T.xc[:, 256:512], X0.indirect(T.bl[:, 16:32]), Q[:], A.is_lt, ["xt", "bl1"] + qk, ["xc1"])
+        mm(T.p6[:, 128:176:3], T.ihn[:], T.sc1[:, 15::16], True, False, ["ihn", "sc1"], ["d3"], ["p6"])
+        mm(T.p6[:, 128:176:3], T.idh[:], T.sc2[:, 15::16], False, True, ["idh", "sc2"], ["d3"], ["p6"])
+        for k in range(16):
+            mm(T.p7[:, 17:64:3], T.wf[:, 15 - k:143 - k], T.xc[:, 256 + k::16], k == 0, k == 15, ["wf", "xc1"], ["b2"], ["p7"])
+        mm(T.p0[:, 0:256], T.idb[:], T.tri[:], True, False, ["idb", "tri"], ["da"], ["p0"])
+        mm(T.p4[:, 0:256], T.idf[:], T.dd[:], True, False, ["idf", "dd"], ["u1p"], ["p4"])
+        for h in (0, 1):
+            mm(T.p4[:, 128 * h:128 * h + 128], T.eq[:, 128 * h:128 * h + 128], T.i4n[:], False, h == 1, ["eq%d" % h, "i4n"], ["u1p"], ["p4"])
         if t:
-            for m, (o, n) in enumerate([(-256, 256)] + SEG):
-                mm(T.p2[:, 256 - n:256], T.b4[:], T.ev[:, 256 + o:256 + o + n], m == 0, m == 15, ["b4", "ev"], ["cv_"], ["p2"])
-        mm(T.p3[:, 0:256], T.idfn[:], T.ax[:], False, False, ["idfn", "ax"], ["da"], ["p3"])
-        mm(T.p1[:, 256:512], T.idb[:], T.xga[:], False, True, ["idb", "xga"], ["xq"], ["p1"])
-        mm(T.p3[:, 0:256], T.idh[:], T.ar[:], False, True, ["idh", "ar"], ["da"], ["p3"])
-        mm(T.p6[:, 0:256], T.idh[:], T.ar[:], False, True, ["idh", "ar"], ["ad"], ["p6"])
+            cp(T.vrh[:], T.vr[:], ["vr"], ["vrh"])
+            equal_v(range(MV // 2))
+        ts(T.f3[:], T.p7[:, 16:64], 8.25 * FAR, A.is_lt, ["b0", "b1", "b2"], ["f3"], ["p7"])
+        scan(T.a3[:], T.f3[:], T.p6[:, 128:176], A.mult, A.add, ["f3", "d3"], ["al"], ["p6"])
+        cp(T.al16[:], T.a3[:, 2::3], ["al"], ["al16"])
+        cp(T.az[:, 0::16], T.a3[:, 2::3], ["al"], ["az"])
+        cp(T.ar[:], T.idw[:].indirect(T.al16[:]), ["idw", "al16"], ["ar"])
+        scan(T.ax[:], T.zr[:], T.az[:], A.mult, A.add, ["zr", "az"], ["ax"])
+        act(T.gg[:, 0:256], T.rcb[:].indirect(T.al16[:]), ["rcb", "al16"], ["gg"])
         if not last:
-            act(T.nx2[:], T.nxr[:, 0:2048].indirect(T.nl16[:]), ["nxr", "nl16"], ["nx2"])
-        act(T.h1[:], T.p1[:, 256:512], ["xq"], ["h1"], ["p1"], scale=0.5, bias=0.25)
-        qrt = T["qr%d" % t]
-        act(T.yy[:, 0::2], Q[:, 0::2], [qk, "sa%d" % t], ["yy0"], scale=0.5, bias=sa)
-        act(T.h1[:], T.h1[:], ["h1"], ["h2"], bias=MAG)
-        act(T.yy[:, 1::2], qrt[:], ["qr%d" % t, "ra%d" % t], ["yy1"], scale=0.5, bias=ra)
-        act(T.xn[:], T.h1[:], ["h2"], ["xn"], bias=-MAG)
-        act(T.y2[:], T.yy[:], ["yy0", "yy1"], ["y2"], bias=MAG)
-        act(QN[:], T.y2[:], ["y2"], [qnk], bias=-MAG)
+            act(T.gg[:, 256:512], T.nxb[:, 0:2048].indirect(T.al16[:]), ["nxb", "al16"], ["gg"])
+        act(T.xga[:], X0.indirect(T.al16[:]), ["xt", "al16"], ["xga"])
+        mm(T.p1[:, 0:256], T.idh[:], T.ar[:], True, False, ["idh", "ar"], ["ca_"], ["p1"])
+        mm(T.p0[:, 0:256], T.idh[:], T.ar[:], False, False, ["idh", "ar"], ["da"], ["p0"])
+        mm(T.p0[:, 0:256], T.ihn[:], T.ax[:], False, True, ["ihn", "ax"], ["da"], ["p0"])
+        nl = 16 if last else 32
+
+        def equal_a(ms):
+            for m in ms:
+                o, n = SEG[m]
+                ts(T.em[:, o:o + n], T.ar[:, 256 - n:256], T.a3[:, 3 * m + 2:3 * m + 3], A.is_equal, ["ar", "al"], ["em%d" % m])
+
+        def count_a(ms):
+            for m in ms:
+                o, n = SEG[m]
+                mm(T.p1[:, 256 - n:256], T.b4[:], T.em[:, o:o + n], False, False, ["b4", "em%d" % m], ["ca_"], ["p1"])
+
+        equal_a(range(10))
+        ts(T.ed[:], T.p0[:, 0:256], 0.0, A.is_equal, ["da"], ["ed"], ["p0"])
+        equal_a(range(10, 15))
+        count_a(range(CA))
+        to_list(T.p6[:, 192:192 + nl], T.w2, "w2", T.gg, "gg", nl, "wl", "p6")
         if not last:
-            act(T.qo[:], QN[:, 1::2], [qnk], ["qo"])
+            cp(T.nl16[:], T.p6[:, 208:224], ["wl"], ["nl16"], ["p6"])
+        act(T.ws[:], T.p6[:, 192:208], ["wl", "c4"], ["ws"], ["p6"], scale=col(4))
+        send(t, "w", T.ws[:], "ws", T["wr%d" % t][:], "wr%d" % t)
+        if not last:
+            act(T.nx2[:], T.nxb[:, 0:2048].indirect(T.nl16[:]), ["nxb", "nl16"], ["nx2"])
+        act(T.we[:], T.p6[:, 192:208], ["wl", "c5"], ["we"], ["p6"], scale=col(5))
+        act(T.yy[:, 128:256], T["qr%d" % t][:], ["qr%d" % t, "ra%d" % t], ["yy1"], scale=0.5, bias=ra)
+        act(T.y2[:, 128:256], T.yy[:, 128:256], ["yy1"], ["y21"], bias=MAG)
+        if not last:
+            act(T.qo[:], T.y2[:, 128:256], ["y21"], ["qo"], bias=-MAG)
+        if t:
+            equal_v(range(MV // 2, MV))
+        else:
+            cp(T.uw[:, 0:512], T.ui[:], ["ui"], ["uw"])
+
+        def x_and_q():
+            mm(T.p3[:, 256:512], T.idb[:], Q[:], True, False, ["idb"] + qk, ["xq"], ["p3"])
+            mm(T.p3[:, 256:512], T.idb[:], T.xga[:], False, True, ["idb", "xga"], ["xq"], ["p3"])
+
+        if last:
+            x_and_q()
+        count_a(range(CA, 15))
+        mm(T.p1[:, 0:256], T.b4[:], T.ed[:], False, True, ["b4", "ed"], ["ca_"], ["p1"])
+        if not last:
+            x_and_q()
+        act(T.u1[:], T.p4[:, 0:256], ["u1p"], ["u1"], ["p4"])
+        act(T.h1[:], T.p3[:, 256:512], ["xq"], ["h1"], ["p3"], scale=0.5 + 1.0 / 2048, bias=MAG)
+        act(T.xn[:], T.h1[:], ["h1"], ["xn"], bias=-MAG)
+        mm(T.p5[:, 0:256], T.idh[:], T.ar[:], True, False, ["idh", "ar"], ["u2p"], ["p5"])
+        for h in (0, 1):
+            mm(T.p5[:, 128 * h:128 * h + 128], T.eq[:, 128 * h:128 * h + 128], T.i4k[:], False, h == 1, ["eq%d" % h, "i4k"], ["u2p"], ["p5"])
+        act(T.u2[:], T.p5[:, 0:256], ["u2p"], ["u2"], ["p5"], bias=-4096.0)
+        if t:
+            for m, (o, n) in enumerate([(1920, 256)] + SEG):
+                mm(T.p0[:, 512 - n:512], T.b4[:], T.ev[:, o:o + n], m == 0, m == 15, ["b4", "ev", "evv"], ["cv_"], ["p0"])
+            act(T.vf[:], T.p0[:, 256:512], ["cv_"], ["vf"], ["p0"], func=F.Sign)
+
+        def list_v():
+            mm(T.p2[:, 256:272], T.idh[:], T.vlh[:], True, False, ["idh", "vlh"], ["cvl"], ["p2"])
+            to_list(T.p2[:, 256:272], T.wf, "wf", T.vf, "vf", 16, "cvl", "p2", False, True)
+
+        if not last:
+            for k in range(GO):
+                gcopy(T.q16[:, 16 + k::32], T.qo[:], 128, ["qo"], ["q16h"])
             send(t + 1, "q", T.qo[:], "qo", T["qr%d" % (t + 1)][:], "qr%d" % (t + 1))
-            repeat_q(range(16 - GK, 16), QN, qnk)
-            for k in range(16 - GK):
-                act(T.q16[:, k::16], T.y2[:], ["y2"], ["q16"], bias=-MAG)
-        else:
-            dma("y", "out", 64, [qnk], ["yq"], T.yq[:], QN[:])
-        for m, (o, n) in enumerate(SEG):
-            ts(T.em[:, o:o + n], T.ar[:, 256 - n:256], T.al[:, m:m + 1], A.is_equal, ["ar", "al"], ["em%d" % m])
-            mm(T.p5[:, 256 - n:256], T.b4[:], T.em[:, o:o + n], False, False, ["b4", "em%d" % m], ["ca_"], ["p5"])
-        ts(T.ed[:], T.p3[:, 0:256], 0.0, A.is_equal, ["da"], ["ed"], ["p3"])
-        mm(T.p5[:, 0:256], T.b4[:], T.ed[:], False, True, ["b4", "ed"], ["ca_"], ["p5"])
-        tt(T.tk[:], T.p6[:, 0:256], T.oh[:], A.mult, ["ad", "oh"], ["ut"], ["p6"])
-        jobs = [("ca_", "p5", T.dgt, "dgt", T.al, "al", T.ap16, "ap16", (T.dm, T.ds, T.lx))]
-        if t:
-            jobs = [("cv_", "p2", T.dgu, "dgu", T.vl, "vl", T.vp16, "vp16", (T.w1, T.sc1, T.d1))] + jobs
-        places(jobs)
+            for k in range(GO, 16):
+                act(T.q16[:, 16 + k::32], T.y2[:, 128:256], ["y21"], ["q16s"], bias=-MAG)
+        act(QN[:, 1::2], T.y2[:, 128:256], ["y21"], [qnk[1]], bias=-MAG)
+        if last:
+            dma("y", "out", 64, qnk, ["yq"], T.yq[:], QN[:])
+        tt(T.dm[:], T.p1[:, 0:256], T.dgt[:], A.min, ["ca_", "dgt"], ["dm"], ["p1"])
+        scan(T.ds[:], T.zr[:], T.dm[:], A.mult, A.add, ["zr", "dm"], ["ds"])
+        cp(T.ap16[:], T.ds[:, 15::16], ["ds"], ["ap16"])
         if not last:
-            cp(T.nxr[:].indirect(T.ap16[:]), T.nx2[:], ["nx2", "ap16"], ["nxr"])
-            dma("y", "nd%d" % t, 16, ["nxr"], ["npf"], T.npf[:], T.nxr[0:128:16, 0:2048])
+            cp(T.nxb[:].indirect(T.ap16[:]), T.nx2[:], ["nx2", "ap16"], ["nxb"])
+            to_list(T.p7[:, 128:256], T.w2, "w2", T.nxb, "nxb", 128, "nxt", "p7")
+        if t:
+            list_v()
         cp(T.xt[:].indirect(T.ap16[:]), T.xn[:], ["xn", "ap16"], ["xt"])
-        if last:
-            dma("y", "out", 64, ["xt"], ["yx"], T.yx[:], T.xt[:, 0:2048])
-        tt(T.vl[:], T.we[:], wrt[:], A.add, ["we", wk], ["vl"])
-        if last:
-            cp(T.vl16[:], T.vl[:], ["vl"], ["vl16"])
-        tt(T.uw[:].indirect(T.vp16[:]), T.tk[:], T.dd[:], A.add, ["ut", "dd", "vp16"], ["uw"])
-        if last:
-            dma("y", "out", 64, ["uw"], ["yu"], T.yu[:], T.uw[:, 0:512])
-        else:
-            cp(T.vl16[:], T.vl[:], ["vl"], ["vl16"])
-        Q, QN, qk, qnk = QN, Q, qnk, qk
+        if not last:
+            cp(T.nxl[:], T.p7[:, 128:256], ["nxt"], ["nxl"], ["p7"])
+        Q, QN, qk, qnk = QN, Q, qnk, ["qae", "qao"] if t == 0 else qk
+        if t == 0:
+            for k in qnk:
+                wr[k], rd[k] = wr["qa"], dict(rd["qa"])
+    dma("y", "out", 64, ["xt"], ["yx"], T.yx[:], X0)
+    new_places(ROUNDS - 1)
+    dma("y", "out", 64, ["uw"], ["yu"], T.yu[:], T.uw[:, 0:512])
     act(T.vr[:], T.idw[:].indirect(T.vl16[:]), ["idw", "vl16"], ["vr"])
-    dma("y", "out", 64, ["vr"], ["yv"], T.yv[:], T.vr[0:128:16, :])
+    dma("s", "out", 64, ["vr"], ["yv"], T.yv[:], T.vr[0:128:16, :])
     for s in SEMAPHORES:
         if total.get(s, 0) > known["p"].get(s, 0):
             g.wait_ge(T.sem[s], total[s])

@@ -10,16 +10,16 @@ for _d, _names in (
                       ("eq", 256), ("fl", 16), ("xc", 512), ("f3", 48), ("em", 1920), ("ed", 256), ("yv1", 2176),
                       ("ev", 2176), ("vf", 256), ("gg", 512), ("nx2", 256), ("xga", 256), ("xn", 256),
                       ("hl", 512), ("ch", 144), ("cg", 128), ("cf", 256), ("dg", 256), ("zr", 256), ("tri", 256),
-                      ("wf", 144), ("w2", 144), ("b8f", 8), ("b8g", 8), ("bs", 16), ("b4", 128),
+                      ("wf", 144), ("w2", 144), ("b8f", 8), ("b8g", 8), ("bs", 16), ("bx", 16), ("off", 256), ("b4", 128),
                       ("base", 256), ("idb", 128), ("idn", 128), ("i4k", 128), ("i4n", 128), ("ones", 128))),
-        ("float16", (("nph", 128), ("npt", 128), ("sw", 512), ("idh", 128), ("ihn", 128), ("b8h", 8), ("b8n", 8),
-                     ("pd", 256), ("ex", 256), ("w1", 256), ("wb", 256), ("sc1", 256), ("sc2", 256), ("ar", 256),
-                     ("az", 256), ("ax", 256), ("vrh", 256), ("vlh", 16), ("dm", 256), ("ds", 256))),
-        ("float32", (("uw", 768), ("idw", 2048), ("dd", 256), ("vl", 16), ("vn", 16), ("vr", 256), ("lx", 16), ("lc", 16),
-                     ("ka", 256), ("key", 256), ("s1", 256), ("s2", 256), ("a3", 48), ("u1", 256), ("u2", 256),
+        ("float16", (("nph", 128), ("npt", 128), ("sw", 512), ("idh", 128), ("ihn", 128), ("wh", 144), ("a0h", 16),
+                     ("pd", 256), ("w1", 256), ("wb", 256), ("sc1", 256), ("sc2", 256), ("ar", 256),
+                     ("az", 256), ("ax", 256), ("vrh", 256), ("vlh", 16), ("rph", 128))),
+        ("float32", (("uw", 768), ("idw", 2048), ("dd", 256), ("vl", 16), ("vn", 16), ("vr", 256), ("dgu", 256), ("lc", 16),
+                     ("ka", 256), ("key", 256), ("s1", 256), ("a3", 48), ("u1", 256), ("u2", 256),
                      ("ws", 16), ("we", 16), ("wr0", 16), ("wr1", 16), ("wr2", 16), ("h1", 256), ("yy", 256), ("y2", 256),
                      ("nj", 32), ("nk", 16), ("cols", 32), ("dgt", 256), ("rst", 256), ("idf", 128),
-                     ("sa", 4), ("ra", 4))),
+                     ("ds", 256), ("sa", 8))),
         ("int32", (("ui", 512), ("pvr", 2048), ("npi", 128), ("rpi", 128), ("ci", 16))),
         ("uint16", (("nxl", 128), ("d16", 256), ("vl16", 16), ("vp16", 16), ("ap16", 16), ("a016", 16), ("bl", 32),
                     ("al16", 16), ("nl16", 16), ("exl", 8)))):
@@ -29,23 +29,46 @@ for _k in range(8):
     SCRATCH["p%d" % _k] = ("psum", [128, 512], "float32")
 
 ROUNDS = 3
-LS = 64
-XV0, XV = 896, 768
+LS = 128
+XV0, XV = 1024, 768
 SEMAPHORES = ["cv", "cs", "ct", "cp", "ldx", "ldq", "ldu", "ldn", "ldr", "ldp", "ldb", "ldc", "out"]
 for _t in range(ROUNDS):
     SEMAPHORES += ["%s%d" % (_a, _t) for _a in ("rq", "ra", "rw", "lq", "la", "lw")]
-G0, S0 = 1, 8
-GE, GO = 9, 9
+PARTS = 4
+EARLY = 4
+LAND = ("ab", "ca", "cb")
+SEMAPHORES += ["%s%d" % (_a, _c) for _a in ("fa", "fb", "fl") for _c in range(PARTS)]
+G0, S0 = 1, 5
+GE, GO = 7, 9
 CA = 2
-MV = 7
-FAR = 262144.0
+MV = 5
+FAR = 524288.0
 BIG = 1048576.0
 MAG = 12582912.0
+
+
+def neighbour(core, T, topo):
+    return [c for c in topo.cores_of(core) if T.rank_of(c) is None and topo.die(c) == topo.die(core)][0]
+
+
+def hand_back(g, core, home, T, topo):
+    rid, pid = topo.addr(home, core)
+    n, back = len(topo.engines(home, core)), len(topo.engines(core, home))
+    for t in range(ROUNDS):
+        for c in range(PARTS):
+            J = slice(4096 // PARTS * c, 4096 // PARTS * (c + 1))
+            g.wait_ge(T.sem["fa%d" % c], n * (t + 1))
+            g.remote_dma(T.ab[:, J], T[LAND[t]][:, J], T.sem["fb%d" % c], T.sem["fl%d" % c], pid, rid, topo.mask(core, home))
+    for c in range(PARTS):
+        g.wait_ge(T.sem["fl%d" % c], back * ROUNDS)
 
 
 def rank_program(g, core, T, topo):
     rank = T.rank_of(core)
     if rank is None:
+        for home in T.cores:
+            if core in topo.cores_of(home) and neighbour(home, T, topo) == core:
+                hand_back(g, core, home, T, topo)
         return
     N = len(T.cores)
     V, S, P = g.vector, g.scalar, g.tensor
@@ -131,6 +154,20 @@ def rank_program(g, core, T, topo):
         total[rs] = len(topo.engines(sender, core)[:8])
         wr[land] = (rs, total[rs])
 
+    def fold(t, c):
+        d = neighbour(core, T, topo)
+        J = slice(4096 // PARTS * c, 4096 // PARTS * (c + 1))
+        R = ["xg%d" % c] + Q16
+        need("p", deps_of(R, ["ab%d" % c], [], None))
+        rid, pid = topo.addr(d, core)
+        g.remote_dma_fused([RemoteDMATransfer(dst_ids=[DstId(rid=rid, pnc=pid)], dma_engine_mask=topo.mask(core, d),
+                                              remote_sem=T.sem["fa%d" % c], srcs=[T.xg[:, J], T.q16[:, J]],
+                                              dsts=[T[LAND[t]][:, J]], alu_op=2)], local_sem=T.sem["fl%d" % c])
+        total["fl%d" % c] = len(topo.engines(core, d)) * (t + 1)
+        total["fb%d" % c] = len(topo.engines(d, core)) * (t + 1)
+        note("fl%d" % c, total["fl%d" % c], R, [], [])
+        note("fb%d" % c, total["fb%d" % c], [], ["ab%d" % c], [])
+
     def act(out, in_, R, W, X=(), func=F.Identity, **kw):
         op("s", R, W, X, lambda: S.activation(out, in_, func, **kw))
 
@@ -209,8 +246,8 @@ def rank_program(g, core, T, topo):
         ts(w[:], C, 0.0, A.is_equal, ["ch"], [k], (), x, A.mult)
     ts(T.wf[:], T.ch[:], col(7), A.is_equal, ["ch", "c7"], ["wf"], (), FAR, A.mult)
     ts(T.w2[:], T.ch[:], col(7), A.is_equal, ["ch", "c7", "c9"], ["w2"], (), col(9), A.mult)
-    for w, k, x in ((T.b8f[:], "b8f", FAR), (T.b8h[:], "b8h", 1.0), (T.b8n[:], "b8n", -1.0)):
-        ts(w, T.cg[:, 0:128:16], col(1), A.is_equal, ["cg", "c1"], [k], (), x, A.mult)
+    ts(T.wh[:], T.ch[:], col(7), A.is_equal, ["ch", "c7"], ["wh"])
+    ts(T.b8f[:], T.cg[:, 0:128:16], col(1), A.is_equal, ["cg", "c1"], ["b8f"], (), FAR, A.mult)
     ts(T.b4[:], T.cg[:], col(1), A.is_equal, ["cg", "c1"], ["b4"], (), 4096.0, A.mult)
     ts(T.dg[:], T.cf[:], col(0), A.is_equal, ["cf", "c0"], ["dg"])
     cp(T.exl[:], T.ci[:, 8:16], ["ci1"], ["exl"])
@@ -220,22 +257,22 @@ def rank_program(g, core, T, topo):
     act(T.ones[:], T.cg[:], ["cg"], ["ones"], scale=0.0, bias=1.0)
     for w, k, x in ((T.idn, "idn", -1.0), (T.i4k, "i4k", 4096.0), (T.i4n, "i4n", -4096.0), (T.idf, "idf", 1.0)):
         act(w[:], T.idb[:], ["idb"], [k], scale=x)
-    for w, k, x in ((T.b8g[:], "b8g", 0.5), (T.bs[:, 0:8], "bs", 16.0 / FAR), (T.bs[:, 8:16], "bs", -16.0 / FAR)):
+    for w, k, x in ((T.b8g[:], "b8g", 0.5), (T.bs[:, 0:8], "bs", 32.0 / FAR), (T.bs[:, 8:16], "bs", -32.0 / FAR),
+                    (T.bx[:, 0:8], "bx", -16.0 / FAR), (T.bx[:, 8:16], "bx", 16.0 / FAR)):
         act(w, T.b8f[:], ["b8f"], [k], scale=x)
-    act(T.base[:, 0:128], T.cg[:], ["cg"], ["base"], scale=0.0, bias=-8.5 * FAR)
-    for p in range(0, 128, 32):
-        act(T.base[p:p + 32, 128:256], T.cg[p:p + 32, :], ["cg"], ["base"], scale=0.0, bias=(-8.5 if p < 128 - LS else -0.5) * FAR)
+    act(T.base[:, 128:256], T.cg[:], ["cg"], ["base"], scale=0.0, bias=-8.5 * FAR)
+    for p0, p1, x in ((0, LS, -0.5), (LS, 128, -8.5)):
+        if p0 < p1:
+            act(T.base[p0:p1, 0:128], T.cg[p0:p1, :], ["cg"], ["base"], scale=0.0, bias=x * FAR)
     act(T.qo[:], T.qa[:, 1::2], ["qa"], ["qo"])
     iota(T.nj[:], [[512, 2], [16, 16]], 0, 0, ["nj"])
-    iota(T.dgt[:], [[2, 256]], 2048, 0, ["dgt"])
+    iota(T.dgt[:], [[0, 256]], -1, 0, ["dgt"])
     for k in range(G0):
         gcopy(T.q16[:, k::16], T.qa[:], 256, ["qa"], ["q16g"])
     send(0, "q", T.qo[:], "qo", T.qr0[:], "qr0")
     for k in range(G0, G0 + S0):
         act(T.q16[:, k::16], T.qa[:], ["qa"], ["q16s"])
     iota(T.idw[:], [[1, 2048]], 0, 0, ["idw"])
-    iota(T.rcb[:], [[0, 2048]], 0, 0, ["rcb"])
-    iota(T.nxb[:, 0:2048], [[0, 2048]], 0, 0, ["nxb"])
     cp(T.nph[:], T.npi[:], ["npi"], ["nph"])
     vtr(T.npt[:], T.nph[:], ["nph"], ["npt"])
     for e in (0, 1):
@@ -247,23 +284,35 @@ def rank_program(g, core, T, topo):
         cp(T.q16[:, k::16], T.qa[:], ["qa"], ["q16v"])
     cp(T.nxl[:], T.p7[:, 128:256], ["nxt"], ["nxl"], ["p7"])
 
-    def two_parts(o, src, sk, tab, tk, sem):
+    TWO = ((0, T.nph, "nph", T.nxb, "nxb", "ldb"), (256, T.rph, "rph", T.rcb, "rcb", "ldc"))
+    cp(T.rph[:], T.rpi[:], ["rpi"], ["rph"])
+    for o, src, sk, tab, tk, sem in TWO:
         cp(T.hl[:, o:o + 128], src[:], [sk], ["hi" + sk])
-        tt(T.hl[:, o + 128:o + 256], src[:], T.hl[:, o:o + 128], A.subtract, [sk, "hi" + sk], ["lo" + sk])
-        for j, k in enumerate(("hi" + sk, "lo" + sk)):
-            dma("y", sem, 32, [k], [tk], tab[j:128:16, 0:2048], T.hl[:, o + 128 * j:o + 128 * j + 128])
+        mm(T.p6[:, o:o + 128], T.idh[:], src[:], True, False, ["idh", sk], ["lp" + sk], ["p6"])
+        mm(T.p6[:, o:o + 128], T.idn[:], T.hl[:, o:o + 128], False, True, ["idn", "hi" + sk], ["lp" + sk], ["p6"])
 
-    two_parts(256, T.rpi, "rpi", T.rcb, "rcb", "ldc")
-    two_parts(0, T.nph, "nph", T.nxb, "nxb", "ldb")
+    def tables_of_two_parts():
+        for o, src, sk, tab, tk, sem in TWO:
+            act(T.hl[:, o + 128:o + 256], T.p6[:, o:o + 128], ["lp" + sk], ["lo" + sk], ["p6"])
+        for o, src, sk, tab, tk, sem in TWO:
+            iota(tab[:, 0:2048], [[0, 2048]], 0, 0, [tk])
+            for j, k in enumerate(("hi" + sk, "lo" + sk)):
+                dma("y", sem, 32, [k], [tk], tab[j:128:16, 0:2048], T.hl[:, o + 128 * j:o + 128 * j + 128])
+
     ts(T.vl[:], T.nj[:, 0:16], 2.0, A.mult, ["nj", "c6"], ["vl"], (), col(6), A.add)
     ts(T.lc[:], T.nj[:, 16:32], col(0), A.add, ["nj", "c0"], ["lc"])
     cp(T.vp16[:], T.vl[:], ["vl"], ["vp16"])
     ts(T.az[:], T.cf[:], 0.0, A.mult, ["cf"], ["az"])
-    tt(T.dgt[:], T.dgt[:], T.dg[:], A.mult, ["dgt", "dg"], ["dgt"])
+    ts(T.f3[:, 0::3], T.cf[:, 0:16], 0.0, A.mult, ["cf"], ["f3"])
+    ts(T.dgt[:, 0::16], T.lc[:], 1536.0, A.add, ["lc", "dgt"], ["dgt"])
     act(T.zr[:], T.cf[:], ["cf"], ["zr"], func=F.Sign)
     act(T.rst[:], T.zr[:], ["zr"], ["rst"], scale=-2.0 * BIG, bias=BIG)
-    act(T.vf[:], T.cf[:], ["cf", "c8"], ["vf"], scale=-1.0, bias=col(8), func=F.Sign)
-    act(T.tri[:], T.vf[:], ["vf"], ["tri"], scale=4096.0, func=F.Relu)
+
+    def constants_for_the_writes():
+        act(T.dgu[:], T.dgt[:], ["dgt"], ["dgu"], bias=-1536.0)
+        act(T.off[:], T.dg[:], ["dg"], ["off"], scale=-BIG, bias=BIG)
+        act(T.vf[:], T.cf[:], ["cf", "c8"], ["vf"], scale=-1.0, bias=col(8), func=F.Sign)
+        act(T.tri[:], T.vf[:], ["vf"], ["tri"], scale=4096.0, func=F.Relu)
 
     SEG = [(0, 0)] * 15
     _o = 0
@@ -271,15 +320,12 @@ def rank_program(g, core, T, topo):
         SEG[m] = (_o, 240 - 16 * m)
         _o += 240 - 16 * m
 
-    def new_places(t, first=True, second=True):
-        if first:
-            if t:
-                tt(T.lx[:], T.p2[:, 256:272], T.lc[:], A.min, ["cvl", "lc"], ["lx"], ["p2"])
-                cp(T.vp16[:], T.lx[:], ["lx"], ["vp16"])
-            tt(T.uw[:].indirect(T.vp16[:]), T.u1[:], T.u2[:], A.max, ["u1", "u2", "vp16"], ["uw"])
-        if second:
-            tt(T.vl[:], T.we[:], T["wr%d" % t][:], A.add, ["we", "wr%d" % t], ["vl"])
-            cp(T.vl16[:], T.vl[:], ["vl"], ["vl16"])
+    def new_places():
+        tt(T.uw[:].indirect(T.vp16[:]), T.u1[:], T.u2[:], A.max, ["u1", "u2", "vp16"], ["uw"])
+
+    def new_recipients(t):
+        tt(T.vl[:], T.we[:], T["wr%d" % t][:], A.add, ["we", "wr%d" % t], ["vl"])
+        cp(T.vl16[:], T.vl[:], ["vl"], ["vl16"])
 
     Q, QN, qk, qnk = T.qa, T.qb, ["qa"], ["qbe", "qbo"]
     LV = 256 - LS
@@ -301,18 +347,22 @@ def rank_program(g, core, T, topo):
             mm(T[pk][:], T.idb[:], src[:, j:j + 512], True, False, ["idb", sk], [pk + "d"], [pk])
             mm(T[pk][:], T.idn[:], T.q16[:, 16 * lane0 + j:16 * lane0 + j + 512], False, True, ["idn"] + Q16, [pk + "d"], [pk])
 
-        def absc(c):
+        def sign(c):
             pk = ("p2", "p3")[c % 2]
-            act(T.ab[:, 512 * c:512 * c + 512], T[pk][:], [pk + "d"], ["ab%d" % (c // 4)], [pk], func=F.Abs)
+            act(T.sg4[:, 512 * c:512 * c + 512], T[pk][:], [pk + "d"], ["sg4"], [pk], func=F.Sign, scale=-1.0, bias=-0.5)
 
-        def marks(l0, l1, k):
-            act(T.xg[:, 16 * l0:16 * l1], X0.indirect(T.d16[:, l0:l1]), ["xt", "d16"], [k])
+        def marks(c):
+            l0, l1 = 256 // PARTS * c, 256 // PARTS * (c + 1)
+            act(T.xg[:, 16 * l0:16 * l1], X0.indirect(T.d16[:, l0:l1]), ["xt", "d16"], ["xg%d" % c])
+            fold(t, c)
 
-        def scores(h):
-            pk = ("p4", "p5")[h]
-            mm(T[pk][:, 0:256], T.idb[:], T.cf[:], True, False, ["idb", "cf"], ["sc%d" % h], [pk])
-            by_lane(T[pk], 0, T.ab, 0, 128 * h, 128 * h + 128, T.bs, "bs", ["ab%d" % h], "sc%d" % h, pk, False)
-            mm(T[pk][:, 256:384], T.dd[:, 128 * h:128 * h + 128], T.idf[:], False, True, ["dd", "idf"], ["sc%d" % h], [pk])
+        def scores(h, folded):
+            pk, parts = ("p4", "p5")[h], range(PARTS // 2 * h, PARTS // 2 * (h + 1))
+            if folded:
+                by_lane(T[pk], 0, T.ab, 0, 128 * h, 128 * h + 128, T.bs, "bs", ["ab%d" % c for c in parts], "sc%d" % h, pk, False, True)
+            else:
+                mm(T[pk][:, 0:256], T.idb[:], T.cf[:], True, False, ["idb", "cf"], ["sc%d" % h], [pk])
+                by_lane(T[pk], 0, T.xg, 0, 128 * h, 128 * h + 128, T.bx, "bx", ["xg%d" % c for c in parts], "sc%d" % h, pk, False)
 
         def lower(h):
             pk = ("p4", "p5")[h]
@@ -324,7 +374,8 @@ def rank_program(g, core, T, topo):
         act(T.x1[:, xv:2048], X0.indirect(T.nxl[:, xv // 16:128]), ["xt", "nxl"], ["x1b"])
         cp(T.x1[:, 0:xv], X0.indirect(T.nxl[:, 0:xv // 16]), ["xt", "nxl"], ["x1a"])
         if t:
-            new_places(t - 1)
+            new_places()
+            new_recipients(t - 1)
             cp(T.d16[:], T.uw[:, 0:512].indirect(T.vl16[:]), ["uw", "vl16"], ["d16"])
             cp(T.vlh[:], T.vl[:], ["vl"], ["vlh"])
         else:
@@ -332,47 +383,48 @@ def rank_program(g, core, T, topo):
             cp(T.dd[:], T.ui[:, 0:512:2], ["ui"], ["dd"])
         act(T.x2[:], T.x1[:].indirect(T.nxl[:]), ["x1a", "x1b", "nxl"], ["x2"])
         walk(T.x1, ["x1a", "x1b"], T.ca, "ca", 0, 128)
-        marks(0, 64, "xga0")
-        marks(64, 128, "xgb0")
+        for c in range(EARLY):
+            marks(c)
         wsum(T.p0, 0, T.ca, "ca", 0, "p0", "k1")
-        diff(0, T.xg, "xga0", 0)
-        diff(1, T.xg, "xga0", 0)
         walk(T.x1, ["x1a", "x1b"], T.ca, "ca", 128, 256)
-        absc(0)
-        absc(1)
         wsum(T.p0, 0, T.ca, "ca", 1, "p0", "k1")
-        diff(2, T.xg, "xgb0", 0)
-        diff(3, T.xg, "xgb0", 0)
         act(T.x3[:], T.x2[:].indirect(T.nxl[:]), ["x2", "nxl"], ["x3"])
-        absc(2)
-        absc(3)
+        for c in range(EARLY, PARTS):
+            marks(c)
         if t:
             act(T.dd[:], T.uw[:, 0:512].indirect(T.vl16[:]), ["uw", "vl16"], ["dd"])
+        else:
+            tables_of_two_parts()
         over(0, T.p0, 0, ["k10", "k11"], "p0")
-        marks(128, 192, "xga1")
         walk(T.x2, ["x2"], T.cb, "cb", 0, 128)
         wsum(T.p1, 0, T.cb, "cb", 0, "p1", "k2")
-        scores(0)
         act(T.x4[:], T.x3[:].indirect(T.nxl[:]), ["x3", "nxl"], ["x4"])
         walk(T.x2, ["x2"], T.cb, "cb", 128, 256)
         wsum(T.p1, 0, T.cb, "cb", 1, "p1", "k2")
-        diff(4, T.xg, "xga1", 0)
-        diff(5, T.xg, "xga1", 0)
-        absc(4)
-        absc(5)
-        marks(192, 256, "xgb1")
+        scores(0, False)
+        scores(1, False)
         walk(T.x3, ["x3"], T.ca, "ca", 0, 128)
         wsum(T.p0, 256, T.ca, "ca", 0, "p0", "k3")
         over(1, T.p1, 0, ["k20", "k21"], "p1")
-        lower(0)
-        act(T.xg4[:, 0:16 * LS], T.x4[:].indirect(T.d16[:, LV:256]), ["x4", "d16"], ["xg4"])
+        share = [(l, min(l + 64, LS)) for l in range(0, LS, 64)]
+        for l0, l1 in share:
+            act(T.xg4[:, 16 * l0:16 * l1], T.x4[:].indirect(T.d16[:, l0:l1]), ["x4", "d16"], ["xg4%d" % (l0 // 64)])
+        diff(0, T.xg4, "xg40", 0)
+        diff(1, T.xg4, "xg40", 0)
+        scores(0, True)
         walk(T.x3, ["x3"], T.ca, "ca", 128, 256)
         wsum(T.p0, 256, T.ca, "ca", 1, "p0", "k3")
-        diff(6, T.xg, "xgb1", 0)
-        diff(7, T.xg, "xgb1", 0)
-        absc(6)
-        absc(7)
-        walk(T.x4, ["x4"], T.cb, "cb", 0, 128)
+        sign(0)
+        sign(1)
+        for c in range(2, LS // 32):
+            diff(c, T.xg4, "xg41", 0)
+        lower(0)
+        over(2, T.p0, 256, ["k30", "k31"], "p0")
+        for c in range(2, LS // 32):
+            sign(c)
+        if LS < 128:
+            walk(T.x4, ["x4"], T.cb, "cb", LS, 128)
+        walk(T.x4, ["x4"], T.cb, "cb", 128, 256)
 
         FOURTH = ((T.p1, 256, "p1"), (T.p6, 0, "p6"))
 
@@ -380,47 +432,54 @@ def rank_program(g, core, T, topo):
             pp, o, pk = FOURTH[h]
             mm(pp[:, o:o + 128], T.idb[:], src, st, sp, ["idb", sk], ["k4%d" % h], [pk])
 
-        mm(T.p7[:, 16:64:3], T.idn[:], T.base[:, 0:16], True, True, ["idn", "base"], ["b0"], ["p7"])
         for h in (0, 1):
             on_top(h, T.base[:, 128 * h:128 * h + 128], "base", True, False)
             for j in range(2):
                 on_top(h, T.rr[:, 256 * j + 128 * h:256 * j + 128 * h + 128], "rr%d" % j, False, False)
-        over(2, T.p0, 256, ["k30", "k31"], "p0")
-        for c in range(LS // 32):
-            diff(c, T.xg4, "xg4", LV)
-        on_top(0, T.rr[:, 512:640], "rr2", False, False)
-        by_lane(T.p1, 256, T.cb, 0, 0, 128, T.b8f, "b8f", ["cb0"], "k40", "p1", False, True)
-        scores(1)
-        for c in range(LS // 32):
-            pk = ("p2", "p3")[c % 2]
-            act(T.sg4[:, 512 * c:512 * c + 512], T[pk][:], [pk + "d"], ["sg4"], [pk], func=F.Sign, scale=-1.0, bias=-0.5)
+        scores(1, True)
         lower(1)
-        walk(T.x4, ["x4"], T.cb, "cb", 128, LV)
-        by_lane(T.p6, 0, T.cb, 0, 128, LV, T.b8f, "b8f", ["cb128"], "k41", "p6", False)
-        by_lane(T.p6, 0, T.sg4, LV, LV, 256, T.b8g, "b8g", ["sg4"], "k41", "p6", False)
-        on_top(1, T.rr[:, 640:768], "rr2", False, True)
+        if t == 0:
+            constants_for_the_writes()
+        on_top(1, T.rr[:, 640:768], "rr2", False, False)
+        if LS < 128:
+            by_lane(T.p1, 256, T.cb, 0, LS, 128, T.b8f, "b8f", ["cb%d" % LS], "k40", "p1", False)
+        by_lane(T.p1, 256, T.sg4, 0, 0, LS, T.b8g, "b8g", ["sg4"], "k40", "p1", False)
+        on_top(0, T.rr[:, 512:640], "rr2", False, True)
+        by_lane(T.p6, 0, T.cb, 0, 128, 256, T.b8f, "b8f", ["cb128"], "k41", "p6", False, True)
+        def equal_v(ms):
+            for m in ms:
+                o, n = SEG[m]
+                ts(T.ev[:, o:o + n], T.vrh[:, 256 - n:256], T.vl[:, m:m + 1], A.is_equal, ["vrh", "vl"], ["evv"])
+
         if t:
+            cp(T.vrh[:], T.idw[:].indirect(T.vl16[:]), ["idw", "vl16"], ["vrh"])
             act(T.vr[:], T.idw[:].indirect(T.vl16[:]), ["idw", "vl16"], ["vr"])
             act(T.vn[:], T.vl[:], ["vl"], ["vn"], scale=-1.0)
             for m in range(MV, 15):
                 o, n = SEG[m]
                 act(T.yv1[:, o:o + n], T.vr[:, 256 - n:256], ["vr", "vn"], ["yv1"], func=F.Abs, bias=T.vn[:, m:m + 1])
+            mm(T.p2[:, 0:256], T.idb[:], T.tri[:], True, False, ["idb", "tri"], ["dv"], ["p2"])
+            for j in range(16):
+                mm(T.p2[:, j:256:16], T.ihn[:], T.vlh[:], False, False, ["ihn", "vlh"], ["dv"], ["p2"])
+            mm(T.p2[:, 0:256], T.idh[:], T.vrh[:], False, True, ["idh", "vrh"], ["dv"], ["p2"])
+            o = SEG[MV][0]
+            act(T.yv1[:, 1920:2176], T.p2[:, 0:256], ["dv"], ["yv1"], ["p2"], func=F.Abs)
+            act(T.ev[:, o:2176], T.yv1[:, o:2176], ["yv1"], ["ev"], func=F.Relu, scale=-1.0, bias=1.0)
         for h, (pp, pk, o) in enumerate(((T.p1, "p1", 256), (T.p6, "p6", 0))):
             H, k, ps = slice(128 * h, 128 * h + 128), str(h), ("p4", "p5")[h]
             tt(T.key[:, H], pp[:, o:o + 128], T.ka[:, H], A.max, ["ka" + k, "k4" + k], ["key" + k], [pk])
             tt(T.key[:, H], T[ps][:, 128:256], T.key[:, H], A.min, ["key" + k, "sc" + k], ["key" + k], [ps])
             scan(T.s1[:, H], T.rst[:, H], T.key[:, H], A.max, A.min, ["rst", "key" + k], ["s1" + k])
             tt(T.eq[:, H], T.s1[:, H].indirect(T.exl[:]), T.key[:, H], A.is_equal, ["s1" + k, "exl", "key" + k], ["eq" + k])
-            tt(T.pd[:, H], T[ps][:, 256:384], T.eq[:, H], A.mult, ["sc" + k, "eq" + k], ["pd" + k], [ps])
-            scan(T.s2[:, H], T.zr[:, H], T.pd[:, H], A.mult, A.add, ["zr", "pd" + k], ["s2" + k])
-            if h:
-                ts(T.fl[:], T.s1[:, 15::16], -65536.0, A.is_ge, ["s10", "s11"], ["fl"])
-            tt(T.ex[:, H], T.s2[:, H].indirect(T.exl[:]), T.dg[:, 0:128], A.mult, ["s2" + k, "exl", "dg"], ["ex" + k])
-            if h:
-                mm(T.p4[:, 400:416], T.ones[:], T.fl[:], True, True, ["ones", "fl"], ["nn"], ["p4"])
-            mm(T.p7[:, 8 * h:8 * h + 8], T.ex[:, H], T.b8h[:], True, True, ["ex" + k, "b8h"], ["a0" + k], ["p7"])
-        cp(T.a016[:], T.p7[:, 0:16], ["a00", "a01"], ["a016"], ["p7"])
-        sa, ra = T.sa[:, t:t + 1], T.ra[:, t:t + 1]
+            mm(T.p3[:, H], T.eq[:, H], T.idb[:], True, True, ["eq" + k, "idb"], ["oh"], ["p3"])
+        ts(T.fl[:], T.s1[:, 15::16], -0.25 * FAR, A.is_ge, ["s10", "s11"], ["fl"])
+        mm(T.p4[:, 400:416], T.ones[:], T.fl[:], True, True, ["ones", "fl"], ["nn"], ["p4"])
+        tt(T.pd[:], T.p3[:, 0:256], T.dd[:], A.mult, ["oh", "dd"], ["pd"], ["p3"])
+        to_list(T.p7[:, 0:16], T.wh, "wh", T.pd, "pd", 16, "a0", "p7")
+        if t:
+            equal_v(range(MV))
+        cp(T.a016[:], T.p7[:, 0:16], ["a0"], ["a016"], ["p7"])
+        sa, ra = T.sa[:, t:t + 1], T.sa[:, 4 + t:5 + t]
         act(T.nk[:], T.p4[:, 400:416], ["nn"], ["nk", "n"], ["p4"], accum_out=col(16))
         act(col(17), col(16), ["n"], ["n1"], scale=1.0 / 256, bias=-0.498046875)
         act(col(20), col(16), ["n"], ["n4"], scale=0.5, bias=-0.25)
@@ -429,57 +488,49 @@ def rank_program(g, core, T, topo):
         act(sa, col(19), ["n3", "n4"], ["sa%d" % t], scale=-128.0, bias=col(20))
         send(t, "a", sa, "sa%d" % t, ra, "ra%d" % t)
         act(T.yy[:, 0:128], Q[:, 0::2], qk + ["sa%d" % t], ["yy0"], scale=0.5, bias=sa)
-        act(T.y2[:, 0:128], T.yy[:, 0:128], ["yy0"], ["y20"], bias=MAG)
-        act(QN[:, 0::2], T.y2[:, 0:128], ["y20"], [qnk[0]], bias=-MAG)
-        if not last:
-            for k in range(GE):
-                gcopy(T.q16[:, k::32], QN[:, 0::2], 128, [qnk[0]], ["q16g"])
-        for h in (0, 1):
-            mm(T.p6[:, 128 + 24 * h + 2:128 + 24 * h + 24:3], T.ex[:, 128 * h:128 * h + 128], T.b8h[:], True, True,
-               ["ex%d" % h, "b8h"], ["d3"], ["p6"])
         if t:
-            mm(T.p2[:, 0:256], T.idf[:], T.vr[:], True, False, ["idf", "vr"], ["dv"], ["p2"])
-            for j in range(16):
-                mm(T.p2[:, j:256:16], T.ihn[:], T.vlh[:], False, False, ["ihn", "vlh"], ["dv"], ["p2"])
-            mm(T.p2[:, 0:256], T.idb[:], T.tri[:], False, True, ["idb", "tri"], ["dv"], ["p2"])
-        if not last:
-            for k in range(GE, 16):
-                act(T.q16[:, k::32], T.y2[:, 0:128], ["y20"], ["q16s"], bias=-MAG)
-        if t:
-            o = SEG[MV][0]
-            act(T.yv1[:, 1920:2176], T.p2[:, 0:256], ["dv"], ["yv1"], ["p2"], func=F.Abs)
-            act(T.ev[:, o:2176], T.yv1[:, o:2176], ["yv1"], ["ev"], func=F.Relu, scale=-1.0, bias=1.0)
-
-        def equal_v(ms):
-            for m in ms:
-                o, n = SEG[m]
-                ts(T.ev[:, o:o + n], T.vrh[:, 256 - n:256], T.vl[:, m:m + 1], A.is_equal, ["vrh", "vl"], ["evv"])
-
+            mm(T.p0[:, 256:512], T.idb[:], T.off[:], True, False, ["idb", "off"], ["cv_"], ["p0"])
+            mm(T.p0[:, 256:512], T.idh[:], T.vrh[:], False, False, ["idh", "vrh"], ["cv_"], ["p0"])
+            for m, (o, n) in enumerate(SEG + [(1920, 256)]):
+                mm(T.p0[:, 512 - n:512], T.b4[:], T.ev[:, o:o + n], False, m == 15, ["b4", "evv" if m < MV else "ev"], ["cv_"], ["p0"])
         tt(T.w1[:], T.pvr[:].indirect(T.a016[:]), T.dg[:], A.mult, ["pvr", "a016", "dg"], ["w1"])
+        cp(T.a0h[:], T.p7[:, 0:16], ["a0"], ["a0h"], ["p7"])
         scan(T.sc1[:], T.zr[:], T.w1[:], A.mult, A.add, ["zr", "w1"], ["sc1"])
         cp(T.bl[:, 0:16], T.sc1[:, 15::16], ["sc1"], ["bl0"])
         tt(T.wb[:], T.pvr[:].indirect(T.bl[:, 0:16]), T.dg[:], A.mult, ["pvr", "bl0", "dg"], ["wb"])
-        tt(T.xc[:, 0:256], X0.indirect(T.bl[:, 0:16]), Q[:], A.is_lt, ["xt", "bl0"] + qk, ["xc0"])
-        for h in (0, 1):
-            po = T.p6[:, 128 + 24 * h + 1:128 + 24 * h + 24:3]
-            mm(po, T.ex[:, 128 * h:128 * h + 128], T.b8n[:], True, False, ["ex%d" % h, "b8n"], ["d3"], ["p6"])
-            mm(po, T.idh[:], T.sc1[:, 128 * h + 15:128 * h + 128:16], False, True, ["idh", "sc1"], ["d3"], ["p6"])
-        to_list(T.p7[:, 18:64:3], T.wf, "wf", T.xc, "xc0", 16, "b1", "p7")
+        act(T.xga[:], X0.indirect(T.bl[:, 0:16]), ["xt", "bl0"], ["xga"])
+        mm(T.p3[:, 256:512], T.idn[:], Q[:], True, False, ["idn"] + qk, ["xq"], ["p3"])
+        mm(T.p3[:, 256:512], T.idb[:], T.xga[:], False, True, ["idb", "xga"], ["xq"], ["p3"])
+        act(T.y2[:, 0:128], T.yy[:, 0:128], ["yy0"], ["y20"], bias=MAG)
+        act(QN[:, 0::2], T.y2[:, 0:128], ["y20"], [qnk[0]], bias=-MAG)
+        act(T.xc[:, 0:256], T.p3[:, 256:512], ["xq"], ["xc0"], ["p3"], func=F.Sign, scale=-1.0, bias=-0.5)
+        if not last:
+            for k in range(GE):
+                gcopy(T.q16[:, k::32], QN[:, 0::2], 128, [qnk[0]], ["q16g"])
+            for k in range(GE, 16):
+                act(T.q16[:, k::32], T.y2[:, 0:128], ["y20"], ["q16s"], bias=-MAG)
+        mm(T.p6[:, 130:176:3], T.idh[:], T.a0h[:], True, True, ["idh", "a0h"], ["d3"], ["p6"])
+        mm(T.p6[:, 129:176:3], T.ihn[:], T.a0h[:], True, False, ["ihn", "a0h"], ["d3"], ["p6"])
+        mm(T.p6[:, 129:176:3], T.idh[:], T.sc1[:, 15::16], False, True, ["idh", "sc1"], ["d3"], ["p6"])
         scan(T.sc2[:], T.zr[:], T.wb[:], A.mult, A.add, ["zr", "wb"], ["sc2"])
         cp(T.bl[:, 16:32], T.sc2[:, 15::16], ["sc2"], ["bl1"])
         tt(T.xc[:, 256:512], X0.indirect(T.bl[:, 16:32]), Q[:], A.is_lt, ["xt", "bl1"] + qk, ["xc1"])
         mm(T.p6[:, 128:176:3], T.ihn[:], T.sc1[:, 15::16], True, False, ["ihn", "sc1"], ["d3"], ["p6"])
         mm(T.p6[:, 128:176:3], T.idh[:], T.sc2[:, 15::16], False, True, ["idh", "sc2"], ["d3"], ["p6"])
         for k in range(16):
-            mm(T.p7[:, 17:64:3], T.wf[:, 15 - k:143 - k], T.xc[:, 256 + k::16], k == 0, k == 15, ["wf", "xc1"], ["b2"], ["p7"])
-        mm(T.p0[:, 0:256], T.idb[:], T.tri[:], True, False, ["idb", "tri"], ["da"], ["p0"])
+            mm(T.p7[:, 16:48], T.wf[:, 15 - k:143 - k], T.xc[:, k::16], k == 0, k == 15, ["wf", "xc0", "xc1"], ["b2"], ["p7"])
+        mm(T.p2[:, 0:256], T.idb[:], T.tri[:], True, False, ["idb", "tri"], ["da"], ["p2"])
+        mm(T.p1[:, 0:256], T.idb[:], T.off[:], True, False, ["idb", "off"], ["ca_"], ["p1"])
         mm(T.p4[:, 0:256], T.idf[:], T.dd[:], True, False, ["idf", "dd"], ["u1p"], ["p4"])
         for h in (0, 1):
             mm(T.p4[:, 128 * h:128 * h + 128], T.eq[:, 128 * h:128 * h + 128], T.i4n[:], False, h == 1, ["eq%d" % h, "i4n"], ["u1p"], ["p4"])
         if t:
-            cp(T.vrh[:], T.vr[:], ["vr"], ["vrh"])
-            equal_v(range(MV // 2))
-        ts(T.f3[:], T.p7[:, 16:64], 8.25 * FAR, A.is_lt, ["b0", "b1", "b2"], ["f3"], ["p7"])
+            scan(T.ds[:], T.dgu[:], T.p0[:, 256:512], A.max, A.min, ["cv_", "dgu"], ["ds"], ["p0"])
+            cp(T.vp16[:], T.ds[:, 15::16], ["ds"], ["vp16"])
+        else:
+            cp(T.uw[:, 0:512], T.ui[:], ["ui"], ["uw"])
+        ts(T.f3[:, 2::3], T.p7[:, 16:32], FAR, A.is_lt, ["b2"], ["f3"], ["p7"])
+        ts(T.f3[:, 1::3], T.p7[:, 32:48], 8.5 * FAR, A.is_lt, ["b2"], ["f3"], ["p7"])
         scan(T.a3[:], T.f3[:], T.p6[:, 128:176], A.mult, A.add, ["f3", "d3"], ["al"], ["p6"])
         cp(T.al16[:], T.a3[:, 2::3], ["al"], ["al16"])
         cp(T.az[:, 0::16], T.a3[:, 2::3], ["al"], ["az"])
@@ -488,10 +539,20 @@ def rank_program(g, core, T, topo):
         act(T.gg[:, 0:256], T.rcb[:].indirect(T.al16[:]), ["rcb", "al16"], ["gg"])
         if not last:
             act(T.gg[:, 256:512], T.nxb[:, 0:2048].indirect(T.al16[:]), ["nxb", "al16"], ["gg"])
+
+        def places_to_write():
+            mm(T.p5[:, 0:256], T.idh[:], T.ar[:], True, False, ["idh", "ar"], ["u2p"], ["p5"])
+            for h in (0, 1):
+                mm(T.p5[:, 128 * h:128 * h + 128], T.eq[:, 128 * h:128 * h + 128], T.i4k[:], False, h == 1, ["eq%d" % h, "i4k"], ["u2p"], ["p5"])
+            act(T.u1[:], T.p4[:, 0:256], ["u1p"], ["u1"], ["p4"])
+            act(T.u2[:], T.p5[:, 0:256], ["u2p"], ["u2"], ["p5"], bias=-4096.0)
+
+        if last:
+            places_to_write()
         act(T.xga[:], X0.indirect(T.al16[:]), ["xt", "al16"], ["xga"])
-        mm(T.p1[:, 0:256], T.idh[:], T.ar[:], True, False, ["idh", "ar"], ["ca_"], ["p1"])
-        mm(T.p0[:, 0:256], T.idh[:], T.ar[:], False, False, ["idh", "ar"], ["da"], ["p0"])
-        mm(T.p0[:, 0:256], T.ihn[:], T.ax[:], False, True, ["ihn", "ax"], ["da"], ["p0"])
+        mm(T.p1[:, 0:256], T.idh[:], T.ar[:], False, False, ["idh", "ar"], ["ca_"], ["p1"])
+        mm(T.p2[:, 0:256], T.idh[:], T.ar[:], False, False, ["idh", "ar"], ["da"], ["p2"])
+        mm(T.p2[:, 0:256], T.ihn[:], T.ax[:], False, True, ["ihn", "ax"], ["da"], ["p2"])
         nl = 16 if last else 32
 
         def equal_a(ms):
@@ -505,7 +566,7 @@ def rank_program(g, core, T, topo):
                 mm(T.p1[:, 256 - n:256], T.b4[:], T.em[:, o:o + n], False, False, ["b4", "em%d" % m], ["ca_"], ["p1"])
 
         equal_a(range(10))
-        ts(T.ed[:], T.p0[:, 0:256], 0.0, A.is_equal, ["da"], ["ed"], ["p0"])
+        ts(T.ed[:], T.p2[:, 0:256], 0.0, A.is_equal, ["da"], ["ed"], ["p2"])
         equal_a(range(10, 15))
         count_a(range(CA))
         to_list(T.p6[:, 192:192 + nl], T.w2, "w2", T.gg, "gg", nl, "wl", "p6")
@@ -520,10 +581,9 @@ def rank_program(g, core, T, topo):
         act(T.y2[:, 128:256], T.yy[:, 128:256], ["yy1"], ["y21"], bias=MAG)
         if not last:
             act(T.qo[:], T.y2[:, 128:256], ["y21"], ["qo"], bias=-MAG)
-        if t:
-            equal_v(range(MV // 2, MV))
-        else:
-            cp(T.uw[:, 0:512], T.ui[:], ["ui"], ["uw"])
+        if last:
+            new_places()
+            dma("y", "out", 64, ["uw"], ["yu"], T.yu[:], T.uw[:, 0:512])
 
         def x_and_q():
             mm(T.p3[:, 256:512], T.idb[:], Q[:], True, False, ["idb"] + qk, ["xq"], ["p3"])
@@ -535,23 +595,10 @@ def rank_program(g, core, T, topo):
         mm(T.p1[:, 0:256], T.b4[:], T.ed[:], False, True, ["b4", "ed"], ["ca_"], ["p1"])
         if not last:
             x_and_q()
-        act(T.u1[:], T.p4[:, 0:256], ["u1p"], ["u1"], ["p4"])
         act(T.h1[:], T.p3[:, 256:512], ["xq"], ["h1"], ["p3"], scale=0.5 + 1.0 / 2048, bias=MAG)
         act(T.xn[:], T.h1[:], ["h1"], ["xn"], bias=-MAG)
-        mm(T.p5[:, 0:256], T.idh[:], T.ar[:], True, False, ["idh", "ar"], ["u2p"], ["p5"])
-        for h in (0, 1):
-            mm(T.p5[:, 128 * h:128 * h + 128], T.eq[:, 128 * h:128 * h + 128], T.i4k[:], False, h == 1, ["eq%d" % h, "i4k"], ["u2p"], ["p5"])
-        act(T.u2[:], T.p5[:, 0:256], ["u2p"], ["u2"], ["p5"], bias=-4096.0)
-        if t:
-            for m, (o, n) in enumerate([(1920, 256)] + SEG):
-                mm(T.p0[:, 512 - n:512], T.b4[:], T.ev[:, o:o + n], m == 0, m == 15, ["b4", "ev", "evv"], ["cv_"], ["p0"])
-            act(T.vf[:], T.p0[:, 256:512], ["cv_"], ["vf"], ["p0"], func=F.Sign)
-
-        def list_v():
-            mm(T.p2[:, 256:272], T.idh[:], T.vlh[:], True, False, ["idh", "vlh"], ["cvl"], ["p2"])
-            to_list(T.p2[:, 256:272], T.wf, "wf", T.vf, "vf", 16, "cvl", "p2", False, True)
-
         if not last:
+            places_to_write()
             for k in range(GO):
                 gcopy(T.q16[:, 16 + k::32], T.qo[:], 128, ["qo"], ["q16h"])
             send(t + 1, "q", T.qo[:], "qo", T["qr%d" % (t + 1)][:], "qr%d" % (t + 1))
@@ -560,14 +607,11 @@ def rank_program(g, core, T, topo):
         act(QN[:, 1::2], T.y2[:, 128:256], ["y21"], [qnk[1]], bias=-MAG)
         if last:
             dma("y", "out", 64, qnk, ["yq"], T.yq[:], QN[:])
-        tt(T.dm[:], T.p1[:, 0:256], T.dgt[:], A.min, ["ca_", "dgt"], ["dm"], ["p1"])
-        scan(T.ds[:], T.zr[:], T.dm[:], A.mult, A.add, ["zr", "dm"], ["ds"])
+        scan(T.ds[:], T.dgt[:], T.p1[:, 0:256], A.max, A.min, ["ca_", "dgt"], ["ds"], ["p1"])
         cp(T.ap16[:], T.ds[:, 15::16], ["ds"], ["ap16"])
         if not last:
             cp(T.nxb[:].indirect(T.ap16[:]), T.nx2[:], ["nx2", "ap16"], ["nxb"])
             to_list(T.p7[:, 128:256], T.w2, "w2", T.nxb, "nxb", 128, "nxt", "p7")
-        if t:
-            list_v()
         cp(T.xt[:].indirect(T.ap16[:]), T.xn[:], ["xn", "ap16"], ["xt"])
         if not last:
             cp(T.nxl[:], T.p7[:, 128:256], ["nxt"], ["nxl"], ["p7"])
@@ -576,8 +620,7 @@ def rank_program(g, core, T, topo):
             for k in qnk:
                 wr[k], rd[k] = wr["qa"], dict(rd["qa"])
     dma("y", "out", 64, ["xt"], ["yx"], T.yx[:], X0)
-    new_places(ROUNDS - 1)
-    dma("y", "out", 64, ["uw"], ["yu"], T.yu[:], T.uw[:, 0:512])
+    new_recipients(ROUNDS - 1)
     act(T.vr[:], T.idw[:].indirect(T.vl16[:]), ["idw", "vl16"], ["vr"])
     dma("s", "out", 64, ["vr"], ["yv"], T.yv[:], T.vr[0:128:16, :])
     for s in SEMAPHORES:

@@ -6,30 +6,30 @@ SCRATCH = {}
 for _d, _names in (
         ("bfloat16", (("xt", 2560), ("nxb", 2560), ("rcb", 2048), ("x1", 2048), ("x2", 2048), ("x3", 2048), ("x4", 2048),
                       ("q16", 4096), ("qa", 256), ("qb", 256), ("qo", 128), ("qr0", 128), ("qr1", 128), ("qr2", 128),
-                      ("xg", 4096), ("ab", 4096), ("ca", 4096), ("cb", 4096), ("xg4", 2048), ("sg4", 2048), ("rr", 768),
-                      ("eq", 256), ("fl", 16), ("xc", 512), ("f3", 48), ("em", 1920), ("ed", 256), ("yv1", 2176),
-                      ("ev", 2176), ("vf", 256), ("gg", 512), ("nx2", 256), ("xga", 256), ("xn", 256),
-                      ("hl", 512), ("ch", 144), ("cg", 128), ("cf", 256), ("dg", 256), ("zr", 256), ("tri", 256),
-                      ("wf", 144), ("w2", 144), ("b8f", 8), ("b8g", 8), ("bs", 16), ("bx", 16), ("off", 256), ("b4", 128),
-                      ("base", 256), ("idb", 128), ("idn", 128), ("i4k", 128), ("i4n", 128), ("ones", 128))),
+                      ("xg", 4096), ("ab", 4096), ("ca", 4096), ("cb", 4096), ("xg4", 3072), ("rr", 768),
+                      ("eq", 256), ("fl", 16), ("xc", 512), ("f3", 48), ("em", 896), ("ed", 256), ("yv1", 1152),
+                      ("ev", 1152), ("vf", 256), ("gg", 512), ("nx2", 256), ("xga", 256), ("xn", 256),
+                      ("hl", 512), ("ch", 144), ("cg", 128), ("cf", 512), ("dg", 256), ("zr", 256), ("tri", 256),
+                      ("wf", 144), ("w2", 144), ("b8f", 8), ("bs", 24), ("bx", 24), ("off", 256), ("b4", 128),
+                      ("base", 256), ("idb", 128), ("idn", 128), ("i4k", 128), ("i4n", 128), ("ones", 256))),
         ("float16", (("nph", 128), ("npt", 128), ("sw", 512), ("idh", 128), ("ihn", 128), ("wh", 144), ("a0h", 16),
                      ("pd", 256), ("w1", 256), ("wb", 256), ("sc1", 256), ("sc2", 256), ("ar", 256),
                      ("az", 256), ("ax", 256), ("vrh", 256), ("vlh", 16), ("rph", 128))),
-        ("float32", (("uw", 768), ("idw", 2048), ("dd", 256), ("vl", 16), ("vn", 16), ("vr", 256), ("dgu", 256), ("lc", 16),
+        ("float32", (("uw", 768), ("idw", 2048), ("dd", 256), ("vl", 16), ("vn", 16), ("vr", 256), ("dgu", 256),
                      ("ka", 256), ("key", 256), ("s1", 256), ("a3", 48), ("u1", 256), ("u2", 256),
                      ("ws", 16), ("we", 16), ("wr0", 16), ("wr1", 16), ("wr2", 16), ("h1", 256), ("yy", 256), ("y2", 256),
                      ("nj", 32), ("nk", 16), ("cols", 32), ("dgt", 256), ("rst", 256), ("idf", 128),
                      ("ds", 256), ("sa", 8))),
-        ("int32", (("ui", 512), ("pvr", 2048), ("npi", 128), ("rpi", 128), ("ci", 16))),
+        ("int32", (("ui", 512), ("pvr", 2048), ("npi", 128), ("rpi", 128), ("ci", 32))),
         ("uint16", (("nxl", 128), ("d16", 256), ("vl16", 16), ("vp16", 16), ("ap16", 16), ("a016", 16), ("bl", 32),
-                    ("al16", 16), ("nl16", 16), ("exl", 8)))):
+                    ("al16", 16), ("nl16", 16), ("exl", 16)))):
     for _n, _c in _names:
         SCRATCH[_n] = ("sbuf", [128, _c], _d)
 for _k in range(8):
     SCRATCH["p%d" % _k] = ("psum", [128, 512], "float32")
 
 ROUNDS = 3
-LS = 128
+LA, LB = 64, 192
 XV0, XV = 1024, 768
 SEMAPHORES = ["cv", "cs", "ct", "cp", "ldx", "ldq", "ldu", "ldn", "ldr", "ldp", "ldb", "ldc", "out"]
 for _t in range(ROUNDS):
@@ -38,10 +38,11 @@ PARTS = 4
 EARLY = 4
 LAND = ("ab", "ca", "cb")
 SEMAPHORES += ["%s%d" % (_a, _c) for _a in ("fa", "fb", "fl") for _c in range(PARTS)]
-G0, S0 = 1, 5
+G0, S0 = 1, 6
 GE, GO = 7, 9
+EA = 8
 CA = 2
-MV = 5
+MW, MV = 2, 7
 FAR = 524288.0
 BIG = 1048576.0
 MAG = 12582912.0
@@ -209,9 +210,9 @@ def rank_program(g, core, T, topo):
             mm(out, w[:, 15 - k:143 - k], src[:, k:16 * n:16], st and k == 0, sp and k == 15, [wk, sk], [dk], [pk])
 
     def by_lane(pout, o, src, s0, l0, l1, w, wk, keys, dk, pk, alone, close=False):
-        n = w.shape[1]
+        w, n = w
         for k in range(16):
-            mm(pout[l0 % 128:(l1 - 1) % 128 + 1, o + k:o + 16 * n:16], src[:, 16 * (l0 - s0) + k:16 * (l1 - s0):16], w[:],
+            mm(pout[l0 % 128:(l1 - 1) % 128 + 1, o + k:o + 16 * n:16], src[:, 16 * (l0 - s0) + k:16 * (l1 - s0):16], w,
                alone, alone or (close and k == 15), [wk] + keys, [dk], [pk])
 
     Q16 = ["q16v", "q16g", "q16h", "q16s"]
@@ -227,8 +228,8 @@ def rank_program(g, core, T, topo):
     iota(T.ci[:, 0:1], [[0, 1]], 0, 1, ["ci0"], True)
     iota(T.ch[:], [[1, 144]], 0, -1, ["ch"])
     iota(T.cg[:], [[1, 8], [0, 16]], 0, 0, ["cg"])
-    iota(T.cf[:], [[0, 16], [1, 16]], 0, 0, ["cf"])
-    iota(T.ci[:, 8:16], [[16, 8]], 15, 0, ["ci1"], True)
+    iota(T.cf[:, 0:256], [[0, 16], [1, 16]], 0, 0, ["cf"])
+    iota(T.ci[:, 16:32], [[16, 16]], 15, 0, ["ci1"], True)
     op("v", ["ci0"], ["ci4"], [], lambda: V.tensor_scalar(T.ci[:, 2:3], T.ci[:, 0:1], 4, None, A.arith_shift_right))
     op("v", ["ci0"], ["ci3"], [], lambda: V.tensor_scalar(T.ci[:, 1:2], T.ci[:, 0:1], 15, None, A.bitwise_and))
     op("v", ["ci0"], ["ci6"], [], lambda: V.tensor_scalar(T.ci[:, 4:5], T.ci[:, 0:1], 1, None, A.bitwise_and))
@@ -249,21 +250,18 @@ def rank_program(g, core, T, topo):
     ts(T.wh[:], T.ch[:], col(7), A.is_equal, ["ch", "c7"], ["wh"])
     ts(T.b8f[:], T.cg[:, 0:128:16], col(1), A.is_equal, ["cg", "c1"], ["b8f"], (), FAR, A.mult)
     ts(T.b4[:], T.cg[:], col(1), A.is_equal, ["cg", "c1"], ["b4"], (), 4096.0, A.mult)
-    ts(T.dg[:], T.cf[:], col(0), A.is_equal, ["cf", "c0"], ["dg"])
-    cp(T.exl[:], T.ci[:, 8:16], ["ci1"], ["exl"])
+    CF = T.cf[:, 0:256]
+    ts(T.dg[:], CF, col(0), A.is_equal, ["cf", "c0"], ["dg"])
+    cp(T.exl[:], T.ci[:, 16:32], ["ci1"], ["exl"])
     act(col(8), col(0), ["c0"], ["c8"], bias=0.5)
     act(col(5), col(4), ["c4"], ["c5"], scale=-1.0, bias=1.0)
     act(col(6), col(0), ["c0"], ["c6"], scale=2.0)
-    act(T.ones[:], T.cg[:], ["cg"], ["ones"], scale=0.0, bias=1.0)
-    for w, k, x in ((T.idn, "idn", -1.0), (T.i4k, "i4k", 4096.0), (T.i4n, "i4n", -4096.0), (T.idf, "idf", 1.0)):
-        act(w[:], T.idb[:], ["idb"], [k], scale=x)
-    for w, k, x in ((T.b8g[:], "b8g", 0.5), (T.bs[:, 0:8], "bs", 32.0 / FAR), (T.bs[:, 8:16], "bs", -32.0 / FAR),
-                    (T.bx[:, 0:8], "bx", -16.0 / FAR), (T.bx[:, 8:16], "bx", 16.0 / FAR)):
-        act(w, T.b8f[:], ["b8f"], [k], scale=x)
-    act(T.base[:, 128:256], T.cg[:], ["cg"], ["base"], scale=0.0, bias=-8.5 * FAR)
-    for p0, p1, x in ((0, LS, -0.5), (LS, 128, -8.5)):
-        if p0 < p1:
-            act(T.base[p0:p1, 0:128], T.cg[p0:p1, :], ["cg"], ["base"], scale=0.0, bias=x * FAR)
+    act(T.idn[:], T.idb[:], ["idb"], ["idn"], scale=-1.0)
+    for j in range(3):
+        act(T.bs[:, 8 * j:8 * j + 8], T.b8f[:], ["b8f"], ["bs"], scale=32.0 * (-1) ** j / FAR)
+        act(T.bx[:, 8 * j:8 * j + 8], T.b8f[:], ["b8f"], ["bx"], scale=-16.0 * (-1) ** j / FAR)
+    for o, p0, p1, x in ((0, 0, LA, -8.5), (0, LA, 128, -1.0), (128, 0, LB - 128, -1.0), (128, LB - 128, 128, -8.5)):
+        act(T.base[p0:p1, o:o + 128], T.cg[p0:p1, :], ["cg"], ["base"], scale=0.0, bias=x * FAR)
     act(T.qo[:], T.qa[:, 1::2], ["qa"], ["qo"])
     iota(T.nj[:], [[512, 2], [16, 16]], 0, 0, ["nj"])
     iota(T.dgt[:], [[0, 256]], -1, 0, ["dgt"])
@@ -272,6 +270,7 @@ def rank_program(g, core, T, topo):
     send(0, "q", T.qo[:], "qo", T.qr0[:], "qr0")
     for k in range(G0, G0 + S0):
         act(T.q16[:, k::16], T.qa[:], ["qa"], ["q16s"])
+    iota(T.cf[:, 256:512], [[0, 16], [1, 16]], 0, 0, ["cf2"])
     iota(T.idw[:], [[1, 2048]], 0, 0, ["idw"])
     cp(T.nph[:], T.npi[:], ["npi"], ["nph"])
     vtr(T.npt[:], T.nph[:], ["nph"], ["npt"])
@@ -299,36 +298,39 @@ def rank_program(g, core, T, topo):
             for j, k in enumerate(("hi" + sk, "lo" + sk)):
                 dma("y", sem, 32, [k], [tk], tab[j:128:16, 0:2048], T.hl[:, o + 128 * j:o + 128 * j + 128])
 
-    ts(T.vl[:], T.nj[:, 0:16], 2.0, A.mult, ["nj", "c6"], ["vl"], (), col(6), A.add)
-    ts(T.lc[:], T.nj[:, 16:32], col(0), A.add, ["nj", "c0"], ["lc"])
-    cp(T.vp16[:], T.vl[:], ["vl"], ["vp16"])
-    ts(T.az[:], T.cf[:], 0.0, A.mult, ["cf"], ["az"])
-    ts(T.f3[:, 0::3], T.cf[:, 0:16], 0.0, A.mult, ["cf"], ["f3"])
-    ts(T.dgt[:, 0::16], T.lc[:], 1536.0, A.add, ["lc", "dgt"], ["dgt"])
-    act(T.zr[:], T.cf[:], ["cf"], ["zr"], func=F.Sign)
-    act(T.rst[:], T.zr[:], ["zr"], ["rst"], scale=-2.0 * BIG, bias=BIG)
+    def constants_for_the_lists():
+        ts(T.vp16[:], T.nj[:, 0:16], 2.0, A.mult, ["nj", "c6"], ["vp16"], (), col(6), A.add)
+        ts(T.az[:], CF, 0.0, A.mult, ["cf"], ["az"])
+        ts(T.f3[:, 0::3], T.cf[:, 0:16], 0.0, A.mult, ["cf"], ["f3"])
+        ts(T.dgt[:, 0::16], T.nj[:, 16:32], col(0), A.add, ["nj", "c0", "dgt"], ["dgt"], (), 1536.0, A.add)
 
     def constants_for_the_writes():
-        act(T.dgu[:], T.dgt[:], ["dgt"], ["dgu"], bias=-1536.0)
+        act(T.zr[:], CF, ["cf"], ["zr"], func=F.Sign)
+        act(T.rst[:], T.zr[:], ["zr"], ["rst"], scale=-2.0 * BIG, bias=BIG)
+        act(T.ones[:], CF, ["cf"], ["ones"], scale=0.0, bias=1.0)
+        for w, k, x in ((T.idf, "idf", 1.0), (T.i4n, "i4n", -4096.0), (T.i4k, "i4k", 4096.0)):
+            act(w[:], T.idb[:], ["idb"], [k], scale=x)
         act(T.off[:], T.dg[:], ["dg"], ["off"], scale=-BIG, bias=BIG)
-        act(T.vf[:], T.cf[:], ["cf", "c8"], ["vf"], scale=-1.0, bias=col(8), func=F.Sign)
+        act(T.vf[:], CF, ["cf", "c8"], ["vf"], scale=-1.0, bias=col(8), func=F.Sign)
         act(T.tri[:], T.vf[:], ["vf"], ["tri"], scale=4096.0, func=F.Relu)
 
-    SEG = [(0, 0)] * 15
-    _o = 0
-    for m in range(15):
-        SEG[m] = (_o, 240 - 16 * m)
-        _o += 240 - 16 * m
+    SEG = []
+    for j in range(7):
+        for h in (0, 1):
+            m, o = 8 * h + j, SEG[-1][1] + SEG[-1][3] - SEG[-1][2] if SEG else 0
+            SEG.append((m, o, 16 * m + 16, 128 * h + 128))
+    ND = 896
+    HALVES = (slice(128, 256), slice(0, 128))
 
-    def new_places():
-        tt(T.uw[:].indirect(T.vp16[:]), T.u1[:], T.u2[:], A.max, ["u1", "u2", "vp16"], ["uw"])
+    def new_places(H):
+        tt(T.uw[:].indirect(T.vp16[:, H.start // 16:H.stop // 16]), T.u1[:, H], T.u2[:, H], A.max, ["u1", "u2", "vp16", "uw"], ["uw"])
 
     def new_recipients(t):
-        tt(T.vl[:], T.we[:], T["wr%d" % t][:], A.add, ["we", "wr%d" % t], ["vl"])
-        cp(T.vl16[:], T.vl[:], ["vl"], ["vl16"])
+        mm(T.p7[:, 64:80], T.idf[:], T.we[:], True, False, ["idf", "we"], ["vlp"], ["p7"])
+        mm(T.p7[:, 64:80], T.idf[:], T["wr%d" % t][:], False, True, ["idf", "wr%d" % t], ["vlp"], ["p7"])
+        cp(T.vl16[:], T.p7[:, 64:80], ["vlp"], ["vl16"], ["p7"])
 
     Q, QN, qk, qnk = T.qa, T.qb, ["qa"], ["qbe", "qbo"]
-    LV = 256 - LS
     X0 = T.xt[:, 0:2048]
     for t in range(ROUNDS):
         last = t == ROUNDS - 1
@@ -336,20 +338,25 @@ def rank_program(g, core, T, topo):
 
         def walk(x, xk, out, ok, l0, l1):
             tt(out[:, 16 * l0:16 * l1], x[:].indirect(T.d16[:, l0:l1]), T.q16[:, 16 * l0:16 * l1], A.is_lt,
-               xk + ["d16"] + Q16, [ok + str(l0)])
+               xk + ["d16"] + Q16, ok)
 
         def wsum(pout, o, out, ok, h, pk, dk):
-            by_lane(pout, o + 128 * h, out, 0, 128 * h, 128 * h + 128, T.b8f, "b8f", [ok + str(128 * h)], dk + str(h), pk, True)
+            by_lane(pout, o + 128 * h, out, 0, 128 * h, 128 * h + 128, (T.b8f[:], 8), "b8f", [ok, ok.replace("cb", "cs")],
+                    dk + str(h), pk, True)
 
-        def diff(c, src, sk, lane0):
-            pk = ("p2", "p3")[c % 2]
-            j = 512 * c
-            mm(T[pk][:], T.idb[:], src[:, j:j + 512], True, False, ["idb", sk], [pk + "d"], [pk])
-            mm(T[pk][:], T.idn[:], T.q16[:, 16 * lane0 + j:16 * lane0 + j + 512], False, True, ["idn"] + Q16, [pk + "d"], [pk])
+        BANKS = ("p2", "p3", "p5", "p6")
 
-        def sign(c):
-            pk = ("p2", "p3")[c % 2]
-            act(T.sg4[:, 512 * c:512 * c + 512], T[pk][:], [pk + "d"], ["sg4"], [pk], func=F.Sign, scale=-1.0, bias=-0.5)
+        def less_q(c):
+            pk, j = BANKS[c % 4], 16 * LA + 512 * c
+            mm(T[pk][:], T.idn[:], T.q16[:, j:j + 512], True, False, ["idn"] + Q16, [pk + "d"], [pk])
+
+        def diff(c, sk):
+            pk = BANKS[c % 4]
+            mm(T[pk][:], T.idb[:], T.xg4[:, 512 * c:512 * c + 512], False, True, ["idb", sk], [pk + "d"], [pk])
+
+        def sign(c, h):
+            pk, j = BANKS[c % 4], 16 * LA + 512 * c
+            act(T.cb[:, j:j + 512], T[pk][:], [pk + "d"], ["cs%d" % h], [pk], func=F.Sign, scale=-1.0, bias=-0.5)
 
         def marks(c):
             l0, l1 = 256 // PARTS * c, 256 // PARTS * (c + 1)
@@ -357,38 +364,35 @@ def rank_program(g, core, T, topo):
             fold(t, c)
 
         def scores(h, folded):
-            pk, parts = ("p4", "p5")[h], range(PARTS // 2 * h, PARTS // 2 * (h + 1))
-            if folded:
-                by_lane(T[pk], 0, T.ab, 0, 128 * h, 128 * h + 128, T.bs, "bs", ["ab%d" % c for c in parts], "sc%d" % h, pk, False, True)
-            else:
-                mm(T[pk][:, 0:256], T.idb[:], T.cf[:], True, False, ["idb", "cf"], ["sc%d" % h], [pk])
-                by_lane(T[pk], 0, T.xg, 0, 128 * h, 128 * h + 128, T.bx, "bx", ["xg%d" % c for c in parts], "sc%d" % h, pk, False)
+            parts = range(PARTS // 2 * h, PARTS // 2 * (h + 1))
+            src, sk, w, wk = (T.ab, "ab", T.bs, "bs") if folded else (T.xg, "xg", T.bx, "bx")
+            by_lane(T.p4, 256 * h, src, 0, 128 * h, 128 * h + 128, (w[:, 8 * h:8 * h + 16], 16), wk, [sk + str(c) for c in parts],
+                    "sc", "p4", False, folded and h == 1)
 
         def lower(h):
-            pk = ("p4", "p5")[h]
-            act(T.ka[:, 128 * h:128 * h + 128], T[pk][:, 0:128], ["sc%d" % h], ["ka%d" % h], [pk], bias=-0.5 * FAR)
+            act(T.ka[:, 128 * h:128 * h + 128], T.p4[:, 384 * h:384 * h + 128], ["sc"], ["ka"], ["p4"], bias=-0.5 * FAR)
 
         def over(j, pp, o, keys, pk):
-            act(T.rr[:, 256 * j:256 * j + 256], pp[:, o:o + 256], keys, ["rr%d" % j], [pk], func=F.Relu, scale=16.0, bias=-128.0 * FAR)
+            act(T.rr[:, 256 * j:256 * j + 256], pp[:, o:o + 256], keys, ["rr%d" % j], [pk], func=F.Relu, scale=32.0, bias=-256.0 * FAR)
 
+        NX = ["nxl", "nxv"]
         act(T.x1[:, xv:2048], X0.indirect(T.nxl[:, xv // 16:128]), ["xt", "nxl"], ["x1b"])
-        cp(T.x1[:, 0:xv], X0.indirect(T.nxl[:, 0:xv // 16]), ["xt", "nxl"], ["x1a"])
         if t:
-            new_places()
+            cp(T.nxl[:, 0:xv // 16], T.p5[:, 256:256 + xv // 16], ["nxu"], ["nxv"], ["p5"])
+        cp(T.x1[:, 0:xv], X0.indirect(T.nxl[:, 0:xv // 16]), ["xt"] + NX, ["x1a"])
+        if t:
+            new_places(HALVES[1])
             new_recipients(t - 1)
             cp(T.d16[:], T.uw[:, 0:512].indirect(T.vl16[:]), ["uw", "vl16"], ["d16"])
-            cp(T.vlh[:], T.vl[:], ["vl"], ["vlh"])
         else:
             cp(T.d16[:], T.ui[:, 0:512:2], ["ui"], ["d16"])
-            cp(T.dd[:], T.ui[:, 0:512:2], ["ui"], ["dd"])
-        act(T.x2[:], T.x1[:].indirect(T.nxl[:]), ["x1a", "x1b", "nxl"], ["x2"])
-        walk(T.x1, ["x1a", "x1b"], T.ca, "ca", 0, 128)
+        act(T.x2[:], T.x1[:].indirect(T.nxl[:]), ["x1a", "x1b"] + NX, ["x2"])
+        walk(T.x1, ["x1a", "x1b"], T.ca, ["ca0", "ca1"], 0, 256)
         for c in range(EARLY):
             marks(c)
-        wsum(T.p0, 0, T.ca, "ca", 0, "p0", "k1")
-        walk(T.x1, ["x1a", "x1b"], T.ca, "ca", 128, 256)
-        wsum(T.p0, 0, T.ca, "ca", 1, "p0", "k1")
-        act(T.x3[:], T.x2[:].indirect(T.nxl[:]), ["x2", "nxl"], ["x3"])
+        wsum(T.p0, 0, T.ca, "ca0", 0, "p0", "k1")
+        wsum(T.p0, 0, T.ca, "ca1", 1, "p0", "k1")
+        act(T.x3[:], T.x2[:].indirect(T.nxl[:]), ["x2"] + NX, ["x3"])
         for c in range(EARLY, PARTS):
             marks(c)
         if t:
@@ -396,91 +400,90 @@ def rank_program(g, core, T, topo):
         else:
             tables_of_two_parts()
         over(0, T.p0, 0, ["k10", "k11"], "p0")
-        walk(T.x2, ["x2"], T.cb, "cb", 0, 128)
-        wsum(T.p1, 0, T.cb, "cb", 0, "p1", "k2")
-        act(T.x4[:], T.x3[:].indirect(T.nxl[:]), ["x3", "nxl"], ["x4"])
-        walk(T.x2, ["x2"], T.cb, "cb", 128, 256)
-        wsum(T.p1, 0, T.cb, "cb", 1, "p1", "k2")
+        if t:
+            act(T.vl[:], T.p7[:, 64:80], ["vlp"], ["vl"], ["p7"])
+            act(T.vn[:], T.p7[:, 64:80], ["vlp"], ["vn"], ["p7"], scale=-1.0)
+        walk(T.x2, ["x2"], T.cb, ["cb0", "cb1", "cs0", "cs1"], 0, 256)
+        act(T.x4[:], T.x3[:].indirect(T.nxl[:]), ["x3"] + NX, ["x4"])
+        mm(T.p4[:], T.idb[:], T.cf[:], True, False, ["idb", "cf", "cf2"], ["sc"], ["p4"])
         scores(0, False)
         scores(1, False)
-        walk(T.x3, ["x3"], T.ca, "ca", 0, 128)
-        wsum(T.p0, 256, T.ca, "ca", 0, "p0", "k3")
+        wsum(T.p1, 0, T.cb, "cb0", 0, "p1", "k2")
+        wsum(T.p1, 0, T.cb, "cb1", 1, "p1", "k2")
+        walk(T.x3, ["x3"], T.ca, ["ca0"], 0, 128)
+        wsum(T.p0, 256, T.ca, "ca0", 0, "p0", "k3")
         over(1, T.p1, 0, ["k20", "k21"], "p1")
-        share = [(l, min(l + 64, LS)) for l in range(0, LS, 64)]
-        for l0, l1 in share:
-            act(T.xg4[:, 16 * l0:16 * l1], T.x4[:].indirect(T.d16[:, l0:l1]), ["x4", "d16"], ["xg4%d" % (l0 // 64)])
-        diff(0, T.xg4, "xg40", 0)
-        diff(1, T.xg4, "xg40", 0)
+        def on_top(src, sk):
+            mm(T.p1[:, 256:512], T.idb[:], src, sk == "base", False, ["idb", sk], ["k4"], ["p1"])
+
+        for h, (l0, l1) in enumerate(((LA, 128), (128, LB))):
+            act(T.xg4[:, 16 * (l0 - LA):16 * (l1 - LA)], T.x4[:].indirect(T.d16[:, l0:l1]), ["x4", "d16"], ["xg4%d" % h])
+        NA, NB = (128 - LA) // 32, (LB - LA) // 32
+        for c in range(NB):
+            less_q(c)
+        on_top(T.base[:], "base")
+        on_top(T.rr[:, 0:256], "rr0")
+        on_top(T.rr[:, 256:512], "rr1")
         scores(0, True)
-        walk(T.x3, ["x3"], T.ca, "ca", 128, 256)
-        wsum(T.p0, 256, T.ca, "ca", 1, "p0", "k3")
-        sign(0)
-        sign(1)
-        for c in range(2, LS // 32):
-            diff(c, T.xg4, "xg41", 0)
-        lower(0)
+        for c in range(NA):
+            diff(c, "xg40")
+        walk(T.x3, ["x3"], T.ca, ["ca1"], 128, 256)
+        wsum(T.p0, 256, T.ca, "ca1", 1, "p0", "k3")
+        for c in range(NA, NB):
+            diff(c, "xg41")
+        walk(T.x4, ["x4"], T.cb, ["cb0"], 0, LA)
+        walk(T.x4, ["x4"], T.cb, ["cb1"], LB, 256)
+        for c in range(NA):
+            sign(c, 0)
         over(2, T.p0, 256, ["k30", "k31"], "p0")
-        for c in range(2, LS // 32):
-            sign(c)
-        if LS < 128:
-            walk(T.x4, ["x4"], T.cb, "cb", LS, 128)
-        walk(T.x4, ["x4"], T.cb, "cb", 128, 256)
-
-        FOURTH = ((T.p1, 256, "p1"), (T.p6, 0, "p6"))
-
-        def on_top(h, src, sk, st, sp):
-            pp, o, pk = FOURTH[h]
-            mm(pp[:, o:o + 128], T.idb[:], src, st, sp, ["idb", sk], ["k4%d" % h], [pk])
-
-        for h in (0, 1):
-            on_top(h, T.base[:, 128 * h:128 * h + 128], "base", True, False)
-            for j in range(2):
-                on_top(h, T.rr[:, 256 * j + 128 * h:256 * j + 128 * h + 128], "rr%d" % j, False, False)
+        by_lane(T.p1, 256, T.cb, 0, 0, 128, (T.b8f[:], 8), "b8f", ["cb0", "cs0"], "k4", "p1", False)
         scores(1, True)
+        on_top(T.rr[:, 512:768], "rr2")
+        for c in range(NA, NB):
+            sign(c, 1)
+        lower(0)
         lower(1)
         if t == 0:
             constants_for_the_writes()
-        on_top(1, T.rr[:, 640:768], "rr2", False, False)
-        if LS < 128:
-            by_lane(T.p1, 256, T.cb, 0, LS, 128, T.b8f, "b8f", ["cb%d" % LS], "k40", "p1", False)
-        by_lane(T.p1, 256, T.sg4, 0, 0, LS, T.b8g, "b8g", ["sg4"], "k40", "p1", False)
-        on_top(0, T.rr[:, 512:640], "rr2", False, True)
-        by_lane(T.p6, 0, T.cb, 0, 128, 256, T.b8f, "b8f", ["cb128"], "k41", "p6", False, True)
-        def equal_v(ms):
-            for m in ms:
-                o, n = SEG[m]
-                ts(T.ev[:, o:o + n], T.vrh[:, 256 - n:256], T.vl[:, m:m + 1], A.is_equal, ["vrh", "vl"], ["evv"])
+        by_lane(T.p1, 384, T.cb, 0, 128, 256, (T.b8f[:], 8), "b8f", ["cb1", "cs1"], "k4", "p1", False, True)
+        def equal_v(segs):
+            for m, o, c0, c1 in segs:
+                ts(T.ev[:, o:o + c1 - c0], T.vrh[:, c0:c1], T.vl[:, m:m + 1], A.is_equal, ["vrh", "vl"], ["evv"])
 
         if t:
+            cp(T.vlh[:], T.vl[:], ["vl"], ["vlh"])
             cp(T.vrh[:], T.idw[:].indirect(T.vl16[:]), ["idw", "vl16"], ["vrh"])
+            equal_v(SEG[:MW])
             act(T.vr[:], T.idw[:].indirect(T.vl16[:]), ["idw", "vl16"], ["vr"])
-            act(T.vn[:], T.vl[:], ["vl"], ["vn"], scale=-1.0)
-            for m in range(MV, 15):
-                o, n = SEG[m]
-                act(T.yv1[:, o:o + n], T.vr[:, 256 - n:256], ["vr", "vn"], ["yv1"], func=F.Abs, bias=T.vn[:, m:m + 1])
+            for m, o, c0, c1 in SEG[MV:]:
+                act(T.yv1[:, o:o + c1 - c0], T.vr[:, c0:c1], ["vr", "vn"], ["yv1"], func=F.Abs, bias=T.vn[:, m:m + 1])
             mm(T.p2[:, 0:256], T.idb[:], T.tri[:], True, False, ["idb", "tri"], ["dv"], ["p2"])
             for j in range(16):
                 mm(T.p2[:, j:256:16], T.ihn[:], T.vlh[:], False, False, ["ihn", "vlh"], ["dv"], ["p2"])
             mm(T.p2[:, 0:256], T.idh[:], T.vrh[:], False, True, ["idh", "vrh"], ["dv"], ["p2"])
-            o = SEG[MV][0]
-            act(T.yv1[:, 1920:2176], T.p2[:, 0:256], ["dv"], ["yv1"], ["p2"], func=F.Abs)
-            act(T.ev[:, o:2176], T.yv1[:, o:2176], ["yv1"], ["ev"], func=F.Relu, scale=-1.0, bias=1.0)
-        for h, (pp, pk, o) in enumerate(((T.p1, "p1", 256), (T.p6, "p6", 0))):
-            H, k, ps = slice(128 * h, 128 * h + 128), str(h), ("p4", "p5")[h]
-            tt(T.key[:, H], pp[:, o:o + 128], T.ka[:, H], A.max, ["ka" + k, "k4" + k], ["key" + k], [pk])
-            tt(T.key[:, H], T[ps][:, 128:256], T.key[:, H], A.min, ["key" + k, "sc" + k], ["key" + k], [ps])
-            scan(T.s1[:, H], T.rst[:, H], T.key[:, H], A.max, A.min, ["rst", "key" + k], ["s1" + k])
-            tt(T.eq[:, H], T.s1[:, H].indirect(T.exl[:]), T.key[:, H], A.is_equal, ["s1" + k, "exl", "key" + k], ["eq" + k])
-            mm(T.p3[:, H], T.eq[:, H], T.idb[:], True, True, ["eq" + k, "idb"], ["oh"], ["p3"])
-        ts(T.fl[:], T.s1[:, 15::16], -0.25 * FAR, A.is_ge, ["s10", "s11"], ["fl"])
-        mm(T.p4[:, 400:416], T.ones[:], T.fl[:], True, True, ["ones", "fl"], ["nn"], ["p4"])
+            act(T.yv1[:, ND:ND + 256], T.p2[:, 0:256], ["dv"], ["yv1"], ["p2"], func=F.Abs)
+        if t == 0:
+            cp(T.dd[:], T.ui[:, 0:512:2], ["ui"], ["dd"])
+        tt(T.key[:], T.p1[:, 256:512], T.ka[:], A.max, ["ka", "k4"], ["key"], ["p1"])
+        tt(T.key[:], T.p4[:, 128:384], T.key[:], A.min, ["key", "sc"], ["key"], ["p4"])
+        scan(T.s1[:], T.rst[:], T.key[:], A.max, A.min, ["rst", "key"], ["s1"])
+        tt(T.eq[:], T.s1[:].indirect(T.exl[:]), T.key[:], A.is_equal, ["s1", "exl", "key"], ["eq"])
+        act(T.fl[:], T.s1[:, 15::16], ["s1"], ["fl"], func=F.Sign, bias=0.25 * FAR)
+        if t:
+            o = SEG[MV][1]
+            act(T.ev[:, o:ND + 256], T.yv1[:, o:ND + 256], ["yv1"], ["ev"], func=F.Relu, scale=-1.0, bias=1.0)
+        for h in (0, 1):
+            mm(T.p3[:, 128 * h:128 * h + 128], T.eq[:, 128 * h:128 * h + 128], T.idb[:], True, True, ["eq", "idb"], ["oh"], ["p3"])
+        mm(T.p6[:, 0:16], T.ones[:, 0:128], T.fl[:], True, True, ["ones", "fl"], ["nn"], ["p6"])
         tt(T.pd[:], T.p3[:, 0:256], T.dd[:], A.mult, ["oh", "dd"], ["pd"], ["p3"])
         to_list(T.p7[:, 0:16], T.wh, "wh", T.pd, "pd", 16, "a0", "p7")
         if t:
-            equal_v(range(MV))
+            equal_v(SEG[MW:MV])
+        else:
+            constants_for_the_lists()
         cp(T.a016[:], T.p7[:, 0:16], ["a0"], ["a016"], ["p7"])
         sa, ra = T.sa[:, t:t + 1], T.sa[:, 4 + t:5 + t]
-        act(T.nk[:], T.p4[:, 400:416], ["nn"], ["nk", "n"], ["p4"], accum_out=col(16))
+        act(T.nk[:], T.p6[:, 0:16], ["nn"], ["nk", "n"], ["p6"], scale=0.5, bias=64.0, accum_out=col(16))
         act(col(17), col(16), ["n"], ["n1"], scale=1.0 / 256, bias=-0.498046875)
         act(col(20), col(16), ["n"], ["n4"], scale=0.5, bias=-0.25)
         act(col(18), col(17), ["n1"], ["n2"], bias=MAG)
@@ -488,27 +491,41 @@ def rank_program(g, core, T, topo):
         act(sa, col(19), ["n3", "n4"], ["sa%d" % t], scale=-128.0, bias=col(20))
         send(t, "a", sa, "sa%d" % t, ra, "ra%d" % t)
         act(T.yy[:, 0:128], Q[:, 0::2], qk + ["sa%d" % t], ["yy0"], scale=0.5, bias=sa)
+        act(T.y2[:, 0:128], T.yy[:, 0:128], ["yy0"], ["y20"], bias=MAG)
+        act(QN[:, 0::2], T.y2[:, 0:128], ["y20"], [qnk[0]], bias=-MAG)
+        if not last:
+            for k in range(GE):
+                gcopy(T.q16[:, k::32], QN[:, 0::2], 128, [qnk[0]], ["q16g"])
         if t:
             mm(T.p0[:, 256:512], T.idb[:], T.off[:], True, False, ["idb", "off"], ["cv_"], ["p0"])
             mm(T.p0[:, 256:512], T.idh[:], T.vrh[:], False, False, ["idh", "vrh"], ["cv_"], ["p0"])
-            for m, (o, n) in enumerate(SEG + [(1920, 256)]):
-                mm(T.p0[:, 512 - n:512], T.b4[:], T.ev[:, o:o + n], False, m == 15, ["b4", "evv" if m < MV else "ev"], ["cv_"], ["p0"])
+            for j, (m, o, c0, c1) in enumerate(SEG + [(0, ND, 0, 256)]):
+                mm(T.p0[:, 256 + c0:256 + c1], T.b4[:], T.ev[:, o:o + c1 - c0], False, j == len(SEG), ["b4", "evv" if j < MV else "ev"],
+                   ["cv_"], ["p0"])
         tt(T.w1[:], T.pvr[:].indirect(T.a016[:]), T.dg[:], A.mult, ["pvr", "a016", "dg"], ["w1"])
         cp(T.a0h[:], T.p7[:, 0:16], ["a0"], ["a0h"], ["p7"])
         scan(T.sc1[:], T.zr[:], T.w1[:], A.mult, A.add, ["zr", "w1"], ["sc1"])
         cp(T.bl[:, 0:16], T.sc1[:, 15::16], ["sc1"], ["bl0"])
         tt(T.wb[:], T.pvr[:].indirect(T.bl[:, 0:16]), T.dg[:], A.mult, ["pvr", "bl0", "dg"], ["wb"])
+        evens = [] if last else list(range(GE, 16))
+
+        def even_copies(ks):
+            for k in ks:
+                act(T.q16[:, k::32], T.y2[:, 0:128], ["y20"], ["q16s"], bias=-MAG)
+
+        even_copies(evens[:3])
         act(T.xga[:], X0.indirect(T.bl[:, 0:16]), ["xt", "bl0"], ["xga"])
         mm(T.p3[:, 256:512], T.idn[:], Q[:], True, False, ["idn"] + qk, ["xq"], ["p3"])
+        mm(T.p4[:, 0:256], T.idf[:], T.dd[:], True, False, ["idf", "dd"], ["u1p"], ["p4"])
         mm(T.p3[:, 256:512], T.idb[:], T.xga[:], False, True, ["idb", "xga"], ["xq"], ["p3"])
-        act(T.y2[:, 0:128], T.yy[:, 0:128], ["yy0"], ["y20"], bias=MAG)
-        act(QN[:, 0::2], T.y2[:, 0:128], ["y20"], [qnk[0]], bias=-MAG)
+        even_copies(evens[3:5])
         act(T.xc[:, 0:256], T.p3[:, 256:512], ["xq"], ["xc0"], ["p3"], func=F.Sign, scale=-1.0, bias=-0.5)
-        if not last:
-            for k in range(GE):
-                gcopy(T.q16[:, k::32], QN[:, 0::2], 128, [qnk[0]], ["q16g"])
-            for k in range(GE, 16):
-                act(T.q16[:, k::32], T.y2[:, 0:128], ["y20"], ["q16s"], bias=-MAG)
+        even_copies(evens[5:])
+        for h in (0, 1):
+            mm(T.p4[:, 128 * h:128 * h + 128], T.eq[:, 128 * h:128 * h + 128], T.i4n[:], False, h == 1, ["eq", "i4n"], ["u1p"], ["p4"])
+        act(T.u1[:], T.p4[:, 0:256], ["u1p"], ["u1"], ["p4"])
+        if t == 0:
+            act(T.dgu[:], T.dgt[:], ["dgt"], ["dgu"], bias=-1536.0)
         mm(T.p6[:, 130:176:3], T.idh[:], T.a0h[:], True, True, ["idh", "a0h"], ["d3"], ["p6"])
         mm(T.p6[:, 129:176:3], T.ihn[:], T.a0h[:], True, False, ["ihn", "a0h"], ["d3"], ["p6"])
         mm(T.p6[:, 129:176:3], T.idh[:], T.sc1[:, 15::16], False, True, ["idh", "sc1"], ["d3"], ["p6"])
@@ -521,9 +538,9 @@ def rank_program(g, core, T, topo):
             mm(T.p7[:, 16:48], T.wf[:, 15 - k:143 - k], T.xc[:, k::16], k == 0, k == 15, ["wf", "xc0", "xc1"], ["b2"], ["p7"])
         mm(T.p2[:, 0:256], T.idb[:], T.tri[:], True, False, ["idb", "tri"], ["da"], ["p2"])
         mm(T.p1[:, 0:256], T.idb[:], T.off[:], True, False, ["idb", "off"], ["ca_"], ["p1"])
-        mm(T.p4[:, 0:256], T.idf[:], T.dd[:], True, False, ["idf", "dd"], ["u1p"], ["p4"])
+        mm(T.p5[:, 0:256], T.i4n[:], T.ones[:], True, False, ["i4n", "ones"], ["u2p"], ["p5"])
         for h in (0, 1):
-            mm(T.p4[:, 128 * h:128 * h + 128], T.eq[:, 128 * h:128 * h + 128], T.i4n[:], False, h == 1, ["eq%d" % h, "i4n"], ["u1p"], ["p4"])
+            mm(T.p5[:, 128 * h:128 * h + 128], T.eq[:, 128 * h:128 * h + 128], T.i4k[:], False, False, ["eq", "i4k"], ["u2p"], ["p5"])
         if t:
             scan(T.ds[:], T.dgu[:], T.p0[:, 256:512], A.max, A.min, ["cv_", "dgu"], ["ds"], ["p0"])
             cp(T.vp16[:], T.ds[:, 15::16], ["ds"], ["vp16"])
@@ -539,50 +556,47 @@ def rank_program(g, core, T, topo):
         act(T.gg[:, 0:256], T.rcb[:].indirect(T.al16[:]), ["rcb", "al16"], ["gg"])
         if not last:
             act(T.gg[:, 256:512], T.nxb[:, 0:2048].indirect(T.al16[:]), ["nxb", "al16"], ["gg"])
+        nl = 16 if last else 32
 
-        def places_to_write():
-            mm(T.p5[:, 0:256], T.idh[:], T.ar[:], True, False, ["idh", "ar"], ["u2p"], ["p5"])
-            for h in (0, 1):
-                mm(T.p5[:, 128 * h:128 * h + 128], T.eq[:, 128 * h:128 * h + 128], T.i4k[:], False, h == 1, ["eq%d" % h, "i4k"], ["u2p"], ["p5"])
-            act(T.u1[:], T.p4[:, 0:256], ["u1p"], ["u1"], ["p4"])
-            act(T.u2[:], T.p5[:, 0:256], ["u2p"], ["u2"], ["p5"], bias=-4096.0)
+        def lists_of_w_and_nx():
+            to_list(T.p6[:, 192:192 + nl], T.w2, "w2", T.gg, "gg", nl, "wl", "p6")
+            if not last:
+                cp(T.nl16[:], T.p6[:, 208:224], ["wl"], ["nl16"], ["p6"])
+            act(T.ws[:], T.p6[:, 192:208], ["wl", "c4"], ["ws"], ["p6"], scale=col(4))
+            send(t, "w", T.ws[:], "ws", T["wr%d" % t][:], "wr%d" % t)
 
         if last:
-            places_to_write()
+            lists_of_w_and_nx()
+        mm(T.p5[:, 0:256], T.idh[:], T.ar[:], False, True, ["idh", "ar"], ["u2p"], ["p5"])
+        act(T.u2[:], T.p5[:, 0:256], ["u2p"], ["u2"], ["p5"])
         act(T.xga[:], X0.indirect(T.al16[:]), ["xt", "al16"], ["xga"])
         mm(T.p1[:, 0:256], T.idh[:], T.ar[:], False, False, ["idh", "ar"], ["ca_"], ["p1"])
         mm(T.p2[:, 0:256], T.idh[:], T.ar[:], False, False, ["idh", "ar"], ["da"], ["p2"])
         mm(T.p2[:, 0:256], T.ihn[:], T.ax[:], False, True, ["ihn", "ax"], ["da"], ["p2"])
-        nl = 16 if last else 32
 
-        def equal_a(ms):
-            for m in ms:
-                o, n = SEG[m]
-                ts(T.em[:, o:o + n], T.ar[:, 256 - n:256], T.a3[:, 3 * m + 2:3 * m + 3], A.is_equal, ["ar", "al"], ["em%d" % m])
+        def equal_a(segs):
+            for m, o, c0, c1 in segs:
+                ts(T.em[:, o:o + c1 - c0], T.ar[:, c0:c1], T.a3[:, 3 * m + 2:3 * m + 3], A.is_equal, ["ar", "al"], ["em%d" % m])
 
-        def count_a(ms):
-            for m in ms:
-                o, n = SEG[m]
-                mm(T.p1[:, 256 - n:256], T.b4[:], T.em[:, o:o + n], False, False, ["b4", "em%d" % m], ["ca_"], ["p1"])
+        def count_a(segs):
+            for m, o, c0, c1 in segs:
+                mm(T.p1[:, c0:c1], T.b4[:], T.em[:, o:o + c1 - c0], False, False, ["b4", "em%d" % m], ["ca_"], ["p1"])
 
-        equal_a(range(10))
+        equal_a(SEG[:EA])
         ts(T.ed[:], T.p2[:, 0:256], 0.0, A.is_equal, ["da"], ["ed"], ["p2"])
-        equal_a(range(10, 15))
-        count_a(range(CA))
-        to_list(T.p6[:, 192:192 + nl], T.w2, "w2", T.gg, "gg", nl, "wl", "p6")
+        equal_a(SEG[EA:])
+        count_a(SEG[:CA])
         if not last:
-            cp(T.nl16[:], T.p6[:, 208:224], ["wl"], ["nl16"], ["p6"])
-        act(T.ws[:], T.p6[:, 192:208], ["wl", "c4"], ["ws"], ["p6"], scale=col(4))
-        send(t, "w", T.ws[:], "ws", T["wr%d" % t][:], "wr%d" % t)
-        if not last:
+            lists_of_w_and_nx()
             act(T.nx2[:], T.nxb[:, 0:2048].indirect(T.nl16[:]), ["nxb", "nl16"], ["nx2"])
         act(T.we[:], T.p6[:, 192:208], ["wl", "c5"], ["we"], ["p6"], scale=col(5))
         act(T.yy[:, 128:256], T["qr%d" % t][:], ["qr%d" % t, "ra%d" % t], ["yy1"], scale=0.5, bias=ra)
         act(T.y2[:, 128:256], T.yy[:, 128:256], ["yy1"], ["y21"], bias=MAG)
         if not last:
             act(T.qo[:], T.y2[:, 128:256], ["y21"], ["qo"], bias=-MAG)
+        new_places(HALVES[0])
         if last:
-            new_places()
+            new_places(HALVES[1])
             dma("y", "out", 64, ["uw"], ["yu"], T.yu[:], T.uw[:, 0:512])
 
         def x_and_q():
@@ -591,14 +605,13 @@ def rank_program(g, core, T, topo):
 
         if last:
             x_and_q()
-        count_a(range(CA, 15))
+        count_a(SEG[CA:])
         mm(T.p1[:, 0:256], T.b4[:], T.ed[:], False, True, ["b4", "ed"], ["ca_"], ["p1"])
         if not last:
             x_and_q()
         act(T.h1[:], T.p3[:, 256:512], ["xq"], ["h1"], ["p3"], scale=0.5 + 1.0 / 2048, bias=MAG)
         act(T.xn[:], T.h1[:], ["h1"], ["xn"], bias=-MAG)
         if not last:
-            places_to_write()
             for k in range(GO):
                 gcopy(T.q16[:, 16 + k::32], T.qo[:], 128, ["qo"], ["q16h"])
             send(t + 1, "q", T.qo[:], "qo", T["qr%d" % (t + 1)][:], "qr%d" % (t + 1))
@@ -610,11 +623,15 @@ def rank_program(g, core, T, topo):
         scan(T.ds[:], T.dgt[:], T.p1[:, 0:256], A.max, A.min, ["ca_", "dgt"], ["ds"], ["p1"])
         cp(T.ap16[:], T.ds[:, 15::16], ["ds"], ["ap16"])
         if not last:
-            cp(T.nxb[:].indirect(T.ap16[:]), T.nx2[:], ["nx2", "ap16"], ["nxb"])
-            to_list(T.p7[:, 128:256], T.w2, "w2", T.nxb, "nxb", 128, "nxt", "p7")
-        cp(T.xt[:].indirect(T.ap16[:]), T.xn[:], ["xn", "ap16"], ["xt"])
+            for H in HALVES:
+                cp(T.nxb[:].indirect(T.ap16[:, H.start // 16:H.stop // 16]), T.nx2[:, H], ["nx2", "ap16", "nxb"], ["nxb"])
+            for po, pk, dk, c0, c1 in ((T.p7[:, 128 + XV // 16:256], "p7", "nxt", XV, 2048), (T.p5[:, 256:256 + XV // 16], "p5", "nxu", 0, XV)):
+                for k in range(16):
+                    mm(po, T.w2[:, 15 - k:143 - k], T.nxb[:, c0 + k:c1:16], k == 0, k == 15, ["w2", "nxb"], [dk], [pk])
+        for H in HALVES:
+            cp(T.xt[:].indirect(T.ap16[:, H.start // 16:H.stop // 16]), T.xn[:, H], ["xn", "ap16", "xt"], ["xt"])
         if not last:
-            cp(T.nxl[:], T.p7[:, 128:256], ["nxt"], ["nxl"], ["p7"])
+            cp(T.nxl[:, XV // 16:128], T.p7[:, 128 + XV // 16:256], ["nxt"], ["nxl"], ["p7"])
         Q, QN, qk, qnk = QN, Q, qnk, ["qae", "qao"] if t == 0 else qk
         if t == 0:
             for k in qnk:

import numpy as np
from concourse.bass import DstId, RemoteDMATransfer
from concourse.mybir import dt, AluOpType as A, AxisListType, ActivationFunctionType as F

SCRATCH = {}
for _d, _names in (
        ("bfloat16", (("xt", 2560), ("nxb", 2560), ("rcb", 2048), ("x1", 2048), ("x2", 2048), ("x3", 2048), ("x4", 2048),
                      ("q16", 4096), ("qa", 256), ("qb", 256), ("qo", 128), ("qr0", 128), ("qr1", 128), ("qr2", 128),
                      ("xg", 4096), ("ab", 4096), ("ca", 4096), ("cb", 4096), ("xg4", 3072), ("rr", 768),
                      ("eq", 256), ("fl", 16), ("xc", 512), ("f3", 48), ("em", 896), ("ed", 256), ("yv1", 1152),
                      ("ev", 1152), ("vf", 256), ("gg", 512), ("nx2", 256), ("xga", 256), ("xn", 256),
                      ("hl", 512), ("ch", 144), ("cg", 128), ("cf", 512), ("dg", 256), ("zr", 256), ("tri", 256),
                      ("wf", 144), ("w2", 144), ("b8f", 8), ("bs", 24), ("bx", 24), ("off", 256), ("b4", 128),
                      ("base", 256), ("idb", 128), ("idn", 128), ("i4k", 128), ("i4n", 128), ("ones", 256))),
        ("float16", (("nph", 128), ("npt", 128), ("sw", 512), ("idh", 128), ("ihn", 128), ("wh", 144), ("a0h", 16),
                     ("pd", 256), ("w1", 256), ("wb", 256), ("sc1", 256), ("sc2", 256), ("ar", 256),
                     ("az", 256), ("ax", 256), ("vrh", 256), ("vlh", 16), ("rph", 128))),
        ("float32", (("uw", 768), ("idw", 2048), ("dd", 256), ("vl", 16), ("vn", 16), ("vr", 256), ("dgu", 256),
                     ("ka", 256), ("key", 256), ("s1", 256), ("a3", 48), ("u1", 256), ("u2", 256),
                     ("ws", 16), ("we", 16), ("wr0", 16), ("wr1", 16), ("wr2", 16), ("h1", 256), ("yy", 256), ("y2", 256),
                     ("nj", 32), ("nk", 16), ("cols", 32), ("dgt", 256), ("rst", 256), ("idf", 128),
                     ("ds", 256), ("sa", 8))),
        ("int32", (("ui", 512), ("pvr", 2048), ("npi", 128), ("rpi", 128), ("ci", 32))),
        ("uint16", (("nxl", 128), ("d16", 256), ("vl16", 16), ("vp16", 16), ("ap16", 16), ("a016", 16), ("bl", 32),
                    ("al16", 16), ("nl16", 16), ("exl", 16)))):
    for _n, _c in _names:
        SCRATCH[_n] = ("sbuf", [128, _c], _d)
for _k in range(8):
    SCRATCH["p%d" % _k] = ("psum", [128, 512], "float32")

ROUNDS = 3
LA, LB = 64, 192
XV0, XV = 1024, 768
SEMAPHORES = ["cv", "cs", "ct", "cp", "ldx", "ldq", "ldu", "ldn", "ldr", "ldp", "ldb", "ldc", "out"]
for _t in range(ROUNDS):
    SEMAPHORES += ["%s%d" % (_a, _t) for _a in ("rq", "ra", "rw", "lq", "la", "lw")]
PARTS = 4
EARLY = 4
LAND = ("ab", "ca", "cb")
SEMAPHORES += ["%s%d" % (_a, _c) for _a in ("fa", "fb", "fl") for _c in range(PARTS)]
G0, S0 = 1, 6
GE, GO = 7, 9
EA = 8
CA = 2
MW, MV = 2, 7
FAR = 524288.0
BIG = 1048576.0
MAG = 12582912.0


def neighbour(core, T, topo):
    return [c for c in topo.cores_of(core) if T.rank_of(c) is None and topo.die(c) == topo.die(core)][0]


def hand_back(g, core, home, T, topo):
    rid, pid = topo.addr(home, core)
    n, back = len(topo.engines(home, core)), len(topo.engines(core, home))
    for t in range(ROUNDS):
        for c in range(PARTS):
            J = slice(4096 // PARTS * c, 4096 // PARTS * (c + 1))
            g.wait_ge(T.sem["fa%d" % c], n * (t + 1))
            g.remote_dma(T.ab[:, J], T[LAND[t]][:, J], T.sem["fb%d" % c], T.sem["fl%d" % c], pid, rid, topo.mask(core, home))
    for c in range(PARTS):
        g.wait_ge(T.sem["fl%d" % c], back * ROUNDS)


def rank_program(g, core, T, topo):
    rank = T.rank_of(core)
    if rank is None:
        for home in T.cores:
            if core in topo.cores_of(home) and neighbour(home, T, topo) == core:
                hand_back(g, core, home, T, topo)
        return
    N = len(T.cores)
    V, S, P = g.vector, g.scalar, g.tensor
    eng = {"v": V, "s": S, "t": P, "p": g, "y": g.sync}
    own = {"v": "cv", "s": "cs", "t": "ct", "p": "cp"}
    total = {}
    known = {e: {} for e in eng}
    clocks = {}
    wr, rd, bank = {}, {}, {}

    def need(e, deps):
        for s in sorted(deps):
            n = deps[s]
            if known[e].get(s, 0) >= n:
                continue
            eng[e].wait_ge(T.sem[s], n)
            for k, c in clocks.get((s, n), {}).items():
                known[e][k] = max(known[e].get(k, 0), c)
            known[e][s] = n

    def deps_of(R, W, X, me):
        d = {}

        def put(s, n):
            d[s] = max(d.get(s, 0), n)
        for k in R:
            if k in wr:
                put(*wr[k])
        for k in W:
            if k in wr and wr[k][0] != me:
                put(*wr[k])
            for s, n in rd.get(k, {}).items():
                if s != me:
                    put(s, n)
        for k in X:
            for s, n in bank.get(k, {}).items():
                if s != me:
                    put(s, n)
        return d

    def note(s, n, R, W, X):
        for k in R:
            rd.setdefault(k, {})[s] = n
        for k in W:
            wr[k] = (s, n)
            rd[k] = {}
        for k in X:
            bank.setdefault(k, {})[s] = n

    def op(e, R, W, X, call):
        me = own[e]
        need(e, deps_of(R, W, X, me))
        n = total.get(me, 0) + 1
        total[me] = n
        call().then_inc(T.sem[me], 1)
        c = dict(known[e])
        c[me] = n
        clocks[(me, n)] = c
        note(me, n, R, W, X)

    def dma(e, sem, full, R, W, out, in_):
        need(e, deps_of(R, W, [], sem))
        total[sem] = total.get(sem, 0) + 16
        eng[e].dma_start(out, in_).then_inc(T.sem[sem], 16)
        c = dict(known[e])
        c[sem] = full
        clocks[(sem, full)] = c
        note(sem, full, R, W, [])

    def send(t, kind, src, key, dst, land):
        d = T.cores[(rank + 1 + t % (N - 1)) % N]
        es = topo.engines(core, d)[:8]
        m = 0
        for x in es:
            m |= 1 << x
        need("p", deps_of([key], [], [], None))
        rid, pid = topo.addr(d, core)
        rs, ls = "r" + kind + str(t), "l" + kind + str(t)
        g.remote_dma(dst, src, T.sem[rs], T.sem[ls], pid, rid, m)
        total[ls] = len(es)
        note(ls, len(es), [key], [], [])
        sender = T.cores[(rank - 1 - t % (N - 1)) % N]
        total[rs] = len(topo.engines(sender, core)[:8])
        wr[land] = (rs, total[rs])

    def fold(t, c):
        d = neighbour(core, T, topo)
        J = slice(4096 // PARTS * c, 4096 // PARTS * (c + 1))
        R = ["xg%d" % c] + Q16
        need("p", deps_of(R, ["ab%d" % c], [], None))
        rid, pid = topo.addr(d, core)
        g.remote_dma_fused([RemoteDMATransfer(dst_ids=[DstId(rid=rid, pnc=pid)], dma_engine_mask=topo.mask(core, d),
                                              remote_sem=T.sem["fa%d" % c], srcs=[T.xg[:, J], T.q16[:, J]],
                                              dsts=[T[LAND[t]][:, J]], alu_op=2)], local_sem=T.sem["fl%d" % c])
        total["fl%d" % c] = len(topo.engines(core, d)) * (t + 1)
        total["fb%d" % c] = len(topo.engines(d, core)) * (t + 1)
        note("fl%d" % c, total["fl%d" % c], R, [], [])
        note("fb%d" % c, total["fb%d" % c], [], ["ab%d" % c], [])

    def act(out, in_, R, W, X=(), func=F.Identity, **kw):
        op("s", R, W, X, lambda: S.activation(out, in_, func, **kw))

    def tt(out, a, b, o, R, W, X=()):
        op("v", R, W, X, lambda: V.tensor_tensor(out, a, b, o))

    def ts(out, a, s1, o1, R, W, X=(), s2=None, o2=None):
        if o2 is None:
            op("v", R, W, X, lambda: V.tensor_scalar(out, a, s1, None, o1))
        else:
            op("v", R, W, X, lambda: V.tensor_scalar(out, a, s1, s2, o1, o2))

    def cp(out, in_, R, W, X=()):
        op("v", R, W, X, lambda: V.tensor_copy(out, in_))

    def vtr(out, in_, R, W, X=()):
        op("v", R, W, X, lambda: V.transpose(out, in_))

    def scan(out, d0, d1, o0, o1, R, W, X=()):
        op("v", R, W, X, lambda: V.tensor_tensor_scan(out, d0, d1, 0.0, o0, o1))

    def mm(out, l, r, st, sp, R, W, X):
        op("t", R, W, X, lambda: P.matmul(out, l, r, st, sp))

    def iota(out, pat, base, cm, W, whole=False):
        if whole:
            op("p", [], W, [], lambda: g.iota(out, pat, base, cm))
        else:
            op("p", [], W, [], lambda: g.iota(out, pat, base, cm, allow_small_or_imprecise_dtypes=True))

    def gcopy(out, in_, n, R, W):
        op("p", R, W, [], lambda: g.affine_select(out, in_, [[0, n]], A.is_gt, 0.0, 1, 0))

    def col(j):
        return T.cols[:, j:j + 1]

    def to_list(out, w, wk, src, sk, n, dk, pk, st=True, sp=True):
        for k in range(16):
            mm(out, w[:, 15 - k:143 - k], src[:, k:16 * n:16], st and k == 0, sp and k == 15, [wk, sk], [dk], [pk])

    def by_lane(pout, o, src, s0, l0, l1, w, wk, keys, dk, pk, alone, close=False):
        w, n = w
        for k in range(16):
            mm(pout[l0 % 128:(l1 - 1) % 128 + 1, o + k:o + 16 * n:16], src[:, 16 * (l0 - s0) + k:16 * (l1 - s0):16], w,
               alone, alone or (close and k == 15), [wk] + keys, [dk], [pk])

    Q16 = ["q16v", "q16g", "q16h", "q16s"]

    dma("y", "ldn", 16, [], ["npi"], T.npi[:], T.nx[:])
    dma("s", "ldq", 16, [], ["qa"], T.qa[:], T.mv[:])
    dma("y", "ldx", 16, [], ["xt"], T.xt[:, 0:2048], T.xd[:])
    dma("y", "ldu", 16, [], ["ui"], T.ui[:], T.ul[:])
    dma("s", "ldr", 16, [], ["rpi"], T.rpi[:], T.rc[:])
    for i in range(16):
        dma("y", "ldp", 256, ["xt", "ui", "qa"], ["pvr"], T.pvr[i:128:16, :], T.pv[:])

    iota(T.ci[:, 0:1], [[0, 1]], 0, 1, ["ci0"], True)
    iota(T.ch[:], [[1, 144]], 0, -1, ["ch"])
    iota(T.cg[:], [[1, 8], [0, 16]], 0, 0, ["cg"])
    iota(T.cf[:, 0:256], [[0, 16], [1, 16]], 0, 0, ["cf"])
    iota(T.ci[:, 16:32], [[16, 16]], 15, 0, ["ci1"], True)
    op("v", ["ci0"], ["ci4"], [], lambda: V.tensor_scalar(T.ci[:, 2:3], T.ci[:, 0:1], 4, None, A.arith_shift_right))
    op("v", ["ci0"], ["ci3"], [], lambda: V.tensor_scalar(T.ci[:, 1:2], T.ci[:, 0:1], 15, None, A.bitwise_and))
    op("v", ["ci0"], ["ci6"], [], lambda: V.tensor_scalar(T.ci[:, 4:5], T.ci[:, 0:1], 1, None, A.bitwise_and))
    op("v", ["ci4"], ["ci5"], [], lambda: V.tensor_scalar(T.ci[:, 3:4], T.ci[:, 2:3], 1, None, A.bitwise_and))
    cp(T.cols[:, 0:2], T.ci[:, 1:3], ["ci3", "ci4"], ["c0", "c1"])
    cp(col(4), T.ci[:, 4:5], ["ci6"], ["c4"])
    cp(col(2), T.ci[:, 3:4], ["ci5"], ["c2"])
    ts(col(3), T.ci[:, 3:4], 0.0, A.is_equal, ["ci5"], ["c3"])
    ts(col(7), T.ci[:, 1:2], -1.0, A.mult, ["ci3"], ["c7"], (), 15.0, A.add)
    ts(col(9), T.ci[:, 1:2], 2.0, A.is_lt, ["ci3"], ["c9"])
    C = T.ch[:, 0:128]
    for j, (x, c) in enumerate(((0.0, 3), (16.0, 3), (-16.0, 2), (0.0, 2))):
        ts(T.sw[:, 128 * j:128 * j + 128], C, x, A.is_equal, ["ch", "c%d" % c], ["sw"], (), col(c), A.mult)
    for w, k, x in ((T.idb, "idb", 1.0), (T.idh, "idh", 1.0), (T.ihn, "ihn", -1.0)):
        ts(w[:], C, 0.0, A.is_equal, ["ch"], [k], (), x, A.mult)
    ts(T.wf[:], T.ch[:], col(7), A.is_equal, ["ch", "c7"], ["wf"], (), FAR, A.mult)
    ts(T.w2[:], T.ch[:], col(7), A.is_equal, ["ch", "c7", "c9"], ["w2"], (), col(9), A.mult)
    ts(T.wh[:], T.ch[:], col(7), A.is_equal, ["ch", "c7"], ["wh"])
    ts(T.b8f[:], T.cg[:, 0:128:16], col(1), A.is_equal, ["cg", "c1"], ["b8f"], (), FAR, A.mult)
    ts(T.b4[:], T.cg[:], col(1), A.is_equal, ["cg", "c1"], ["b4"], (), 4096.0, A.mult)
    CF = T.cf[:, 0:256]
    ts(T.dg[:], CF, col(0), A.is_equal, ["cf", "c0"], ["dg"])
    cp(T.exl[:], T.ci[:, 16:32], ["ci1"], ["exl"])
    act(col(8), col(0), ["c0"], ["c8"], bias=0.5)
    act(col(5), col(4), ["c4"], ["c5"], scale=-1.0, bias=1.0)
    act(col(6), col(0), ["c0"], ["c6"], scale=2.0)
    act(T.idn[:], T.idb[:], ["idb"], ["idn"], scale=-1.0)
    for j in range(3):
        act(T.bs[:, 8 * j:8 * j + 8], T.b8f[:], ["b8f"], ["bs"], scale=32.0 * (-1) ** j / FAR)
        act(T.bx[:, 8 * j:8 * j + 8], T.b8f[:], ["b8f"], ["bx"], scale=-16.0 * (-1) ** j / FAR)
    for o, p0, p1, x in ((0, 0, LA, -8.5), (0, LA, 128, -1.0), (128, 0, LB - 128, -1.0), (128, LB - 128, 128, -8.5)):
        act(T.base[p0:p1, o:o + 128], T.cg[p0:p1, :], ["cg"], ["base"], scale=0.0, bias=x * FAR)
    act(T.qo[:], T.qa[:, 1::2], ["qa"], ["qo"])
    iota(T.nj[:], [[512, 2], [16, 16]], 0, 0, ["nj"])
    iota(T.dgt[:], [[0, 256]], -1, 0, ["dgt"])
    for k in range(G0):
        gcopy(T.q16[:, k::16], T.qa[:], 256, ["qa"], ["q16g"])
    send(0, "q", T.qo[:], "qo", T.qr0[:], "qr0")
    for k in range(G0, G0 + S0):
        act(T.q16[:, k::16], T.qa[:], ["qa"], ["q16s"])
    iota(T.cf[:, 256:512], [[0, 16], [1, 16]], 0, 0, ["cf2"])
    iota(T.idw[:], [[1, 2048]], 0, 0, ["idw"])
    cp(T.nph[:], T.npi[:], ["npi"], ["nph"])
    vtr(T.npt[:], T.nph[:], ["nph"], ["npt"])
    for e in (0, 1):
        for b in range(4):
            for h in (0, 1):
                mm(T.p7[:, 128 + 2 * b + e:256:8], T.sw[:, 128 * (2 * e + h):128 * (2 * e + h) + 128],
                   T.npt[:, 32 * b + 16 * h:32 * b + 16 * h + 16], h == 0, h == 1, ["sw", "npt"], ["nxt"], ["p7"])
    for k in range(G0 + S0, 16):
        cp(T.q16[:, k::16], T.qa[:], ["qa"], ["q16v"])
    cp(T.nxl[:], T.p7[:, 128:256], ["nxt"], ["nxl"], ["p7"])

    TWO = ((0, T.nph, "nph", T.nxb, "nxb", "ldb"), (256, T.rph, "rph", T.rcb, "rcb", "ldc"))
    cp(T.rph[:], T.rpi[:], ["rpi"], ["rph"])
    for o, src, sk, tab, tk, sem in TWO:
        cp(T.hl[:, o:o + 128], src[:], [sk], ["hi" + sk])
        mm(T.p6[:, o:o + 128], T.idh[:], src[:], True, False, ["idh", sk], ["lp" + sk], ["p6"])
        mm(T.p6[:, o:o + 128], T.idn[:], T.hl[:, o:o + 128], False, True, ["idn", "hi" + sk], ["lp" + sk], ["p6"])

    def tables_of_two_parts():
        for o, src, sk, tab, tk, sem in TWO:
            act(T.hl[:, o + 128:o + 256], T.p6[:, o:o + 128], ["lp" + sk], ["lo" + sk], ["p6"])
        for o, src, sk, tab, tk, sem in TWO:
            iota(tab[:, 0:2048], [[0, 2048]], 0, 0, [tk])
            for j, k in enumerate(("hi" + sk, "lo" + sk)):
                dma("y", sem, 32, [k], [tk], tab[j:128:16, 0:2048], T.hl[:, o + 128 * j:o + 128 * j + 128])

    def constants_for_the_lists():
        ts(T.vp16[:], T.nj[:, 0:16], 2.0, A.mult, ["nj", "c6"], ["vp16"], (), col(6), A.add)
        ts(T.az[:], CF, 0.0, A.mult, ["cf"], ["az"])
        ts(T.f3[:, 0::3], T.cf[:, 0:16], 0.0, A.mult, ["cf"], ["f3"])
        ts(T.dgt[:, 0::16], T.nj[:, 16:32], col(0), A.add, ["nj", "c0", "dgt"], ["dgt"], (), 1536.0, A.add)

    def constants_for_the_writes():
        act(T.zr[:], CF, ["cf"], ["zr"], func=F.Sign)
        act(T.rst[:], T.zr[:], ["zr"], ["rst"], scale=-2.0 * BIG, bias=BIG)
        act(T.ones[:], CF, ["cf"], ["ones"], scale=0.0, bias=1.0)
        for w, k, x in ((T.idf, "idf", 1.0), (T.i4n, "i4n", -4096.0), (T.i4k, "i4k", 4096.0)):
            act(w[:], T.idb[:], ["idb"], [k], scale=x)
        act(T.off[:], T.dg[:], ["dg"], ["off"], scale=-BIG, bias=BIG)
        act(T.vf[:], CF, ["cf", "c8"], ["vf"], scale=-1.0, bias=col(8), func=F.Sign)
        act(T.tri[:], T.vf[:], ["vf"], ["tri"], scale=4096.0, func=F.Relu)

    SEG = []
    for j in range(7):
        for h in (0, 1):
            m, o = 8 * h + j, SEG[-1][1] + SEG[-1][3] - SEG[-1][2] if SEG else 0
            SEG.append((m, o, 16 * m + 16, 128 * h + 128))
    ND = 896
    HALVES = (slice(128, 256), slice(0, 128))

    def new_places(H):
        tt(T.uw[:].indirect(T.vp16[:, H.start // 16:H.stop // 16]), T.u1[:, H], T.u2[:, H], A.max, ["u1", "u2", "vp16", "uw"], ["uw"])

    def new_recipients(t):
        mm(T.p7[:, 64:80], T.idf[:], T.we[:], True, False, ["idf", "we"], ["vlp"], ["p7"])
        mm(T.p7[:, 64:80], T.idf[:], T["wr%d" % t][:], False, True, ["idf", "wr%d" % t], ["vlp"], ["p7"])
        cp(T.vl16[:], T.p7[:, 64:80], ["vlp"], ["vl16"], ["p7"])

    Q, QN, qk, qnk = T.qa, T.qb, ["qa"], ["qbe", "qbo"]
    X0 = T.xt[:, 0:2048]
    for t in range(ROUNDS):
        last = t == ROUNDS - 1
        xv = XV if t else XV0

        def walk(x, xk, out, ok, l0, l1):
            tt(out[:, 16 * l0:16 * l1], x[:].indirect(T.d16[:, l0:l1]), T.q16[:, 16 * l0:16 * l1], A.is_lt,
               xk + ["d16"] + Q16, ok)

        def wsum(pout, o, out, ok, h, pk, dk):
            by_lane(pout, o + 128 * h, out, 0, 128 * h, 128 * h + 128, (T.b8f[:], 8), "b8f", [ok, ok.replace("cb", "cs")],
                    dk + str(h), pk, True)

        BANKS = ("p2", "p3", "p5", "p6")

        def less_q(c):
            pk, j = BANKS[c % 4], 16 * LA + 512 * c
            mm(T[pk][:], T.idn[:], T.q16[:, j:j + 512], True, False, ["idn"] + Q16, [pk + "d"], [pk])

        def diff(c, sk):
            pk = BANKS[c % 4]
            mm(T[pk][:], T.idb[:], T.xg4[:, 512 * c:512 * c + 512], False, True, ["idb", sk], [pk + "d"], [pk])

        def sign(c, h):
            pk, j = BANKS[c % 4], 16 * LA + 512 * c
            act(T.cb[:, j:j + 512], T[pk][:], [pk + "d"], ["cs%d" % h], [pk], func=F.Sign, scale=-1.0, bias=-0.5)

        def marks(c):
            l0, l1 = 256 // PARTS * c, 256 // PARTS * (c + 1)
            act(T.xg[:, 16 * l0:16 * l1], X0.indirect(T.d16[:, l0:l1]), ["xt", "d16"], ["xg%d" % c])
            fold(t, c)

        def scores(h, folded):
            parts = range(PARTS // 2 * h, PARTS // 2 * (h + 1))
            src, sk, w, wk = (T.ab, "ab", T.bs, "bs") if folded else (T.xg, "xg", T.bx, "bx")
            by_lane(T.p4, 256 * h, src, 0, 128 * h, 128 * h + 128, (w[:, 8 * h:8 * h + 16], 16), wk, [sk + str(c) for c in parts],
                    "sc", "p4", False, folded and h == 1)

        def lower(h):
            act(T.ka[:, 128 * h:128 * h + 128], T.p4[:, 384 * h:384 * h + 128], ["sc"], ["ka"], ["p4"], bias=-0.5 * FAR)

        def over(j, pp, o, keys, pk):
            act(T.rr[:, 256 * j:256 * j + 256], pp[:, o:o + 256], keys, ["rr%d" % j], [pk], func=F.Relu, scale=32.0, bias=-256.0 * FAR)

        NX = ["nxl", "nxv"]
        act(T.x1[:, xv:2048], X0.indirect(T.nxl[:, xv // 16:128]), ["xt", "nxl"], ["x1b"])
        if t:
            cp(T.nxl[:, 0:xv // 16], T.p5[:, 256:256 + xv // 16], ["nxu"], ["nxv"], ["p5"])
        cp(T.x1[:, 0:xv], X0.indirect(T.nxl[:, 0:xv // 16]), ["xt"] + NX, ["x1a"])
        if t:
            new_places(HALVES[1])
            new_recipients(t - 1)
            cp(T.d16[:], T.uw[:, 0:512].indirect(T.vl16[:]), ["uw", "vl16"], ["d16"])
        else:
            cp(T.d16[:], T.ui[:, 0:512:2], ["ui"], ["d16"])
        act(T.x2[:], T.x1[:].indirect(T.nxl[:]), ["x1a", "x1b"] + NX, ["x2"])
        walk(T.x1, ["x1a", "x1b"], T.ca, ["ca0", "ca1"], 0, 256)
        for c in range(EARLY):
            marks(c)
        wsum(T.p0, 0, T.ca, "ca0", 0, "p0", "k1")
        wsum(T.p0, 0, T.ca, "ca1", 1, "p0", "k1")
        act(T.x3[:], T.x2[:].indirect(T.nxl[:]), ["x2"] + NX, ["x3"])
        for c in range(EARLY, PARTS):
            marks(c)
        if t:
            act(T.dd[:], T.uw[:, 0:512].indirect(T.vl16[:]), ["uw", "vl16"], ["dd"])
        else:
            tables_of_two_parts()
        over(0, T.p0, 0, ["k10", "k11"], "p0")
        if t:
            act(T.vl[:], T.p7[:, 64:80], ["vlp"], ["vl"], ["p7"])
            act(T.vn[:], T.p7[:, 64:80], ["vlp"], ["vn"], ["p7"], scale=-1.0)
        walk(T.x2, ["x2"], T.cb, ["cb0", "cb1", "cs0", "cs1"], 0, 256)
        act(T.x4[:], T.x3[:].indirect(T.nxl[:]), ["x3"] + NX, ["x4"])
        mm(T.p4[:], T.idb[:], T.cf[:], True, False, ["idb", "cf", "cf2"], ["sc"], ["p4"])
        scores(0, False)
        scores(1, False)
        wsum(T.p1, 0, T.cb, "cb0", 0, "p1", "k2")
        wsum(T.p1, 0, T.cb, "cb1", 1, "p1", "k2")
        walk(T.x3, ["x3"], T.ca, ["ca0"], 0, 128)
        wsum(T.p0, 256, T.ca, "ca0", 0, "p0", "k3")
        over(1, T.p1, 0, ["k20", "k21"], "p1")
        def on_top(src, sk):
            mm(T.p1[:, 256:512], T.idb[:], src, sk == "base", False, ["idb", sk], ["k4"], ["p1"])

        for h, (l0, l1) in enumerate(((LA, 128), (128, LB))):
            act(T.xg4[:, 16 * (l0 - LA):16 * (l1 - LA)], T.x4[:].indirect(T.d16[:, l0:l1]), ["x4", "d16"], ["xg4%d" % h])
        NA, NB = (128 - LA) // 32, (LB - LA) // 32
        for c in range(NB):
            less_q(c)
        on_top(T.base[:], "base")
        on_top(T.rr[:, 0:256], "rr0")
        on_top(T.rr[:, 256:512], "rr1")
        scores(0, True)
        for c in range(NA):
            diff(c, "xg40")
        walk(T.x3, ["x3"], T.ca, ["ca1"], 128, 256)
        wsum(T.p0, 256, T.ca, "ca1", 1, "p0", "k3")
        for c in range(NA, NB):
            diff(c, "xg41")
        walk(T.x4, ["x4"], T.cb, ["cb0"], 0, LA)
        walk(T.x4, ["x4"], T.cb, ["cb1"], LB, 256)
        for c in range(NA):
            sign(c, 0)
        over(2, T.p0, 256, ["k30", "k31"], "p0")
        by_lane(T.p1, 256, T.cb, 0, 0, 128, (T.b8f[:], 8), "b8f", ["cb0", "cs0"], "k4", "p1", False)
        scores(1, True)
        on_top(T.rr[:, 512:768], "rr2")
        for c in range(NA, NB):
            sign(c, 1)
        lower(0)
        lower(1)
        if t == 0:
            constants_for_the_writes()
        by_lane(T.p1, 384, T.cb, 0, 128, 256, (T.b8f[:], 8), "b8f", ["cb1", "cs1"], "k4", "p1", False, True)
        def equal_v(segs):
            for m, o, c0, c1 in segs:
                ts(T.ev[:, o:o + c1 - c0], T.vrh[:, c0:c1], T.vl[:, m:m + 1], A.is_equal, ["vrh", "vl"], ["evv"])

        if t:
            cp(T.vlh[:], T.vl[:], ["vl"], ["vlh"])
            cp(T.vrh[:], T.idw[:].indirect(T.vl16[:]), ["idw", "vl16"], ["vrh"])
            equal_v(SEG[:MW])
            act(T.vr[:], T.idw[:].indirect(T.vl16[:]), ["idw", "vl16"], ["vr"])
            for m, o, c0, c1 in SEG[MV:]:
                act(T.yv1[:, o:o + c1 - c0], T.vr[:, c0:c1], ["vr", "vn"], ["yv1"], func=F.Abs, bias=T.vn[:, m:m + 1])
            mm(T.p2[:, 0:256], T.idb[:], T.tri[:], True, False, ["idb", "tri"], ["dv"], ["p2"])
            for j in range(16):
                mm(T.p2[:, j:256:16], T.ihn[:], T.vlh[:], False, False, ["ihn", "vlh"], ["dv"], ["p2"])
            mm(T.p2[:, 0:256], T.idh[:], T.vrh[:], False, True, ["idh", "vrh"], ["dv"], ["p2"])
            act(T.yv1[:, ND:ND + 256], T.p2[:, 0:256], ["dv"], ["yv1"], ["p2"], func=F.Abs)
        if t == 0:
            cp(T.dd[:], T.ui[:, 0:512:2], ["ui"], ["dd"])
        tt(T.key[:], T.p1[:, 256:512], T.ka[:], A.max, ["ka", "k4"], ["key"], ["p1"])
        tt(T.key[:], T.p4[:, 128:384], T.key[:], A.min, ["key", "sc"], ["key"], ["p4"])
        scan(T.s1[:], T.rst[:], T.key[:], A.max, A.min, ["rst", "key"], ["s1"])
        tt(T.eq[:], T.s1[:].indirect(T.exl[:]), T.key[:], A.is_equal, ["s1", "exl", "key"], ["eq"])
        act(T.fl[:], T.s1[:, 15::16], ["s1"], ["fl"], func=F.Sign, bias=0.25 * FAR)
        if t:
            o = SEG[MV][1]
            act(T.ev[:, o:ND + 256], T.yv1[:, o:ND + 256], ["yv1"], ["ev"], func=F.Relu, scale=-1.0, bias=1.0)
        for h in (0, 1):
            mm(T.p3[:, 128 * h:128 * h + 128], T.eq[:, 128 * h:128 * h + 128], T.idb[:], True, True, ["eq", "idb"], ["oh"], ["p3"])
        mm(T.p6[:, 0:16], T.ones[:, 0:128], T.fl[:], True, True, ["ones", "fl"], ["nn"], ["p6"])
        tt(T.pd[:], T.p3[:, 0:256], T.dd[:], A.mult, ["oh", "dd"], ["pd"], ["p3"])
        to_list(T.p7[:, 0:16], T.wh, "wh", T.pd, "pd", 16, "a0", "p7")
        if t:
            equal_v(SEG[MW:MV])
        else:
            constants_for_the_lists()
        cp(T.a016[:], T.p7[:, 0:16], ["a0"], ["a016"], ["p7"])
        sa, ra = T.sa[:, t:t + 1], T.sa[:, 4 + t:5 + t]
        act(T.nk[:], T.p6[:, 0:16], ["nn"], ["nk", "n"], ["p6"], scale=0.5, bias=64.0, accum_out=col(16))
        act(col(17), col(16), ["n"], ["n1"], scale=1.0 / 256, bias=-0.498046875)
        act(col(20), col(16), ["n"], ["n4"], scale=0.5, bias=-0.25)
        act(col(18), col(17), ["n1"], ["n2"], bias=MAG)
        act(col(19), col(18), ["n2"], ["n3"], bias=-MAG)
        act(sa, col(19), ["n3", "n4"], ["sa%d" % t], scale=-128.0, bias=col(20))
        send(t, "a", sa, "sa%d" % t, ra, "ra%d" % t)
        act(T.yy[:, 0:128], Q[:, 0::2], qk + ["sa%d" % t], ["yy0"], scale=0.5, bias=sa)
        act(T.y2[:, 0:128], T.yy[:, 0:128], ["yy0"], ["y20"], bias=MAG)
        act(QN[:, 0::2], T.y2[:, 0:128], ["y20"], [qnk[0]], bias=-MAG)
        if not last:
            for k in range(GE):
                gcopy(T.q16[:, k::32], QN[:, 0::2], 128, [qnk[0]], ["q16g"])
        if t:
            mm(T.p0[:, 256:512], T.idb[:], T.off[:], True, False, ["idb", "off"], ["cv_"], ["p0"])
            mm(T.p0[:, 256:512], T.idh[:], T.vrh[:], False, False, ["idh", "vrh"], ["cv_"], ["p0"])
            for j, (m, o, c0, c1) in enumerate(SEG + [(0, ND, 0, 256)]):
                mm(T.p0[:, 256 + c0:256 + c1], T.b4[:], T.ev[:, o:o + c1 - c0], False, j == len(SEG), ["b4", "evv" if j < MV else "ev"],
                   ["cv_"], ["p0"])
        tt(T.w1[:], T.pvr[:].indirect(T.a016[:]), T.dg[:], A.mult, ["pvr", "a016", "dg"], ["w1"])
        cp(T.a0h[:], T.p7[:, 0:16], ["a0"], ["a0h"], ["p7"])
        scan(T.sc1[:], T.zr[:], T.w1[:], A.mult, A.add, ["zr", "w1"], ["sc1"])
        cp(T.bl[:, 0:16], T.sc1[:, 15::16], ["sc1"], ["bl0"])
        tt(T.wb[:], T.pvr[:].indirect(T.bl[:, 0:16]), T.dg[:], A.mult, ["pvr", "bl0", "dg"], ["wb"])
        evens = [] if last else list(range(GE, 16))

        def even_copies(ks):
            for k in ks:
                act(T.q16[:, k::32], T.y2[:, 0:128], ["y20"], ["q16s"], bias=-MAG)

        even_copies(evens[:3])
        act(T.xga[:], X0.indirect(T.bl[:, 0:16]), ["xt", "bl0"], ["xga"])
        mm(T.p3[:, 256:512], T.idn[:], Q[:], True, False, ["idn"] + qk, ["xq"], ["p3"])
        mm(T.p4[:, 0:256], T.idf[:], T.dd[:], True, False, ["idf", "dd"], ["u1p"], ["p4"])
        mm(T.p3[:, 256:512], T.idb[:], T.xga[:], False, True, ["idb", "xga"], ["xq"], ["p3"])
        even_copies(evens[3:5])
        act(T.xc[:, 0:256], T.p3[:, 256:512], ["xq"], ["xc0"], ["p3"], func=F.Sign, scale=-1.0, bias=-0.5)
        even_copies(evens[5:])
        for h in (0, 1):
            mm(T.p4[:, 128 * h:128 * h + 128], T.eq[:, 128 * h:128 * h + 128], T.i4n[:], False, h == 1, ["eq", "i4n"], ["u1p"], ["p4"])
        act(T.u1[:], T.p4[:, 0:256], ["u1p"], ["u1"], ["p4"])
        if t == 0:
            act(T.dgu[:], T.dgt[:], ["dgt"], ["dgu"], bias=-1536.0)
        mm(T.p6[:, 130:176:3], T.idh[:], T.a0h[:], True, True, ["idh", "a0h"], ["d3"], ["p6"])
        mm(T.p6[:, 129:176:3], T.ihn[:], T.a0h[:], True, False, ["ihn", "a0h"], ["d3"], ["p6"])
        mm(T.p6[:, 129:176:3], T.idh[:], T.sc1[:, 15::16], False, True, ["idh", "sc1"], ["d3"], ["p6"])
        scan(T.sc2[:], T.zr[:], T.wb[:], A.mult, A.add, ["zr", "wb"], ["sc2"])
        cp(T.bl[:, 16:32], T.sc2[:, 15::16], ["sc2"], ["bl1"])
        tt(T.xc[:, 256:512], X0.indirect(T.bl[:, 16:32]), Q[:], A.is_lt, ["xt", "bl1"] + qk, ["xc1"])
        mm(T.p6[:, 128:176:3], T.ihn[:], T.sc1[:, 15::16], True, False, ["ihn", "sc1"], ["d3"], ["p6"])
        mm(T.p6[:, 128:176:3], T.idh[:], T.sc2[:, 15::16], False, True, ["idh", "sc2"], ["d3"], ["p6"])
        for k in range(16):
            mm(T.p7[:, 16:48], T.wf[:, 15 - k:143 - k], T.xc[:, k::16], k == 0, k == 15, ["wf", "xc0", "xc1"], ["b2"], ["p7"])
        mm(T.p2[:, 0:256], T.idb[:], T.tri[:], True, False, ["idb", "tri"], ["da"], ["p2"])
        mm(T.p1[:, 0:256], T.idb[:], T.off[:], True, False, ["idb", "off"], ["ca_"], ["p1"])
        mm(T.p5[:, 0:256], T.i4n[:], T.ones[:], True, False, ["i4n", "ones"], ["u2p"], ["p5"])
        for h in (0, 1):
            mm(T.p5[:, 128 * h:128 * h + 128], T.eq[:, 128 * h:128 * h + 128], T.i4k[:], False, False, ["eq", "i4k"], ["u2p"], ["p5"])
        if t:
            scan(T.ds[:], T.dgu[:], T.p0[:, 256:512], A.max, A.min, ["cv_", "dgu"], ["ds"], ["p0"])
            cp(T.vp16[:], T.ds[:, 15::16], ["ds"], ["vp16"])
        else:
            cp(T.uw[:, 0:512], T.ui[:], ["ui"], ["uw"])
        ts(T.f3[:, 2::3], T.p7[:, 16:32], FAR, A.is_lt, ["b2"], ["f3"], ["p7"])
        ts(T.f3[:, 1::3], T.p7[:, 32:48], 8.5 * FAR, A.is_lt, ["b2"], ["f3"], ["p7"])
        scan(T.a3[:], T.f3[:], T.p6[:, 128:176], A.mult, A.add, ["f3", "d3"], ["al"], ["p6"])
        cp(T.al16[:], T.a3[:, 2::3], ["al"], ["al16"])
        cp(T.az[:, 0::16], T.a3[:, 2::3], ["al"], ["az"])
        cp(T.ar[:], T.idw[:].indirect(T.al16[:]), ["idw", "al16"], ["ar"])
        scan(T.ax[:], T.zr[:], T.az[:], A.mult, A.add, ["zr", "az"], ["ax"])
        act(T.gg[:, 0:256], T.rcb[:].indirect(T.al16[:]), ["rcb", "al16"], ["gg"])
        if not last:
            act(T.gg[:, 256:512], T.nxb[:, 0:2048].indirect(T.al16[:]), ["nxb", "al16"], ["gg"])
        nl = 16 if last else 32

        def lists_of_w_and_nx():
            to_list(T.p6[:, 192:192 + nl], T.w2, "w2", T.gg, "gg", nl, "wl", "p6")
            if not last:
                cp(T.nl16[:], T.p6[:, 208:224], ["wl"], ["nl16"], ["p6"])
            act(T.ws[:], T.p6[:, 192:208], ["wl", "c4"], ["ws"], ["p6"], scale=col(4))
            send(t, "w", T.ws[:], "ws", T["wr%d" % t][:], "wr%d" % t)

        if last:
            lists_of_w_and_nx()
        mm(T.p5[:, 0:256], T.idh[:], T.ar[:], False, True, ["idh", "ar"], ["u2p"], ["p5"])
        act(T.u2[:], T.p5[:, 0:256], ["u2p"], ["u2"], ["p5"])
        act(T.xga[:], X0.indirect(T.al16[:]), ["xt", "al16"], ["xga"])
        mm(T.p1[:, 0:256], T.idh[:], T.ar[:], False, False, ["idh", "ar"], ["ca_"], ["p1"])
        mm(T.p2[:, 0:256], T.idh[:], T.ar[:], False, False, ["idh", "ar"], ["da"], ["p2"])
        mm(T.p2[:, 0:256], T.ihn[:], T.ax[:], False, True, ["ihn", "ax"], ["da"], ["p2"])

        def equal_a(segs):
            for m, o, c0, c1 in segs:
                ts(T.em[:, o:o + c1 - c0], T.ar[:, c0:c1], T.a3[:, 3 * m + 2:3 * m + 3], A.is_equal, ["ar", "al"], ["em%d" % m])

        def count_a(segs):
            for m, o, c0, c1 in segs:
                mm(T.p1[:, c0:c1], T.b4[:], T.em[:, o:o + c1 - c0], False, False, ["b4", "em%d" % m], ["ca_"], ["p1"])

        equal_a(SEG[:EA])
        ts(T.ed[:], T.p2[:, 0:256], 0.0, A.is_equal, ["da"], ["ed"], ["p2"])
        equal_a(SEG[EA:])
        count_a(SEG[:CA])
        if not last:
            lists_of_w_and_nx()
            act(T.nx2[:], T.nxb[:, 0:2048].indirect(T.nl16[:]), ["nxb", "nl16"], ["nx2"])
        act(T.we[:], T.p6[:, 192:208], ["wl", "c5"], ["we"], ["p6"], scale=col(5))
        act(T.yy[:, 128:256], T["qr%d" % t][:], ["qr%d" % t, "ra%d" % t], ["yy1"], scale=0.5, bias=ra)
        act(T.y2[:, 128:256], T.yy[:, 128:256], ["yy1"], ["y21"], bias=MAG)
        if not last:
            act(T.qo[:], T.y2[:, 128:256], ["y21"], ["qo"], bias=-MAG)
        new_places(HALVES[0])
        if last:
            new_places(HALVES[1])
            dma("y", "out", 64, ["uw"], ["yu"], T.yu[:], T.uw[:, 0:512])

        def x_and_q():
            mm(T.p3[:, 256:512], T.idb[:], Q[:], True, False, ["idb"] + qk, ["xq"], ["p3"])
            mm(T.p3[:, 256:512], T.idb[:], T.xga[:], False, True, ["idb", "xga"], ["xq"], ["p3"])

        if last:
            x_and_q()
        count_a(SEG[CA:])
        mm(T.p1[:, 0:256], T.b4[:], T.ed[:], False, True, ["b4", "ed"], ["ca_"], ["p1"])
        if not last:
            x_and_q()
        act(T.h1[:], T.p3[:, 256:512], ["xq"], ["h1"], ["p3"], scale=0.5 + 1.0 / 2048, bias=MAG)
        act(T.xn[:], T.h1[:], ["h1"], ["xn"], bias=-MAG)
        if not last:
            for k in range(GO):
                gcopy(T.q16[:, 16 + k::32], T.qo[:], 128, ["qo"], ["q16h"])
            send(t + 1, "q", T.qo[:], "qo", T["qr%d" % (t + 1)][:], "qr%d" % (t + 1))
            for k in range(GO, 16):
                act(T.q16[:, 16 + k::32], T.y2[:, 128:256], ["y21"], ["q16s"], bias=-MAG)
        act(QN[:, 1::2], T.y2[:, 128:256], ["y21"], [qnk[1]], bias=-MAG)
        if last:
            dma("y", "out", 64, qnk, ["yq"], T.yq[:], QN[:])
        scan(T.ds[:], T.dgt[:], T.p1[:, 0:256], A.max, A.min, ["ca_", "dgt"], ["ds"], ["p1"])
        cp(T.ap16[:], T.ds[:, 15::16], ["ds"], ["ap16"])
        if not last:
            for H in HALVES:
                cp(T.nxb[:].indirect(T.ap16[:, H.start // 16:H.stop // 16]), T.nx2[:, H], ["nx2", "ap16", "nxb"], ["nxb"])
            for po, pk, dk, c0, c1 in ((T.p7[:, 128 + XV // 16:256], "p7", "nxt", XV, 2048), (T.p5[:, 256:256 + XV // 16], "p5", "nxu", 0, XV)):
                for k in range(16):
                    mm(po, T.w2[:, 15 - k:143 - k], T.nxb[:, c0 + k:c1:16], k == 0, k == 15, ["w2", "nxb"], [dk], [pk])
        for H in HALVES:
            cp(T.xt[:].indirect(T.ap16[:, H.start // 16:H.stop // 16]), T.xn[:, H], ["xn", "ap16", "xt"], ["xt"])
        if not last:
            cp(T.nxl[:, XV // 16:128], T.p7[:, 128 + XV // 16:256], ["nxt"], ["nxl"], ["p7"])
        Q, QN, qk, qnk = QN, Q, qnk, ["qae", "qao"] if t == 0 else qk
        if t == 0:
            for k in qnk:
                wr[k], rd[k] = wr["qa"], dict(rd["qa"])
    dma("y", "out", 64, ["xt"], ["yx"], T.yx[:], X0)
    new_recipients(ROUNDS - 1)
    act(T.vr[:], T.idw[:].indirect(T.vl16[:]), ["idw", "vl16"], ["vr"])
    dma("s", "out", 64, ["vr"], ["yv"], T.yv[:], T.vr[0:128:16, :])
    for s in SEMAPHORES:
        if total.get(s, 0) > known["p"].get(s, 0):
            g.wait_ge(T.sem[s], total[s])
